import numpy as np, ml_dtypes
CORES = [24,25,26,27,28,29,30,31]
N = 8
BF = ml_dtypes.bfloat16
W, L, M, P, Q, F, RO = 2048, 8, 8, 16, 16, 4, 2
CAP = (N - 1) * Q
def look(u, m):
    return (u * (u >> 5) + (2 * m + 1) * u) & (W - 1)
def pick(x, ix):
    return np.take_along_axis(x, ix[..., None, :], -1)
def pack(x, w, th):
    return {"x0": np.ascontiguousarray(x.reshape(N, 128, W)).astype(np.float32).astype(BF), "wt": np.ascontiguousarray(w).reshape(N, 128, 1).astype(np.float32).astype(BF),
            "th": np.repeat(th, 16, axis=1).astype(np.int32)}
def texture(rng):
    x = np.empty((N, 8, 16, W), np.int64); stock = rng.permutation(np.array([8, 24, 60, 120, 200, 300, 400, 600]))
    for g in range(8):
        n = int(stock[g]); base = rng.integers(0, 256, (n, 16))
        for q in range(N):
            e = 1.5 + rng.random()
            x[q, g] = (base[np.minimum((n * rng.random(W) ** e).astype(np.int64), n - 1)] + rng.integers(-2, 3, (W, 16))).T
    return np.clip(x, 0, 255)
def far(rng):
    return rng.integers(0, 256, (N, 8, 16, W))
def weights(rng):
    w = rng.integers(0, 256, (8, 16)); w[:, 0] = 1; w[:, 1] = 16; w[:, 13:] = 0
    return w
def with_hash(rng, w, u):
    k = rng.integers(0, 256, (len(u), 16)); v = (u - k[:, 2:] @ w[2:]) & (W - 1)
    k[:, 0] = v & 15; k[:, 1] = v >> 4
    return k
def odd(rng, m, n):
    u = np.arange(1, W, 2); u = rng.permutation(u[((u >> 5) & 1) == 0])
    i = np.unique(look(u, m), return_index=True)[1]
    assert len(i) >= n
    return rng.permutation(u[i])[:n]
def runs(rng):
    r = W // (L + F); n = min(r, CAP + 12)
    return L * np.sort(rng.permutation(r)[:n]) + L - 2
def setup_inputs(rng):
    return pack(texture(rng), rng.integers(0, 256, (N, 8, 16)), rng.integers(20, 41, (N, 8, 2)))
def setup_inputs_room(rng):
    x = far(rng); w = weights(rng); th = np.stack([rng.integers(1, 60, (N, 8)), rng.choice(np.array([1, 2, 40]), (N, 8))], axis=-1)
    th[rng.integers(0, N), rng.integers(4, 6), 1] = 0
    for g in range(8):
        m = g % M; p = runs(rng); n = len(p); u = odd(rng, m, n); c = look(u, m); k = with_hash(rng, w[g], u)
        for q in range(N):
            a = int(rng.choice(np.array([0, 1, CAP - 1, CAP, CAP + 1, n])))
            if q == 0: a = (CAP, CAP + 1, n, CAP - 1, 1, 0, CAP, CAP + 1)[g]
            i = rng.permutation(n)[:a]
            x[q, g][:, c] = k.T; x[q, g][:, p[i]] = k[i].T
    return pack(x, np.broadcast_to(w, (N, 8, 16)), th)
def setup_inputs_ties(rng):
    x = far(rng); w = weights(rng); t = rng.integers(2, 250, 8); t2 = t + rng.integers(-1, 2, (N, 8))
    for g in range(1, 8, 2):
        a = 4 * int(rng.integers(65, 124)) + g % 4; t2[:, g] = a; t[g] = a + int(rng.integers(0, 2))
    th = np.stack([np.broadcast_to(t, (N, 8)), t2], axis=-1)
    for g in range(8):
        m = g % M; p = runs(rng); n = len(p); u = odd(rng, m, n); k = with_hash(rng, w[g], u); k[:, 13:] = 0; more = 255 * (g % 2)
        for q in range(N):
            for c in (look(u, m + 1), look(u, m)):
                z = k + 0; z[:, 14] = rng.integers(0, 3, n); x[q, g][:, c] = z.T
            z = k + 0; z[:, 13] = more; z[:, 15] = t[g] - more + rng.integers(-2, 1, n); x[q, g][:, p] = z.T
    return pack(x, np.broadcast_to(w, (N, 8, 16)), th)
def over_the_end(rng, x, w, g):
    p = W - L - 2; every = np.arange(W); first = look(every, 0); later = look(every, np.arange(1, P)[:, None])
    good = (first >= L) & (first < p - L)
    j, uk = np.nonzero((later > W - F) & good & ~np.any(later == p, axis=0))
    i = int(rng.integers(0, len(uk))); u = int(uk[i]); c1 = int(first[u]); c2 = int(later[j[i], u])
    a = int(rng.choice(every[good & (first != c1)])); ca = int(first[a])
    k = with_hash(rng, w[g], np.array([u]))[0]; k[15] = 0; near = k + 0; near[15] = 3
    ka = with_hash(rng, w[g], np.full(N, a))
    for q in range(N):
        x[q, g][:, [0, ca]] = ka[q][:, None]; x[q, g][:, c1] = near; x[q, g][:, [p, c2 - F]] = k[:, None]
def setup_inputs_ends(rng):
    x = far(rng); w = weights(rng); th = rng.integers(1, 60, (N, 8, 2))
    mm, uu = np.nonzero(look(np.arange(W), np.arange(M)[:, None]) >= W - L // 2)
    for g in range(8):
        if g % 4 == 3:
            over_the_end(rng, x, w, g); th[:, g] = rng.integers(4, 60, (N, 2))
            continue
        if g % 2 == 0:
            o = rng.permutation(len(uu)); c, i = np.unique(look(uu[o], mm[o]), return_index=True); u = uu[o][i]; p = L * rng.permutation(len(u))
        else:
            u = odd(rng, g % M, 1); c = look(u, g % M); p = np.array([W - 2])
        k = with_hash(rng, w[g], u)
        for q in range(N):
            x[q, g][:, c] = k.T; x[q, g][:, p] = k.T
    return pack(x, np.broadcast_to(w, (N, 8, 16)), th)
def setup_inputs_alike(rng):
    x = texture(rng); w = rng.integers(0, 256, (N, 8, 16)); th = rng.integers(20, 41, (N, 8, 2))
    for g in range(0, 8, 2):
        base = rng.integers(0, 256, (4, 16)); x[:, g] = base[rng.integers(0, 4, (N, W))].transpose(0, 2, 1)
    th[:, 0] = 1; th[:, 2] = 4096; th[:, 4, 0] = 0; th[:, 1, 0] = 4096; th[:, 1, 1] = 0; th[:, 3, 1] = 4096
    w[:, 6] = 0; w[:, 5] = 255
    x[:, 1, :, 0] = 255
    w[:, 7] = rng.integers(230, 256, (N, 16))
    up = rng.random((N, 1, W)) < 0.5; up[::2] = False
    x[:, 7] = np.where(up, 255 - rng.integers(0, 40, (N, 16, W)), rng.integers(0, 40, (N, 16, W)))
    for q in range(N):
        x[q, 1][:, L * (1 + rng.permutation(W // L - 1)[:W // L // 2])] = 0
        if q % 2 == 0:
            th[q, 7, 0] = rng.integers(150, 260); th[q, 7, 1] = rng.integers(3100, 3600)
        else:
            th[q, 7, 0] = rng.integers(2048, 3000); th[q, 7, 1] = rng.integers(100, 4097)
            c = look((255 * int(np.sum(w[q, 7]))) & (W - 1), 0); x[q, 7][:, [0, L, c]] = 255
    th[0, 7, 1] = 4096
    return pack(x, w, th)
def setup_inputs_spread(rng):
    x = np.minimum((np.exp2(8 * rng.random((N, 8, 1, W))) * rng.random((N, 8, 16, W))).astype(np.int64), 255)
    w = np.minimum(np.exp2(8 * rng.random((N, 8, 16))).astype(np.int64), 255) * (rng.random((N, 8, 16)) > 0.0625)
    return pack(x, w, np.minimum(np.exp2(12 * rng.random((N, 8, 2))).astype(np.int64), 4096))
def check_inputs(d):
    bad = []
    for k in ("x0", "wt"):
        v = np.asarray(d[k]).astype(np.float32)
        if not np.all((v >= 0) & (v <= 255) & (v == np.floor(v))): bad.append("whole numbers of " + k)
    v = np.asarray(d["th"])
    if np.min(v) < 0 or np.max(v) > 4096: bad.append("range of th")
    v = v.reshape(N, 8, 16, 2)
    if np.any(v != v[:, :, :1]): bad.append("rows of th alike in a group")
    return bad
def reference(x0, wt, th):
    x = x0.astype(np.float32).astype(np.int64).reshape(N, 8, 16, W); w = wt.astype(np.float32).astype(np.int64).reshape(N, 8, 16, 1)
    t = th.astype(np.int64).reshape(N, 8, 16, 2)[:, :, 0]; here = np.arange(W)
    for rnd in range(RO):
        u = np.add.reduce(w * x, axis=2) & (W - 1)
        nx = np.zeros_like(u) + ((here + 1) & (W - 1))
        for m in range(M - 1, -1, -1):
            c = look(u, m); near = np.add.reduce(np.abs(pick(x, c) - x), axis=2) < t[..., :1]
            nx = np.where(near, (c + 1) & (W - 1), nx)
        s = np.zeros((N, 8, W // L, L), np.int64); s[..., 0] = L * np.arange(W // L)
        for k in range(1, L): s[..., k] = np.take_along_axis(nx, s[..., k - 1], -1)
        jump = np.zeros(s.shape, bool); jump[..., :-1] = s[..., 1:] != ((s[..., :-1] + 1) & (W - 1))
        s = s.reshape(N, 8, W); jump = jump.reshape(N, 8, W)
        site = np.argsort(~jump, axis=-1, kind="stable")[..., :CAP]
        live = np.take_along_axis(jump, site, -1); ask = pick(x, np.take_along_axis(s, site, -1))
        found = np.zeros((N, 8, CAP), bool); fill = np.zeros((N, 8, 16, CAP, F), np.int64)
        for q in range(N):
            for d in range(1, N):
                b = (q + d) % N; cut = slice((d - 1) * Q, d * Q); a = ask[q][:, :, cut]
                v = np.add.reduce(w[b] * a, axis=1) & (W - 1); c = look(v[..., None], np.arange(P))
                off = np.add.reduce(np.abs(pick(x[b], c.reshape(8, -1)).reshape(8, 16, Q, P) - a[..., None]), axis=1)
                best = np.take_along_axis(c, np.argmin(off, axis=-1)[..., None], -1)
                found[q][:, cut] = np.min(off, axis=-1) < t[b][:, 1:]
                fill[q][:, :, cut] = pick(x[b], ((best + 1 + np.arange(F)) & (W - 1)).reshape(8, -1)).reshape(8, 16, Q, F)
        found = found & live
        more = np.zeros((N, 8, W), np.int64); np.put_along_axis(more, site, found.astype(np.int64) * F, -1)
        place = here + np.add.accumulate(more, axis=-1) - more
        z = np.zeros((N, 8, 16, W + F * CAP + 1), np.int64)
        np.put_along_axis(z, place[:, :, None], pick(x, s), -1)
        at = np.take_along_axis(place, site, -1)[..., None] + 1 + np.arange(F)
        at = np.where(found[..., None], at, W + F * CAP).reshape(N, 8, 1, CAP * F)
        np.put_along_axis(z, at, fill.reshape(N, 8, 16, CAP * F), -1)
        x = np.ascontiguousarray(z[..., :W])
    return {"y": x.reshape(N, 128, W).astype(np.float32).astype(BF)}

@@ -1,0 +1,581 @@
+from concourse.bass import DstId, RemoteDMATransfer
+from concourse.mybir import AluOpType as Op, ActivationFunctionType as AF
+
+NR, W, F, RO = 8, 2048, 4, 2
+ND = NR - 1
+NS = ND * 16
+XW = 3072
+NONE = 2064
+DUMP = 2560
+SL = 3
+ENG = 2
+
+SB = {
+    "X0": (XW, "bfloat16"), "X1": (XW, "bfloat16"), "X2": (XW, "bfloat16"), "XC": (2048, "bfloat16"), "wtb": (1, "bfloat16"), "thi": (2, "int32"),
+    "t1f": (1, "float32"), "t2f": (1, "float32"), "ones": (2048, "bfloat16"),
+    "B144": (144, "bfloat16"), "Z": (144, "bfloat16"), "WZ": (144, "bfloat16"), "Z16": (144, "bfloat16"), "BOm2": (128, "bfloat16"),
+    "TriS": (128, "bfloat16"), "TriI": (128, "bfloat16"), "Id": (128, "bfloat16"), "NId": (128, "bfloat16"), "EZ": (2048, "bfloat16"),
+    "M16": (256, "bfloat16"), "R16c": (128, "bfloat16"), "Rk": (128, "bfloat16"), "Rs": (128, "bfloat16"), "R64k": (64, "bfloat16"),
+    "Rc": (128, "bfloat16"), "WM": (256, "bfloat16"), "MOFF": (112, "float32"), "PP": (128, "float32"), "S2048": (16, "float32"),
+    "D640": (8, "float32"), "RSW": (256, "bfloat16"), "R1": (128, "bfloat16"), "R2": (128, "bfloat16"), "S128": (256, "float32"),
+    "N112": (112, "float32"), "MB": (112, "bfloat16"), "MT": (112, "int32"), "IT": (128, "bfloat16"), "ITa": (128, "bfloat16"),
+    "O16": (128, "float32"), "tw": (64, "int32"), "tq": (64, "int32"), "tr": (64, "int32"), "tb": (448, "int32"), "tc": (448, "float32"),
+    "tl": (448, "float32"), "tk": (512, "float32"), "KTw": (64, "bfloat16"), "KT": (1024, "bfloat16"),
+    "vI": (128, "int32"), "u": (128, "int32"), "h": (128, "int32"), "hb": (128, "bfloat16"), "KK": (1024, "float32"),
+    "QI": (1024, "int32"), "OI": (1024, "int32"), "OF": (1024, "uint16"), "G7": (2048, "bfloat16"), "G6": (2048, "bfloat16"),
+    "E": (1024, "bfloat16"), "HS": (1024, "bfloat16"), "K3": (128, "float32"), "q3": (128, "int32"), "c3": (128, "int32"),
+    "dp": (128, "float32"), "cc": (128, "float32"), "DV": (128, "float32"), "D2": (128, "float32"), "c10": (128, "float32"),
+    "h5": (128, "float32"), "TF": (128, "float16"),
+    "NX": (2064, "float32"), "GM": (256, "float16"), "CH": (256, "float16"), "LS": (128, "uint16"),
+    "SA": (128, "float32"), "XS": (2048, "bfloat16"), "dI": (128, "int32"), "dA": (128, "int32"), "D1": (128, "bfloat16"),
+    "CT": (128, "bfloat16"), "CQ": (128, "bfloat16"), "zz": (16, "float32"), "zs": (16, "float32"), "XB": (24, "float32"), "bs": (16, "float32"),
+    "ps": (16, "float32"), "pl": (16, "uint16"), "VAL": (256, "float32"), "SW": (2304, "float32"), "nm": (112, "float32"),
+    "YB": (224, "float32"), "YM": (224, "float32"), "YC": (224, "float32"), "VI": (112, "int32"), "PL": (112, "int32"),
+    "wi": (16, "int32"), "wq": (8, "int32"), "wr": (8, "float32"), "wx": (8, "float32"), "kl": (8, "uint16"),
+    "PR": (112, "float32"), "PM": (112, "float16"), "PC": (112, "float16"), "sl": (8, "uint16"), "P4": (8, "float32"), "nl": (112, "float32"),
+    "aI": (8, "int32"), "U16": (112, "int32"), "H16": (112, "int32"), "K16": (112, "int32"), "Q16": (112, "int32"), "C16": (112, "int32"),
+    "OA": (112, "uint16"), "A4": (448, "bfloat16"), "DA": (1792, "bfloat16"),
+    "k1": (56, "float32"), "k2": (56, "float32"), "k3": (32, "float32"), "k4": (16, "float32"), "kb": (8, "float32"),
+    "bi": (8, "int32"), "bm": (8, "int32"), "b2": (8, "float32"), "b3": (8, "float32"), "b4": (8, "int32"), "b5": (8, "int32"), "nf": (8, "float32"),
+    "cf": (8, "float32"), "OL": (32, "uint16"),
+    "FM": (112, "bfloat16"), "FC": (112, "bfloat16"), "X7": (8, "float32"), "in7": (8, "float32"), "A7": (8, "float32"), "zf": (8, "float32"),
+    "zd": (8, "float32"), "AQ": (8, "float32"), "Ai": (8, "int32"), "lh": (16, "int32"), "lf": (16, "float32"), "hh": (8, "float32"),
+    "SL": (32, "uint16"), "LD": (896, "bfloat16"), "RG": (896, "bfloat16"), "RE": (896, "bfloat16"), "SR": (128, "uint16"),
+}
+HOME = {}
+
+
+def _pack():
+    homes, n = {}, {}
+    for k, (c, d) in SB.items():
+        if c > 448 or k in ("wtb", "thi"):
+            homes[k] = (c, d)
+            HOME[k] = (k, 0)
+        else:
+            h = "pool_" + d
+            o = n.get(h, 0)
+            HOME[k] = (h, o)
+            n[h] = o + (c + 15) // 16 * 16
+            homes[h] = (n[h], d)
+    return homes
+
+
+SCRATCH = {k: ("sbuf", [128, c], d) for k, (c, d) in _pack().items()}
+for _i in range(8):
+    SCRATCH["D%d_" % _i] = ("sbuf", [128, 2048], "bfloat16")
+    HOME["D%d_" % _i] = ("D%d_" % _i, 0)
+    SCRATCH["p%d" % _i] = ("psum", [128, 512], "float32")
+    HOME["p%d" % _i] = ("p%d" % _i, 0)
+for _i in range(RO):
+    for _n, _c in (("AS", 112), ("AL", 112), ("FS", 448), ("FL", 448)):
+        SCRATCH["%s%d" % (_n, _i)] = ("sbuf", [128, _c], "bfloat16")
+        HOME["%s%d" % (_n, _i)] = ("%s%d" % (_n, _i), 0)
+SEMAPHORES = ["qV", "qS", "qP", "qG", "dX", "dW", "dT", "dY"] + ["%s%d" % (n, i) for i in range(RO) for n in ("ask", "ans", "la", "lb")]
+
+
+def rank_program(g, core, T, topo):
+    rank = T.rank_of(core)
+    if rank is None:
+        return
+    queues = {"V": g.vector, "S": g.scalar, "P": g.tensor, "G": g, "Y": g.sync}
+    done = {q: 0 for q in queues}
+    known = {q: {} for q in queues}
+    clocks, log = {}, {}
+
+    def A(name, lo=0, hi=None, st=1, parts=128):
+        home, o = HOME[name]
+        if hi is None:
+            hi = SB[name][0] if name in SB else SCRATCH[name][1][1]
+        ap = T[home][0:parts, o + lo:o + hi] if st == 1 else T[home][0:parts, o + lo:o + hi:st]
+        return (ap, [(home, o + lo, o + hi, st)])
+
+    def I(win, off):
+        return (win[0].indirect(off[0]), win[1] + off[1])
+
+    def apart(lo, hi, st, lo2, hi2, st2):
+        return lo >= hi2 or lo2 >= hi or (st == st2 and st > 1 and (lo - lo2) % st != 0)
+
+    def sync(q, outs, ins):
+        need = {}
+        for w, regs in ((True, outs), (False, ins)):
+            for (n, lo, hi, st) in regs:
+                bank = n[0] == "p" and n[1].isdigit()
+                for (q2, i2, lo2, hi2, st2, w2) in log.get(n, ()):
+                    if bank and q2 != q:
+                        hit = True
+                    elif q2 == q and q == "P":
+                        hit = False
+                    else:
+                        hit = (w or w2) and not apart(lo, hi, st, lo2, hi2, st2)
+                    if hit:
+                        need[q2] = max(need.get(q2, 0), i2)
+        k = known[q]
+        for q2, i2 in sorted(need.items(), key=lambda t: -sum(clocks[t].values())):
+            if k.get(q2, 0) >= i2:
+                continue
+            queues[q].wait_ge(T.sem[q2 if q2 not in queues else "q" + q2], i2)
+            for a, b in clocks[(q2, i2)].items():
+                k[a] = max(k.get(a, 0), b)
+
+    def note(q, i, outs, ins):
+        for w, regs in ((True, outs), (False, ins)):
+            for (n, lo, hi, st) in regs:
+                def inside(e):
+                    return lo <= e[2] and e[3] <= hi and (st == 1 or (e[4] == st and (e[2] - lo) % st == 0))
+                l = log.setdefault(n, [])
+                if w:
+                    l[:] = [e for e in l if not (inside(e) and e[1] <= clocks[(q, i)].get(e[0], 0))]
+                l[:] = [e for e in l if not (e[0] == q and e[5] == w and inside(e))]
+                l.append((q, i, lo, hi, st, w))
+
+    def do(q, call, outs, ins):
+        o = [r for x in outs for r in x[1]]
+        n = [r for x in ins for r in x[1]]
+        sync(q, o, n)
+        done[q] += 1
+        call().then_inc(T.sem["q" + q], 1)
+        c = dict(known[q])
+        c[q] = done[q]
+        clocks[(q, done[q])] = c
+        note(q, done[q], o, n)
+
+    def event(sem, val, outs, ins, base):
+        c = dict(base)
+        c[sem] = val
+        clocks[(sem, val)] = c
+        note(sem, val, [r for x in outs for r in x[1]], [r for x in ins for r in x[1]])
+
+    def load(q, sem, out, src):
+        queues[q].dma_start(out[0], src).then_inc(T.sem[sem], 16)
+        event(sem, 16, [out], [], known[q])
+
+    def cp(out, in_):
+        do("V", lambda: g.vector.tensor_copy(out[0], in_[0]), [out], [in_])
+
+    def tt(out, a, b, op):
+        do("V", lambda: g.vector.tensor_tensor(out[0], a[0], b[0], op), [out], [a, b])
+
+    def ts(out, a, s1, op0, s2=None, op1=None):
+        col = isinstance(s1, tuple)
+        x1 = s1[0] if col else s1
+        ins = [a, s1] if col else [a]
+        if op1 is None:
+            do("V", lambda: g.vector.tensor_scalar(out[0], a[0], x1, None, op0), [out], ins)
+        else:
+            do("V", lambda: g.vector.tensor_scalar(out[0], a[0], x1, s2, op0, op1), [out], ins)
+
+    def scan(out, a, b, op0=Op.mult, op1=Op.add):
+        do("V", lambda: g.vector.tensor_tensor_scan(out[0], a[0], b[0], 0.0, op0, op1), [out], [a, b])
+
+    def fill(out, c):
+        do("V", lambda: g.vector.memset(out[0], c), [out], [])
+
+    def act(out, in_, f=AF.Copy, **kw):
+        ins = [in_] + [x for x in kw.values() if isinstance(x, tuple)]
+        k2 = {a: x[0] if isinstance(x, tuple) else x for a, x in kw.items()}
+        do("S", lambda: g.scalar.activation(out[0], in_[0], f, **k2), [out], ins)
+
+    def mm(out, l, r, start=True, stop=True):
+        do("P", lambda: g.tensor.matmul(out[0], l[0], r[0], start, stop), [out], [l, r])
+
+    def sel(out, in_, pat, op, base, cm):
+        do("G", lambda: g.affine_select(out[0], in_[0], pat, op, 0.0, base, cm), [out], [in_])
+
+    def iota(out, pat, base, cm):
+        do("G", lambda: g.iota(out[0], pat, base, cm, allow_small_or_imprecise_dtypes=True), [out], [])
+
+    def Z(name, i):
+        return A(name, 15 - i, 143 - i)
+
+    def EZ(i):
+        return A("EZ", 128 * i, 128 * i + 128)
+
+    BO = A("B144", 0, 128)
+    L16 = A("M16", 0, 128, parts=16)
+    WP = A("p7", 384, 384 + NS)
+    TH = A("p7", 256, 256 + NS)
+
+    load("Y", "dX", A("X0", 0, W), T.x0[:])
+    load("S", "dW", A("wtb"), T.wt[:])
+    load("S", "dT", A("thi"), T.th[:])
+    fill(A("ones", 0, 256), 1.0)
+    fill(A("ones", 256, 2048), 1.0)
+    iota(A("R64k", parts=16), [[0, 64]], 0, 64)
+    iota(A("Rc"), [[1, 128]], 0, 0)
+    sel(A("M16", parts=16), A("ones", 0, 256, parts=16), [[0, 16], [1, 16]], Op.is_equal, 0, -1)
+    sel(A("B144"), A("ones", 0, 144), [[-16, 9], [0, 16]], Op.is_ge, 0, 1)
+    sel(A("B144"), A("B144"), [[16, 9], [0, 16]], Op.is_ge, 15, -1)
+    sel(A("Z"), A("B144"), [[0, 9], [1, 16]], Op.is_equal, -15, 0)
+    sel(A("Id"), A("ones", 0, 128), [[-1, 128]], Op.is_equal, 0, 1)
+    iota(A("R16c", parts=16), [[16, 128]], 0, 0)
+    iota(A("Rk", parts=16), [[0, 128]], 0, 1)
+    iota(A("Rs", parts=16), [[0, 128]], -2 * NS, 1)
+    sel(A("EZ"), A("ones"), [[-1, 16], [-16, 8], [0, 16]], Op.is_equal, 0, 1)
+    sel(A("RSW"), A("ones", 0, 256), [[0, 16], [1, 16]], Op.is_gt, 0, 0)
+    sel(A("R1"), A("ones", 0, 128), [[0, 16], [1, 8]], Op.not_equal, -1, 0)
+    sel(A("TriS"), BO, [[1, 128]], Op.is_gt, 0, -1)
+    sel(A("TriI"), BO, [[1, 128]], Op.is_ge, 0, -1)
+    iota(A("S128"), [[128, 256]], 128, 0)
+    iota(A("N112"), [[1, 112]], 0, 0)
+    iota(A("MB"), [[1, 16], [0, 7]], 0, 0)
+    iota(A("MT"), [[2, 16], [0, 7]], 1, 0)
+    iota(A("ITa"), [[0, 8], [1, 16]], 1, 0)
+    fill(A("X0", W, W + 32), -1.0)
+    fill(A("tk", 0, 64), -8.0)
+    fill(A("E"), 0.0)
+    fill(A("D1"), 0.0)
+    fill(A("XB"), 0.0)
+    fill(A("X7"), 0.0)
+    mm(A("p7", 0, 256), L16, A("M16", parts=16))
+    mm(A("p5", 0, 64), L16, A("R64k", parts=16), True, False)
+    mm(A("p5", 0, 64), L16, A("Rc", 0, 64, parts=16), False, True)
+    cp(A("tw"), A("p5", 0, 64))
+
+    def part(name, k):
+        return A(name, 64 * k, 64 * k + 64)
+
+    ts(A("tq"), A("tw"), 127, Op.bitwise_and)
+    ts(A("tr"), A("tw"), 7, Op.logical_shift_right)
+    for k in range(7):
+        ts(part("tb", k), A("tq"), 6 - k, Op.logical_shift_right, 1, Op.bitwise_and)
+    cp(part("tc", 0), part("tb", 0))
+    for k in range(1, 7):
+        tt(part("tc", k), part("tc", k - 1), part("tb", k), Op.add)
+    ts(A("WZ"), A("Z"), A("wtb"), Op.mult)
+    cp(A("t1f"), A("thi", 0, 1))
+    ts(A("t2f"), A("thi", 1, 2), 16.0, Op.mult)
+    for k in range(7):
+        tt(part("tl", k), part("tc", k), A("tr"), Op.is_le)
+    for k in range(7):
+        tt(A("KTw") if k == 6 else part("tk", k + 1), part("tk", k), part("tl", k), Op.add)
+
+    def constants_1():
+        mm(A("p6", 0, 128), L16, A("R16c", parts=16), True, False)
+        mm(A("p6", 0, 128), L16, A("Rk", parts=16), False, True)
+        act(A("PP"), A("p6", 0, 128))
+        act(A("Z16"), A("Z"), scale=16.0)
+        act(A("BOm2"), BO, scale=-2.0)
+        act(A("R2"), A("R1"), scale=2.0)
+        act(A("MOFF"), A("WM", 0, NS), scale=-1000.0, bias=1000.0)
+        act(A("S2048"), A("PP", 0, 16), bias=2048.0)
+        act(A("D640", 0, 7), A("PP", 0, 7), bias=float(DUMP // 4))
+        act(A("SA", 0, 128, 8), A("PP", 0, 16), scale=8.0)
+
+    def constants_2():
+        cp(WP, A("WM", 0, NS))
+        tt(A("O16"), A("ITa"), BO, Op.mult)
+        ts(A("IT"), A("O16"), 1.0, Op.subtract)
+
+    def table():
+        for i in range(16):
+            mm(A("p%d" % (4 + i // 8), 64 * (i % 8), 64 * (i % 8) + 64), EZ(i), A("KTw"))
+        for b in range(2):
+            act(A("KT", 512 * b, 512 * b + 512), A("p%d" % (4 + b)))
+
+    def exchange(src, dst, w, ls, rs, back):
+        sync("G", [], A(src)[1])
+        tr = []
+        for d in range(1, NR):
+            to = T.cores[(rank - d) % NR if back else (rank + d) % NR]
+            rid, pid, _ = topo.addr(to)
+            mask = 0
+            for e in topo.engines(core, to)[ENG * (d - 1):ENG * d]:
+                mask |= 1 << e
+            tr.append(RemoteDMATransfer(dst_ids=[DstId(rid=rid, pnc=pid)], dma_engine_mask=mask, remote_sem=T.sem[rs],
+                                        src=A(src, w * (d - 1), w * d)[0], dst=A(dst, w * (d - 1), w * d)[0]))
+        g.remote_dma_fused(tr, local_sem=T.sem[ls])
+        event(rs, ENG * ND, [A(dst)], [], {})
+
+    def one_round(rnd):
+        X, XN = "X%d" % rnd, "X%d" % (rnd + 1)
+        AL, AS, FL, FS = ("%s%d" % (n, rnd) for n in ("AL", "AS", "FL", "FS"))
+        win = A(X, 0, W + 32)
+        first = 7 - SL // 2
+
+        def half(name, b):
+            return A(name, 1024 * b, 1024 * b + 1024)
+
+        for i in range(16):
+            mm(A("p0", 0, 128), Z("WZ", i), A(X, i, W, 16), i == 0, i == 15)
+        if rnd == 0:
+            act(A("WM"), A("p7", 0, 256))
+            act(A("NId"), A("Id"), scale=-1.0)
+        for b in range(2):
+            act(half("XC", b), half(X, b))
+        cp(A("vI"), A("p0", 0, 128))
+        ts(A("u"), A("vI"), 2047, Op.bitwise_and)
+        ts(A("h"), A("u"), 5, Op.logical_shift_right)
+        cp(A("hb"), A("h"))
+        cp(A("p7", 0, 128), A("u"))
+
+        def plus(m):
+            act(A("KK", 128 * m, 128 * m + 128), A("hb"), bias=float(2 * m + 1))
+
+        def look(m):
+            return A("OI", 128 * m, 128 * m + 128)
+
+        def prep(m0, m1):
+            for m in range(m0, m1):
+                tt(A("QI", 128 * m, 128 * m + 128), A("KK", 128 * m, 128 * m + 128), A("p7", 0, 128), Op.mult)
+            ts(A("OI", 128 * m0, 128 * m1), A("QI", 128 * m0, 128 * m1), 2047, Op.bitwise_and)
+            cp(A("OF", 128 * m0, 128 * m1), A("OI", 128 * m0, 128 * m1))
+
+        def offs(m, b):
+            return A("OF", 128 * m + 64 * b, 128 * m + 64 * b + 64)
+
+        def pd(m, b=None):
+            bank, o = (("p0", 0), ("p6", 0), ("p1", 0), ("p1", 1))[m] if m < 4 else ("p2", m - 4)
+            return A(bank, 128 * o, 128 * o + 128) if b is None else A(bank, 128 * o + 64 * b, 128 * o + 64 * b + 64)
+
+        def gather(m, b):
+            tt(half("D%d_" % m, b), I(win, offs(m, b)), half("XC", b), Op.subtract)
+
+        def absum(m, b):
+            d = half("D%d_" % m, b)
+            act(d, d, AF.Abs)
+            sums(m, b)
+
+        def sums(m, b):
+            for i in range(16):
+                mm(pd(m, b), Z("Z", i), A("D%d_" % m, 1024 * b + i, 1024 * b + 1024, 16), i == 0, i == 15)
+
+        def near(m):
+            ts(A("E", 8 - m, 1024, 8), pd(m), A("t1f"), Op.is_ge)
+
+        order = [(m, b) for m in range(7, -1, -1) for b in range(2)]
+        theirs = order[SL:]
+
+        def own(m):
+            bs = [b for b in range(2) if (m, b) in order[:SL]]
+            for b in bs:
+                act(half("G%d" % m, b), I(win, offs(m, b)))
+                if (m, b) == (7, 0):
+                    for x in range(first - 1, -1, -1):
+                        plus(x)
+            for b in bs:
+                for x in (2 * b, 2 * b + 1):
+                    mm(A("p%d" % (3 + x)), A("NId"), A(X, 512 * x, 512 * x + 512), True, False)
+                    mm(A("p%d" % (3 + x)), A("Id"), A("G%d" % m, 512 * x, 512 * x + 512), False, True)
+            for b in bs:
+                for x in (2 * b, 2 * b + 1):
+                    act(A("D%d_" % m, 512 * x, 512 * x + 512), A("p%d" % (3 + x)), AF.Abs)
+                sums(m, b)
+
+        for m in range(7, first - 1, -1):
+            plus(m)
+        prep(7, 8)
+        own(7)
+        prep(first, 7)
+        for n, (m, b) in enumerate(theirs):
+            gather(m, b)
+            if n == 0:
+                if rnd == 0:
+                    constants_1()
+                own(6)
+                act(A("h5"), A("hb"), bias=5.0)
+            if n == 1 - SL % 2:
+                prep(0, first)
+            if n:
+                absum(*theirs[n - 1])
+            if (m, b) == (3, 0) and rnd == 0:
+                table()
+            if (m, b) == (2, 1):
+                if rnd == 0:
+                    constants_2()
+                for x in range(7, 3, -1):
+                    near(x)
+                fill(A("SW", 0, NS), 0.0)
+        absum(*theirs[-1])
+
+        tt(A("c10"), look(1), look(0), Op.subtract)
+        near(3)
+        near(2)
+        scan(A("HS"), A("E"), A("E"))
+        M = A("HS", 6, 1024, 8)
+        T1, T2 = A("p7", 128, 256), A("p7", 256, 384)
+        ts(T1, M, 2.0, Op.mult)
+        ts(T2, M, 6.0, Op.is_ge)
+        tt(A("K3"), T1, A("h5"), Op.add)
+        tt(A("q3"), A("K3"), A("p7", 0, 128), Op.mult)
+        ts(A("c3"), A("q3"), 2047, Op.bitwise_and)
+        tt(A("dp"), A("PP"), A("c3"), Op.subtract)
+        tt(A("cc"), A("c3"), look(1), Op.subtract)
+        tt(T1, T2, A("dp"), Op.mult)
+        tt(A("D2"), T1, A("cc"), Op.add)
+        ts(A("p2", 256, 384), pd(1), A("t1f"), Op.is_ge)
+        tt(A("p2", 384, 512), A("p2", 256, 384), A("D2"), Op.mult)
+        tt(A("DV"), A("p2", 384, 512), A("c10"), Op.add)
+        places = ((("p3", 0, 8, "V"), ("p4", 8, 16, "S")), (("p5", 0, 7, "S"), ("p6", 7, 13, "V"), ("p1", 13, 16, "S")))
+        for b in range(2):
+            lo, hi = 64 * b, 64 * b + 64
+            e, d = A("p2", lo, hi), A("p2", 128 + lo, 128 + hi)
+            ts(e, pd(0, b), A("t1f"), Op.is_ge)
+            tt(d, e, A("DV", lo, hi), Op.mult)
+            tt(A("TF", lo, hi), d, A("OI", lo, hi), Op.add)
+            for p, i0, i1, q in places[b]:
+                for i in range(i0, i1):
+                    mm(A(p, 64 * (i - i0), 64 * (i - i0) + 64), EZ(i), A("TF", lo, hi))
+        for b in range(2):
+            for p, i0, i1, q in places[b]:
+                for i in range(i0, i1):
+                    o, n = A("NX", i + 1024 * b, 1024 * b + 1024, 16), A(p, 64 * (i - i0), 64 * (i - i0) + 64)
+                    if q == "V":
+                        ts(o, n, 1.0, Op.add)
+                    else:
+                        act(o, n, bias=1.0)
+        cp(A("NX", W, W + 1), A("NX", 0, 1))
+        cp(A(X, W, W + 4), A(X, 0, 4))
+
+        act(A("XS", 0, W, 8), A(X, 0, W, 8))
+        for k in range(1, 8):
+            if k == 1:
+                tt(A("GM"), A("NX", 0, W, 8), A("WM"), Op.mult)
+            else:
+                tt(A("GM"), I(A("NX", 0, W + 1), A("LS", 16 * k - 16, 16 * k)), A("WM"), Op.mult)
+            scan(A("CH"), A("RSW"), A("GM"))
+            cp(A("LS", 16 * k, 16 * k + 16), A("CH", 15, 256, 16))
+            cp(A("SA", k, 128, 8), A("CH", 15, 256, 16))
+            act(A("XS", k, W, 8), I(win, A("LS", 16 * k, 16 * k + 16)))
+
+        tt(A("dI", 0, 127), A("SA", 1, 128), A("SA", 0, 127), Op.subtract)
+        ts(A("dA", 0, 127), A("dI", 0, 127), 2047, Op.bitwise_and)
+        ts(A("D1", 1, 128), A("dA", 0, 127), 1.0, Op.not_equal)
+        scan(A("CT"), A("R1"), A("D1"))
+        TW = A("CT", 7, 128, 8)
+        mm(A("p7", 16, 32), BO, TW)
+        mm(A("p7", 0, 16), A("TriS"), TW)
+        scan(A("CQ"), A("R2"), A("D1"))
+        for i in range(16):
+            mm(A("p0", i, 256, 16), EZ(i), A("CQ", 7, 128, 8))
+        ts(A("zz"), TW, 0.0, Op.is_equal)
+        tt(A("zs"), A("zz"), A("S2048"), Op.mult)
+        scan(A("XB", 1, 17), A("ones", 0, 16), A("p7", 16, 32))
+        tt(A("bs"), A("p7", 0, 16), A("XB", 0, 16), Op.add)
+        tt(A("ps"), A("bs"), A("zs"), Op.max)
+        cp(A("pl"), A("ps"))
+        tt(A("VAL"), A("p0", 0, 256), A("S128"), Op.add)
+        cp(I(A("SW"), A("pl")), A("VAL"))
+        scan(A("YB", 0, NS), A("SW", 0, NS), A("SW", 0, NS), Op.max, Op.max)
+        ts(A("nm"), A("SW", 0, NS), 0.0, Op.is_equal)
+        scan(A("YB", NS, 2 * NS), A("nm"), A("nm"))
+        tt(A("YM", 0, NS), A("YB", 0, NS), WP, Op.mult)
+        tt(A("YM", NS, 2 * NS), A("YB", NS, 2 * NS), WP, Op.mult)
+        scan(A("YC"), A("RSW", 0, 2 * NS), A("YM"))
+        cp(A("wi", 0, 7), A("YC", 15, NS, 16))
+        ts(A("wr", 0, 7), A("YC", NS + 15, 2 * NS, 16), 7.0, Op.min, 128.0, Op.mult)
+        ts(A("wq", 0, 7), A("wi", 0, 7), 127, Op.bitwise_and)
+        tt(A("wx", 0, 7), A("wr", 0, 7), A("wq", 0, 7), Op.add)
+        cp(A("kl", 0, 7), A("wx", 0, 7))
+        cp(A("VI"), A("YB", 0, NS))
+        ts(A("PL"), A("VI"), 4, Op.logical_shift_right, 65528, Op.bitwise_and)
+        tt(A("PR"), I(A("KT"), A("kl", 0, 7)), A("PL"), Op.add)
+        tt(A("PM"), A("PR"), WP, Op.mult)
+        scan(A("PC"), A("RSW", 0, NS), A("PM"))
+        cp(A("sl", 0, 7), A("PC", 15, NS, 16))
+        cp(A(AS), I(A("XS"), A("sl", 0, 7)))
+        exchange(AS, AL, 16, "la%d" % rnd, "ask%d" % rnd, False)
+        ts(A("P4", 0, 7), A("PC", 15, NS, 16), 3.0, Op.subtract, 0.25, Op.mult)
+        ts(A("nl"), A("N112"), A("XB", 16, 17), Op.is_ge, 1000.0, Op.mult)
+        tt(TH, A("nl"), A("MOFF"), Op.max)
+
+        for i in range(16):
+            mm(A("p0", 0, 7), Z("WZ", i), A(AL, i, NS, 16), i == 0, i == 15)
+        for b in range(4):
+            act(A("A4", NS * b, NS * b + NS), A(AL))
+        cp(A("aI", 0, 7), A("p0", 0, 7))
+        ts(A("U16", 0, 7), A("aI", 0, 7), 2047, Op.bitwise_and)
+        for n in (7, 14, 28, 56):
+            cp(A("U16", n, 2 * n), A("U16", 0, n))
+        ts(A("H16"), A("U16"), 5, Op.logical_shift_right)
+        tt(A("K16"), A("H16"), A("MT"), Op.add)
+        tt(A("Q16"), A("K16"), A("U16"), Op.mult)
+        ts(A("C16"), A("Q16"), 2047, Op.bitwise_and)
+        cp(A("OA"), A("C16"))
+
+        def quarter(b):
+            return A("DA", 448 * b, 448 * b + 448)
+
+        act(A("G7", 0, 448), I(win, A("OA", 0, 28)))
+        mm(A("p3", 0, 448), A("NId"), A("A4"), True, False)
+        mm(A("p3", 0, 448), A("Id"), A("G7", 0, 448), False, True)
+        for b in range(1, 4):
+            tt(quarter(b), I(win, A("OA", 28 * b, 28 * b + 28)), A("A4"), Op.subtract)
+            act(quarter(b), quarter(b), AF.Abs)
+            if b == 1:
+                act(quarter(0), A("p3", 0, 448), AF.Abs)
+        for b in range(2):
+            o = A("p%d" % (1 + b), 0, 56)
+            mm(o, A("Id"), A("MB", 56 * b, 56 * b + 56), True, False)
+            for i in range(16):
+                mm(o, Z("Z16", i), A("DA", 896 * b + i, 896 * b + 896, 16), False, i == 15)
+        cp(A("k1"), A("p1", 0, 56))
+        tt(A("k2"), A("p2", 0, 56), A("k1"), Op.min)
+        tt(A("k3", 0, 28), A("k2", 0, 28), A("k2", 28, 56), Op.min)
+        tt(A("k4", 0, 14), A("k3", 0, 14), A("k3", 14, 28), Op.min)
+        tt(A("kb", 0, 7), A("k4", 0, 7), A("k4", 7, 14), Op.min)
+        cp(A("bi", 0, 7), A("kb", 0, 7))
+        ts(A("nf", 0, 7), A("kb", 0, 7), A("t2f"), Op.is_ge, float(NONE - 1), Op.mult)
+        ts(A("bm", 0, 7), A("bi", 0, 7), 15, Op.bitwise_and)
+        ts(A("b2", 0, 7), A("bm", 0, 7), 2.0, Op.mult, 1.0, Op.add)
+        tt(A("b3", 0, 7), A("b2", 0, 7), A("H16", 0, 7), Op.add)
+        tt(A("b4", 0, 7), A("b3", 0, 7), A("U16", 0, 7), Op.mult)
+        ts(A("b5", 0, 7), A("b4", 0, 7), 2047, Op.bitwise_and)
+        tt(A("cf", 0, 7), A("b5", 0, 7), A("nf", 0, 7), Op.max)
+        for f in (2, 3, 0, 1):
+            ts(A("OL", 8 * f, 8 * f + 7), A("cf", 0, 7), float(1 + f), Op.add)
+            if f > 1:
+                act(A(FS, f, 448, F), I(win, A("OL", 8 * f, 8 * f + 7)))
+        for f in (0, 1):
+            cp(A(FS, f, 448, F), I(win, A("OL", 8 * f, 8 * f + 7)))
+        exchange(FS, FL, 64, "lb%d" % rnd, "ans%d" % rnd, True)
+
+        CN = A("p4", 0, 128)
+        mm(CN, L16, A("R16c", parts=16), True, False)
+        mm(CN, L16, A("Rs", parts=16), False, False)
+        tt(A("FM"), A(FL, 0, 448, F), TH, Op.is_ge)
+        scan(A("FC"), A("RSW", 0, NS), A("FM"))
+        FW = A("FC", 15, NS, 16)
+        mm(A("p7", 8, 15), BO, FW)
+        mm(A("p7", 0, 7), A("TriI"), FW)
+        ts(A("zf", 0, 7), FW, 0.0, Op.is_equal)
+        tt(A("zd", 0, 7), A("zf", 0, 7), A("D640", 0, 7), Op.mult)
+        scan(A("X7", 1, 8), A("ones", 0, 7), A("p7", 8, 15))
+        tt(A("in7", 0, 7), A("p7", 0, 7), A("X7", 0, 7), Op.add)
+        tt(A("A7", 0, 7), A("in7", 0, 7), A("P4", 0, 7), Op.add)
+        tt(A("AQ", 0, 7), A("A7", 0, 7), A("zd", 0, 7), Op.max)
+        ts(A("Ai", 0, 7), A("AQ", 0, 7), 4.0, Op.mult)
+        ts(A("lh", 7, 14), A("Ai", 0, 7), 4, Op.logical_shift_right)
+        ts(A("lh", 0, 7), A("Ai", 0, 7), 15, Op.bitwise_and)
+        cp(A("lf", 0, 14), A("lh", 0, 14))
+        ts(A("hh", 0, 7), A("lf", 7, 14), -1.0, Op.mult, -0.5, Op.add)
+        for d in range(ND):
+            rg, ld, re_ = (A(n, 128 * d, 128 * d + 128) for n in ("RG", "LD", "RE"))
+            act(rg, A("Rc"), AF.Sign, bias=A("hh", d, d + 1))
+            mm(CN, A("BOm2"), rg, False, False)
+            ts(ld, A("IT"), A("lf", d, d + 1), Op.is_ge, -4.0, Op.mult)
+            ts(re_, A("Rc"), A("lf", 7 + d, 8 + d), Op.is_equal)
+            mm(CN, ld, re_, False, d == ND - 1)
+        for f in range(F):
+            ts(A("SL", 8 * f, 8 * f + 7), A("AQ", 0, 7), 4.0, Op.mult, float(f), Op.add)
+        cp(A("SR"), CN)
+        act(A(XN, 1024, 2048), I(A("XS"), A("SR", 64, 128)))
+        cp(A(XN, 0, 1024), I(A("XS"), A("SR", 0, 64)))
+        for f in range(F):
+            cp(I(A(XN), A("SL", 8 * f, 8 * f + 7)), A(FL, f, 448, F))
+        if rnd < RO - 1:
+            fill(A(XN, W, W + 32), -1.0)
+
+    for rnd in range(RO):
+        one_round(rnd)
+
+    y = A("X%d" % RO, 0, W)
+    sync("Y", [], y[1])
+    g.sync.dma_start(T.y[:], y[0]).then_inc(T.sem.dY, 16)
+    g.sync.wait_ge(T.sem.dY, 16)
+    for s in ("dX", "dW", "dT"):
+        g.wait_ge(T.sem[s], 16)
+    for q in ("V", "S", "P", "G"):
+        g.wait_ge(T.sem["q" + q], done[q])
+    for rnd in range(RO):
+        for n in ("la", "lb", "ask", "ans"):
+            g.wait_ge(T.sem["%s%d" % (n, rnd)], ENG * ND)

@@ -5,42 +5,41 @@ NR, W, F, RO = 8, 2048, 4, 2
 ND = NR - 1
 NS = ND * 16
 XW = 3072
-NONE = 2064
+NONE = 2056
 DUMP = 2560
-SL = 3
+FB = 16 * (F + 1)
+BIG = 2.0 ** 31
 ENG = 2
+TAG = [""]
 
 SB = {
     "X0": (XW, "bfloat16"), "X1": (XW, "bfloat16"), "X2": (XW, "bfloat16"), "XC": (2048, "bfloat16"), "wtb": (1, "bfloat16"), "thi": (2, "int32"),
     "t1f": (1, "float32"), "t2f": (1, "float32"), "ones": (2048, "bfloat16"),
-    "B144": (144, "bfloat16"), "Z": (144, "bfloat16"), "WZ": (144, "bfloat16"), "Z16": (144, "bfloat16"), "BOm2": (128, "bfloat16"),
-    "TriS": (128, "bfloat16"), "TriI": (128, "bfloat16"), "Id": (128, "bfloat16"), "NId": (128, "bfloat16"), "EZ": (2048, "bfloat16"),
-    "M16": (256, "bfloat16"), "R16c": (128, "bfloat16"), "Rk": (128, "bfloat16"), "Rs": (128, "bfloat16"), "R64k": (64, "bfloat16"),
-    "Rc": (128, "bfloat16"), "WM": (256, "bfloat16"), "MOFF": (112, "float32"), "PP": (128, "float32"), "S2048": (16, "float32"),
-    "D640": (8, "float32"), "RSW": (256, "bfloat16"), "R1": (128, "bfloat16"), "R2": (128, "bfloat16"), "S128": (256, "float32"),
-    "N112": (112, "float32"), "MB": (112, "bfloat16"), "MT": (112, "int32"), "IT": (128, "bfloat16"), "ITa": (128, "bfloat16"),
-    "O16": (128, "float32"), "tw": (64, "int32"), "tq": (64, "int32"), "tr": (64, "int32"), "tb": (448, "int32"), "tc": (448, "float32"),
-    "tl": (448, "float32"), "tk": (512, "float32"), "KTw": (64, "bfloat16"), "KT": (1024, "bfloat16"),
+    "B144": (144, "bfloat16"), "Z": (144, "bfloat16"), "WZ": (144, "bfloat16"), "Z2": (144, "bfloat16"), "Zn": (144, "bfloat16"),
+    "Z32": (144, "bfloat16"), "Pk": (144, "bfloat16"), "BO4": (128, "bfloat16"), "TriS": (128, "bfloat16"), "TriI": (128, "bfloat16"),
+    "TriI4": (128, "bfloat16"), "Id": (128, "bfloat16"), "NId": (128, "bfloat16"), "EZ": (2048, "bfloat16"),
+    "M16": (272, "bfloat16"), "R16c": (128, "bfloat16"), "Rk": (128, "bfloat16"), "Rs": (128, "bfloat16"), "R64": (256, "bfloat16"),
+    "R16f": (144, "float32"), "R16h": (144, "float32"), "WM": (272, "bfloat16"), "AV": (112, "bfloat16"), "AW": (112, "bfloat16"), "SC": (1, "float32"),
+    "PP": (128, "float32"), "S2": (16, "float32"), "D4n": (8, "float32"), "RSW": (128, "bfloat16"), "R1": (128, "bfloat16"), "R2": (128, "bfloat16"),
+    "N112": (112, "float32"), "MB": (112, "bfloat16"), "MT": (112, "int32"), "IT": (128, "bfloat16"), "IU": (128, "bfloat16"), "ITa": (128, "bfloat16"),
+    "O16": (128, "float32"), "O17": (128, "float32"), "KM": (512, "bfloat16"), "KT": (528, "bfloat16"),
     "vI": (128, "int32"), "u": (128, "int32"), "h": (128, "int32"), "hb": (128, "bfloat16"), "KK": (1024, "float32"),
-    "QI": (1024, "int32"), "OI": (1024, "int32"), "OF": (1024, "uint16"), "G7": (2048, "bfloat16"), "G6": (2048, "bfloat16"),
-    "E": (1024, "bfloat16"), "HS": (1024, "bfloat16"), "K3": (128, "float32"), "q3": (128, "int32"), "c3": (128, "int32"),
-    "dp": (128, "float32"), "cc": (128, "float32"), "DV": (128, "float32"), "D2": (128, "float32"), "c10": (128, "float32"),
-    "h5": (128, "float32"), "TF": (128, "float16"),
-    "NX": (2064, "float32"), "GM": (256, "float16"), "CH": (256, "float16"), "LS": (128, "uint16"),
-    "SA": (128, "float32"), "XS": (2048, "bfloat16"), "dI": (128, "int32"), "dA": (128, "int32"), "D1": (128, "bfloat16"),
-    "CT": (128, "bfloat16"), "CQ": (128, "bfloat16"), "zz": (16, "float32"), "zs": (16, "float32"), "XB": (24, "float32"), "bs": (16, "float32"),
-    "ps": (16, "float32"), "pl": (16, "uint16"), "VAL": (256, "float32"), "SW": (2304, "float32"), "nm": (112, "float32"),
-    "YB": (224, "float32"), "YM": (224, "float32"), "YC": (224, "float32"), "VI": (112, "int32"), "PL": (112, "int32"),
-    "wi": (16, "int32"), "wq": (8, "int32"), "wr": (8, "float32"), "wx": (8, "float32"), "kl": (8, "uint16"),
-    "PR": (112, "float32"), "PM": (112, "float16"), "PC": (112, "float16"), "sl": (8, "uint16"), "P4": (8, "float32"), "nl": (112, "float32"),
-    "aI": (8, "int32"), "U16": (112, "int32"), "H16": (112, "int32"), "K16": (112, "int32"), "Q16": (112, "int32"), "C16": (112, "int32"),
-    "OA": (112, "uint16"), "A4": (448, "bfloat16"), "DA": (1792, "bfloat16"),
-    "k1": (56, "float32"), "k2": (56, "float32"), "k3": (32, "float32"), "k4": (16, "float32"), "kb": (8, "float32"),
-    "bi": (8, "int32"), "bm": (8, "int32"), "b2": (8, "float32"), "b3": (8, "float32"), "b4": (8, "int32"), "b5": (8, "int32"), "nf": (8, "float32"),
-    "cf": (8, "float32"), "OL": (32, "uint16"),
-    "FM": (112, "bfloat16"), "FC": (112, "bfloat16"), "X7": (8, "float32"), "in7": (8, "float32"), "A7": (8, "float32"), "zf": (8, "float32"),
-    "zd": (8, "float32"), "AQ": (8, "float32"), "Ai": (8, "int32"), "lh": (16, "int32"), "lf": (16, "float32"), "hh": (8, "float32"),
-    "SL": (32, "uint16"), "LD": (896, "bfloat16"), "RG": (896, "bfloat16"), "RE": (896, "bfloat16"), "SR": (128, "uint16"),
+    "QI": (1024, "int32"), "OI": (1024, "int32"), "OF": (1024, "uint16"),
+    "E0": (576, "bfloat16"), "H0": (576, "bfloat16"), "E1": (448, "bfloat16"), "H1": (448, "bfloat16"),
+    "K3": (128, "float32"), "q3": (128, "int32"), "c3": (128, "int32"), "dp": (128, "float32"), "cc": (64, "float32"), "DV": (64, "float32"),
+    "D2": (64, "float32"), "c10": (64, "float32"), "TF": (128, "float16"),
+    "NX": (2064, "float32"), "GM": (2048, "float16"), "CH": (2048, "float16"), "LS": (128, "uint16"),
+    "SA": (128, "int32"), "SM": (128, "int32"), "XS": (2064, "bfloat16"), "D1": (128, "bfloat16"),
+    "CT": (128, "bfloat16"), "CQ": (128, "bfloat16"), "TX": (32, "bfloat16"), "FX": (32, "bfloat16"), "zz": (16, "float32"), "Wz": (16, "float32"),
+    "f6": (16, "bfloat16"), "n6": (16, "float32"), "zs": (16, "float16"), "pl": (16, "uint16"), "VAL": (256, "float32"), "SW": (4352, "float32"),
+    "Y": (112, "float32"), "YW": (112, "float32"), "VI": (112, "int32"), "PL": (112, "int32"), "dead": (112, "float32"), "PD": (112, "float32"),
+    "wi": (8, "int32"), "wq": (8, "int32"), "kl": (8, "uint16"), "PR": (112, "float32"), "PW": (112, "float32"), "sl": (8, "uint16"), "P3": (8, "float16"),
+    "aI": (28, "int32"), "U4": (28, "int32"), "H4": (28, "int32"), "K16": (112, "int32"), "Q16": (112, "int32"), "C16": (112, "int32"),
+    "OA": (112, "uint16"), "GA": (448, "bfloat16"), "DA": (1792, "bfloat16"),
+    "k1": (28, "float32"), "k2": (28, "float32"), "k3": (28, "float32"), "k4": (28, "float32"), "k5": (16, "float32"),
+    "bi": (8, "int32"), "bm": (8, "int32"), "b3": (8, "int32"), "b4": (8, "int32"), "b5": (8, "int32"), "OL": (32, "uint16"),
+    "zd": (8, "float32"), "Af": (8, "float32"), "Ai": (8, "int32"), "lo": (8, "int32"), "lf": (8, "float32"),
+    "SL": (32, "uint16"), "LD": (896, "bfloat16"), "LE": (896, "bfloat16"), "RG": (1008, "bfloat16"), "SR": (128, "uint16"),
 }
 HOME = {}
 
@@ -62,15 +61,16 @@ def _pack():
 
 SCRATCH = {k: ("sbuf", [128, c], d) for k, (c, d) in _pack().items()}
 for _i in range(8):
-    SCRATCH["D%d_" % _i] = ("sbuf", [128, 2048], "bfloat16")
-    HOME["D%d_" % _i] = ("D%d_" % _i, 0)
+    for _n in ("D%d_", "R%d_"):
+        SCRATCH[_n % _i] = ("sbuf", [128, 2048], "bfloat16")
+        HOME[_n % _i] = (_n % _i, 0)
     SCRATCH["p%d" % _i] = ("psum", [128, 512], "float32")
     HOME["p%d" % _i] = ("p%d" % _i, 0)
 for _i in range(RO):
-    for _n, _c in (("AS", 112), ("AL", 112), ("FS", 448), ("FL", 448)):
+    for _n, _c in (("AS", NS), ("AL", 4 * NS), ("FS", ND * FB), ("FL", ND * FB)):
         SCRATCH["%s%d" % (_n, _i)] = ("sbuf", [128, _c], "bfloat16")
         HOME["%s%d" % (_n, _i)] = ("%s%d" % (_n, _i), 0)
-SEMAPHORES = ["qV", "qS", "qP", "qG", "dX", "dW", "dT", "dY"] + ["%s%d" % (n, i) for i in range(RO) for n in ("ask", "ans", "la", "lb")]
+SEMAPHORES = ["qV", "qS", "qP", "qG", "dX0", "dX1", "dW", "dT", "dY"] + ["%s%d" % (n, i) for i in range(RO) for n in ("ask", "ans", "la", "lb")]
 
 
 def rank_program(g, core, T, topo):
@@ -93,7 +93,7 @@ def rank_program(g, core, T, topo):
         return (win[0].indirect(off[0]), win[1] + off[1])
 
     def apart(lo, hi, st, lo2, hi2, st2):
-        return lo >= hi2 or lo2 >= hi or (st == st2 and st > 1 and (lo - lo2) % st != 0)
+        return lo >= hi2 or lo2 >= hi or (st > 1 and st2 > 1 and st % min(st, st2) == 0 and st2 % min(st, st2) == 0 and (lo - lo2) % min(st, st2) != 0)
 
     def sync(q, outs, ins):
         need = {}
@@ -164,8 +164,8 @@ def rank_program(g, core, T, topo):
         else:
             do("V", lambda: g.vector.tensor_scalar(out[0], a[0], x1, s2, op0, op1), [out], ins)
 
-    def scan(out, a, b, op0=Op.mult, op1=Op.add):
-        do("V", lambda: g.vector.tensor_tensor_scan(out[0], a[0], b[0], 0.0, op0, op1), [out], [a, b])
+    def scan(out, a, b, op0=Op.mult, op1=Op.add, initial=0.0):
+        do("V", lambda: g.vector.tensor_tensor_scan(out[0], a[0], b[0], initial, op0, op1), [out], [a, b])
 
     def fill(out, c):
         do("V", lambda: g.vector.memset(out[0], c), [out], [])
@@ -190,87 +190,88 @@ def rank_program(g, core, T, topo):
     def EZ(i):
         return A("EZ", 128 * i, 128 * i + 128)
 
+    def half(name, b):
+        return A(name, 1024 * b, 1024 * b + 1024)
+
     BO = A("B144", 0, 128)
     L16 = A("M16", 0, 128, parts=16)
-    WP = A("p7", 384, 384 + NS)
-    TH = A("p7", 256, 256 + NS)
+    Id = A("Id")
 
-    load("Y", "dX", A("X0", 0, W), T.x0[:])
+    for b in range(2):
+        load("Y", "dX%d" % b, half("X0", b), T.x0[:, 1024 * b:1024 * b + 1024])
     load("S", "dW", A("wtb"), T.wt[:])
     load("S", "dT", A("thi"), T.th[:])
-    fill(A("ones", 0, 256), 1.0)
-    fill(A("ones", 256, 2048), 1.0)
-    iota(A("R64k", parts=16), [[0, 64]], 0, 64)
-    iota(A("Rc"), [[1, 128]], 0, 0)
-    sel(A("M16", parts=16), A("ones", 0, 256, parts=16), [[0, 16], [1, 16]], Op.is_equal, 0, -1)
+    fill(A("ones", 0, 272), 1.0)
     sel(A("B144"), A("ones", 0, 144), [[-16, 9], [0, 16]], Op.is_ge, 0, 1)
     sel(A("B144"), A("B144"), [[16, 9], [0, 16]], Op.is_ge, 15, -1)
     sel(A("Z"), A("B144"), [[0, 9], [1, 16]], Op.is_equal, -15, 0)
-    sel(A("Id"), A("ones", 0, 128), [[-1, 128]], Op.is_equal, 0, 1)
+    sel(Id, A("ones", 0, 128), [[-1, 128]], Op.is_equal, 0, 1)
+    sel(A("M16", parts=16), A("ones", 0, 272, parts=16), [[0, 17], [1, 16]], Op.is_equal, 0, -1)
     iota(A("R16c", parts=16), [[16, 128]], 0, 0)
     iota(A("Rk", parts=16), [[0, 128]], 0, 1)
-    iota(A("Rs", parts=16), [[0, 128]], -2 * NS, 1)
-    sel(A("EZ"), A("ones"), [[-1, 16], [-16, 8], [0, 16]], Op.is_equal, 0, 1)
-    sel(A("RSW"), A("ones", 0, 256), [[0, 16], [1, 16]], Op.is_gt, 0, 0)
-    sel(A("R1"), A("ones", 0, 128), [[0, 16], [1, 8]], Op.not_equal, -1, 0)
-    sel(A("TriS"), BO, [[1, 128]], Op.is_gt, 0, -1)
-    sel(A("TriI"), BO, [[1, 128]], Op.is_ge, 0, -1)
-    iota(A("S128"), [[128, 256]], 128, 0)
-    iota(A("N112"), [[1, 112]], 0, 0)
-    iota(A("MB"), [[1, 16], [0, 7]], 0, 0)
-    iota(A("MT"), [[2, 16], [0, 7]], 1, 0)
-    iota(A("ITa"), [[0, 8], [1, 16]], 1, 0)
-    fill(A("X0", W, W + 32), -1.0)
-    fill(A("tk", 0, 64), -8.0)
-    fill(A("E"), 0.0)
-    fill(A("D1"), 0.0)
-    fill(A("XB"), 0.0)
-    fill(A("X7"), 0.0)
-    mm(A("p7", 0, 256), L16, A("M16", parts=16))
-    mm(A("p5", 0, 64), L16, A("R64k", parts=16), True, False)
-    mm(A("p5", 0, 64), L16, A("Rc", 0, 64, parts=16), False, True)
-    cp(A("tw"), A("p5", 0, 64))
-
-    def part(name, k):
-        return A(name, 64 * k, 64 * k + 64)
-
-    ts(A("tq"), A("tw"), 127, Op.bitwise_and)
-    ts(A("tr"), A("tw"), 7, Op.logical_shift_right)
-    for k in range(7):
-        ts(part("tb", k), A("tq"), 6 - k, Op.logical_shift_right, 1, Op.bitwise_and)
-    cp(part("tc", 0), part("tb", 0))
-    for k in range(1, 7):
-        tt(part("tc", k), part("tc", k - 1), part("tb", k), Op.add)
+    fill(A("KM"), 7.0)
+    fill(A("KT", 0, 24), 6.0)
+    for j in range(6):
+        fill(A("KM", 8 << j, 16 << j, 8), 5.0 - j)
+    for j in range(6):
+        n = 8 << j
+        tt(A("KT", 16 + n, 16 + 2 * n), A("KT", 15, 15 + n), A("KM", n, 2 * n), Op.min)
+        if j == 0:
+            fill(A("ones", 272, 2048), 1.0)
+        if j == 1:
+            for name in ("E0", "E1"):
+                fill(A(name), 0.0)
+        if j == 2:
+            for name in ("FS0", "FS1"):
+                fill(A(name), 0.0)
+        if j == 3:
+            for name in ("D1", "TX", "FX"):
+                fill(A(name), 0.0)
+            fill(A("XS", W, W + 16), 512.0)
     ts(A("WZ"), A("Z"), A("wtb"), Op.mult)
     cp(A("t1f"), A("thi", 0, 1))
-    ts(A("t2f"), A("thi", 1, 2), 16.0, Op.mult)
-    for k in range(7):
-        tt(part("tl", k), part("tc", k), A("tr"), Op.is_le)
-    for k in range(7):
-        tt(A("KTw") if k == 6 else part("tk", k + 1), part("tk", k), part("tl", k), Op.add)
+    ts(A("t2f"), A("thi", 1, 2), 32.0, Op.mult)
+    act(A("NId"), Id, scale=-1.0)
+    act(A("Z2"), A("Z"), scale=2.0)
+    act(A("Zn"), A("Z"), scale=-1.0)
+    act(A("Z32"), A("Z"), scale=32.0)
+    act(A("BO4"), BO, scale=1.0 / 1024)
+    mm(A("p3", 0, 272), L16, A("M16", parts=16))
+    mm(A("p4", 0, 128), L16, A("R16c", parts=16), True, False)
+    mm(A("p4", 0, 128), L16, A("Rk", parts=16), False, True)
+    act(A("WM"), A("p3", 0, 272))
+    act(A("PP"), A("p4", 0, 128))
 
-    def constants_1():
-        mm(A("p6", 0, 128), L16, A("R16c", parts=16), True, False)
-        mm(A("p6", 0, 128), L16, A("Rk", parts=16), False, True)
-        act(A("PP"), A("p6", 0, 128))
-        act(A("Z16"), A("Z"), scale=16.0)
-        act(A("BOm2"), BO, scale=-2.0)
+    def constants_G():
+        sel(A("EZ"), A("ones"), [[-1, 16], [-16, 8], [0, 16]], Op.is_equal, 0, 1)
+        sel(A("Pk"), A("ones", 0, 144), [[-16, 9], [-8, 16]], Op.is_equal, 112, 1)
+        sel(A("Pk"), A("Pk"), [[0, 9], [1, 16]], Op.is_ge, -14, 0)
+        sel(A("RSW"), A("ones", 0, 128), [[0, 8], [1, 16]], Op.is_gt, 0, 0)
+        sel(A("R1"), A("ones", 0, 128), [[0, 16], [1, 8]], Op.not_equal, -1, 0)
+        sel(A("TriS"), BO, [[1, 128]], Op.is_gt, 0, -1)
+        sel(A("TriI"), BO, [[1, 128]], Op.is_ge, 0, -1)
+        iota(A("R64", parts=16), [[64, 256]], 0, 0)
+        iota(A("Rs", parts=16), [[0, 128]], -2 * NS, 1)
+        iota(A("N112"), [[1, NS]], 0, 0)
+        iota(A("MB"), [[2, 16], [0, ND]], 0, 0)
+        iota(A("MT"), [[2, 16], [0, ND]], 1, 0)
+        iota(A("ITa"), [[0, 8], [1, 16]], 1, 0)
+        iota(A("R16f"), [[16, 144]], 0, 0)
+
+    def constants_late():
         act(A("R2"), A("R1"), scale=2.0)
-        act(A("MOFF"), A("WM", 0, NS), scale=-1000.0, bias=1000.0)
-        act(A("S2048"), A("PP", 0, 16), bias=2048.0)
-        act(A("D640", 0, 7), A("PP", 0, 7), bias=float(DUMP // 4))
-        act(A("SA", 0, 128, 8), A("PP", 0, 16), scale=8.0)
-
-    def constants_2():
-        cp(WP, A("WM", 0, NS))
+        act(A("TriI4"), A("TriI"), scale=1.0 / 1024)
+        act(A("S2"), A("PP", 0, 16), scale=2.0, bias=2048.0)
+        act(A("D4n", 0, ND), A("PP", 0, ND), scale=4.0, bias=float(DUMP))
+        act(A("R16h"), A("R16f"), bias=-0.5)
+        ts(A("SM", 0, 16), A("PP", 0, 16), 8.0, Op.mult)
+        ts(A("AV"), A("WM", 15, 15 + NS), BIG, Op.mult, 1.0, Op.max)
+        ts(A("SC"), A("WM", 15, 16), 1.0, Op.mult, 1.0 / BIG, Op.max)
         tt(A("O16"), A("ITa"), BO, Op.mult)
+        ts(A("O17"), BO, -100.0, Op.mult, 99.0, Op.add)
+        tt(A("AW"), A("AV"), A("WM", 0, NS), Op.subtract)
         ts(A("IT"), A("O16"), 1.0, Op.subtract)
-
-    def table():
-        for i in range(16):
-            mm(A("p%d" % (4 + i // 8), 64 * (i % 8), 64 * (i % 8) + 64), EZ(i), A("KTw"))
-        for b in range(2):
-            act(A("KT", 512 * b, 512 * b + 512), A("p%d" % (4 + b)))
+        tt(A("IU"), A("O16"), A("O17"), Op.add)
 
     def exchange(src, dst, w, ls, rs, back):
         sync("G", [], A(src)[1])
@@ -284,286 +285,380 @@ def rank_program(g, core, T, topo):
             tr.append(RemoteDMATransfer(dst_ids=[DstId(rid=rid, pnc=pid)], dma_engine_mask=mask, remote_sem=T.sem[rs],
                                         src=A(src, w * (d - 1), w * d)[0], dst=A(dst, w * (d - 1), w * d)[0]))
         g.remote_dma_fused(tr, local_sem=T.sem[ls])
-        event(rs, ENG * ND, [A(dst)], [], {})
+        event(rs, ENG * ND, [A(dst, 0, w * ND)], [], {})
+
+    def successors(rnd):
+        X = "X%d" % rnd
+        win = A(X, 0, W)
+
+        def hw(name, b):
+            return A(name, 64 * b, 64 * b + 64)
+
+        def lk(name, b, m0, m1=None):
+            return A(name, 512 * b + 64 * m0, 512 * b + 64 * (m0 + 1 if m1 is None else m1))
+
+        def temp(k):
+            return A("p7", 128 + 64 * k, 192 + 64 * k)
+
+        def pd(m, b, lo=0, hi=64):
+            bank, o = ("p1", 64 * m) if b == 0 else ("p2", 64 * m) if m > 1 else ("p0", 128) if m else ("p1", 0)
+            return A(bank, o + lo, o + hi)
+
+        def split(b):
+            ts(hw("u", b), hw("vI", b), 2047, Op.bitwise_and)
+            ts(hw("h", b), hw("vI", b), 5, Op.logical_shift_right, 63, Op.bitwise_and)
+
+        def plus(b, ms):
+            for m in ms:
+                act(lk("KK", b, m), hw("hb", b), bias=float(2 * m + 1))
+
+        def times(b, ms):
+            for m in ms:
+                tt(lk("QI", b, m), lk("KK", b, m), hw("p7", b), Op.mult)
+
+        def mod(b, m0, m1):
+            ts(lk("OI", b, m0, m1), lk("QI", b, m0, m1), 2047, Op.bitwise_and)
+
+        def offsets(b, m0, m1):
+            cp(lk("OF", b, m0, m1), lk("OI", b, m0, m1))
+
+        def part(name, m, b, lo, hi, first=0, st=1):
+            return A(name % m, 1024 * b + 16 * lo + first, 1024 * b + 16 * hi, st)
+
+        def sums(m, b, sides, lo=0, hi=64):
+            for n, (z, name) in enumerate(sides):
+                for i in range(16):
+                    mm(pd(m, b, lo, hi), Z(z, i), part(name, m, b, lo, hi, i, 16), n == 0 and i == 0, n == len(sides) - 1 and i == 15)
+
+        def gather(m, b, lo=0, hi=64):
+            o = 512 * b + 64 * m
+            tt(part("D%d_", m, b, lo, hi), I(win, A("OF", o + lo, o + hi)), A("XC", 1024 * b + 16 * lo, 1024 * b + 16 * hi), Op.subtract)
+
+        def relu(m, b):
+            ts(part("R%d_", m, b, 0, 64), part("D%d_", m, b, 0, 64), 0.0, Op.max)
+            sums(m, b, (("Zn", "D%d_"), ("Z2", "R%d_")))
+
+        def size(m, b, lo=0, hi=64):
+            act(part("R%d_", m, b, lo, hi), part("D%d_", m, b, lo, hi), AF.Abs)
+            sums(m, b, (("Z", "R%d_"),), lo, hi)
+
+        turn = [0]
+
+        def take(m, b):
+            act(half("D%d_" % m, b), I(win, lk("OF", b, m)))
+            turn[0] = 1 - turn[0]
+            for x in range(2):
+                o, c = A("p%d" % (3 + 2 * turn[0] + x)), 1024 * b + 512 * x
+                mm(o, A("NId"), A(X, c, c + 512), True, False)
+                mm(o, Id, A("D%d_" % m, c, c + 512), False, True)
+            return (m, b, 3 + 2 * turn[0])
+
+        def finish(t):
+            m, b, bank = t
+            for x in range(2):
+                act(part("R%d_", m, b, 32 * x, 32 * x + 32), A("p%d" % (bank + x)), AF.Abs)
+            sums(m, b, (("Z", "R%d_"),))
+
+        def far(b, ms):
+            n = 9 - 2 * b
+            for m in ms:
+                ts(A("E%d" % b, 8 - m, 64 * n, n), pd(m, b), A("t1f"), Op.is_ge)
+
+        def first_near(b):
+            n, m0 = 9 - 2 * b, 2 * b
+            M = A("H%d" % b, n - 1, 64 * n, n)
+            K, q, c, dp = (hw(x, b) for x in ("K3", "q3", "c3", "dp"))
+            return [lambda: scan(A("H%d" % b), A("E%d" % b), A("E%d" % b)),
+                    lambda: (ts(temp(0), M, 2.0, Op.mult, 2.0 * m0 + 1, Op.add), ts(temp(1), M, float(n - 1), Op.is_ge)),
+                    lambda: tt(K, temp(0), hw("hb", b), Op.add),
+                    lambda: tt(q, K, hw("p7", b), Op.mult),
+                    lambda: ts(c, q, 2047, Op.bitwise_and),
+                    lambda: tt(dp, hw("PP", b), c, Op.subtract),
+                    lambda: tt(temp(0), temp(1), dp, Op.mult)]
+
+        def spread(b, banks):
+            for i in range(16):
+                mm(A(banks[i // 8], 64 * (i % 8), 64 * (i % 8) + 64), EZ(i), hw("TF", b))
+
+        def table(b, banks, i):
+            return A("NX", 1024 * b + i, 1024 * b + 1024, 16), A(banks[i // 8], 64 * (i % 8), 64 * (i % 8) + 64)
+
+        TAG[0] = "head"
+        for b in range(2):
+            for i in range(16):
+                mm(hw("p0", b), Z("WZ", i), A(X, 1024 * b + i, 1024 * b + 1024, 16), i == 0, i == 15)
+            if b == 0:
+                act(half("XC", 0), half(X, 0))
+                cp(hw("vI", 0), hw("p0", 0))
+        sel(half("XC", 1), half(X, 1), [[0, 1024]], Op.is_ge, 0, 0)
+        if rnd == 0:
+            constants_G()
+        split(0)
+        ts(lk("KK", 0, 7), hw("h", 0), 15.0, Op.add)
+        cp(hw("p7", 0), hw("u", 0))
+        cp(hw("hb", 0), hw("h", 0))
+        for m in (6, 5, 4):
+            ts(lk("KK", 0, m), hw("h", 0), 2.0 * m + 1, Op.add)
+        plus(0, (3, 2, 1, 0))
+        times(0, (7, 6, 5, 4))
+        mod(0, 7, 8)
+        mod(0, 4, 7)
+        offsets(0, 7, 8)
+        offsets(0, 4, 7)
+        cp(hw("vI", 1), hw("p0", 1))
+        TAG[0] = "dist0"
+        t7 = take(7, 0)
+        gather(6, 0)
+        times(0, (3, 2, 1, 0))
+        split(1)
+        t5 = take(5, 0)
+        gather(4, 0)
+        mod(0, 0, 4)
+        cp(hw("hb", 1), hw("h", 1))
+        cp(hw("p7", 1), hw("u", 1))
+        offsets(0, 0, 4)
+        relu(6, 0)
+        finish(t7)
+        plus(1, range(7, -1, -1))
+        t3 = take(3, 0)
+        gather(2, 0)
+        times(1, range(7, -1, -1))
+        relu(4, 0)
+        finish(t5)
+        mod(1, 0, 8)
+        t1 = take(1, 0)
+        gather(0, 0)
+        offsets(1, 0, 8)
+        relu(2, 0)
+        finish(t3)
+        relu(0, 0)
+        TAG[0] = "dist1"
+        t7 = take(7, 1)
+        gather(6, 1)
+        finish(t1)
+        t5 = take(5, 1)
+        gather(4, 1)
+        far(0, range(7, -1, -1))
+        steps = first_near(0)
+        relu(6, 1)
+        finish(t7)
+        steps[0]()
+        relu(4, 1)
+        for s in steps[1:4]:
+            s()
+        t3 = take(3, 1)
+        gather(2, 1, 0, 32)
+        steps[4]()
+        gather(2, 1, 32, 64)
+        steps[5]()
+        finish(t5)
+        fill(A("SW", 0, NS), 0.0)
+        tt(A("c10"), lk("OI", 1, 1), lk("OI", 1, 0), Op.subtract)
+        steps[6]()
+        relu(2, 1)
+        tt(hw("TF", 0), temp(0), hw("c3", 0), Op.add)
+        finish(t3)
+        spread(0, ("p0", "p1"))
+        TAG[0] = "last"
+        gather(1, 1, 0, 32)
+        gather(1, 1, 32, 64)
+        for i in range(16):
+            act(*table(0, ("p0", "p1"), i))
+        far(1, range(7, 1, -1))
+        steps = first_near(1)
+        size(1, 1)
+        steps[0]()
+        gather(0, 1, 0, 32)
+        steps[1]()
+        steps[2]()
+        gather(0, 1, 32, 64)
+        size(0, 1, 0, 32)
+        size(0, 1, 32, 64)
+        for s in steps[3:6]:
+            s()
+        tt(A("cc"), hw("c3", 1), lk("OI", 1, 1), Op.subtract)
+        steps[6]()
+        ts(temp(2), pd(1, 1), A("t1f"), Op.is_ge)
+        tt(A("D2"), temp(0), A("cc"), Op.add)
+        tt(temp(3), temp(2), A("D2"), Op.mult)
+        tt(A("DV"), temp(3), A("c10"), Op.add)
+        ts(temp(4), pd(0, 1), A("t1f"), Op.is_ge)
+        tt(temp(5), temp(4), A("DV"), Op.mult)
+        tt(hw("TF", 1), temp(5), lk("OI", 1, 0), Op.add)
+        TAG[0] = "table"
+        act(A("NX", W, W + 1), A("NX", 0, 1))
+        act(A(X, W, W + F), A(X, 0, F))
+        for t in range(8):
+            mm(A("p2", 0, 16), A("Pk", 14 - 2 * t, 142 - 2 * t), A("TF", t, 128, 8), t == 0, t == 7)
+        spread(1, ("p3", "p4"))
+        ts(A("LS", 16, 32), A("p2", 0, 16), 1.0, Op.add)
+        ts(A("SA", 16, 32), A("p2", 0, 16), 1.0, Op.add)
+        tt(A("D1", 1, 128, 8), A("p2", 0, 16), A("SM", 0, 16), Op.not_equal)
+        for i in range(8):
+            cp(*table(1, ("p3", "p4"), i))
+            act(*table(1, ("p3", "p4"), 8 + i))
 
     def one_round(rnd):
         X, XN = "X%d" % rnd, "X%d" % (rnd + 1)
         AL, AS, FL, FS = ("%s%d" % (n, rnd) for n in ("AL", "AS", "FL", "FS"))
-        win = A(X, 0, W + 32)
-        first = 7 - SL // 2
-
-        def half(name, b):
-            return A(name, 1024 * b, 1024 * b + 1024)
-
-        for i in range(16):
-            mm(A("p0", 0, 128), Z("WZ", i), A(X, i, W, 16), i == 0, i == 15)
+        win = A(X, 0, W + F)
         if rnd == 0:
-            act(A("WM"), A("p7", 0, 256))
-            act(A("NId"), A("Id"), scale=-1.0)
-        for b in range(2):
-            act(half("XC", b), half(X, b))
-        cp(A("vI"), A("p0", 0, 128))
-        ts(A("u"), A("vI"), 2047, Op.bitwise_and)
-        ts(A("h"), A("u"), 5, Op.logical_shift_right)
-        cp(A("hb"), A("h"))
-        cp(A("p7", 0, 128), A("u"))
+            ts(A("SM", 0, 16), A("PP", 0, 16), 8.0, Op.mult)
+        successors(rnd)
 
-        def plus(m):
-            act(A("KK", 128 * m, 128 * m + 128), A("hb"), bias=float(2 * m + 1))
+        TAG[0] = "runs"
 
-        def look(m):
-            return A("OI", 128 * m, 128 * m + 128)
-
-        def prep(m0, m1):
-            for m in range(m0, m1):
-                tt(A("QI", 128 * m, 128 * m + 128), A("KK", 128 * m, 128 * m + 128), A("p7", 0, 128), Op.mult)
-            ts(A("OI", 128 * m0, 128 * m1), A("QI", 128 * m0, 128 * m1), 2047, Op.bitwise_and)
-            cp(A("OF", 128 * m0, 128 * m1), A("OI", 128 * m0, 128 * m1))
-
-        def offs(m, b):
-            return A("OF", 128 * m + 64 * b, 128 * m + 64 * b + 64)
-
-        def pd(m, b=None):
-            bank, o = (("p0", 0), ("p6", 0), ("p1", 0), ("p1", 1))[m] if m < 4 else ("p2", m - 4)
-            return A(bank, 128 * o, 128 * o + 128) if b is None else A(bank, 128 * o + 64 * b, 128 * o + 64 * b + 64)
-
-        def gather(m, b):
-            tt(half("D%d_" % m, b), I(win, offs(m, b)), half("XC", b), Op.subtract)
-
-        def absum(m, b):
-            d = half("D%d_" % m, b)
-            act(d, d, AF.Abs)
-            sums(m, b)
-
-        def sums(m, b):
-            for i in range(16):
-                mm(pd(m, b), Z("Z", i), A("D%d_" % m, 1024 * b + i, 1024 * b + 1024, 16), i == 0, i == 15)
-
-        def near(m):
-            ts(A("E", 8 - m, 1024, 8), pd(m), A("t1f"), Op.is_ge)
-
-        order = [(m, b) for m in range(7, -1, -1) for b in range(2)]
-        theirs = order[SL:]
-
-        def own(m):
-            bs = [b for b in range(2) if (m, b) in order[:SL]]
-            for b in bs:
-                act(half("G%d" % m, b), I(win, offs(m, b)))
-                if (m, b) == (7, 0):
-                    for x in range(first - 1, -1, -1):
-                        plus(x)
-            for b in bs:
-                for x in (2 * b, 2 * b + 1):
-                    mm(A("p%d" % (3 + x)), A("NId"), A(X, 512 * x, 512 * x + 512), True, False)
-                    mm(A("p%d" % (3 + x)), A("Id"), A("G%d" % m, 512 * x, 512 * x + 512), False, True)
-            for b in bs:
-                for x in (2 * b, 2 * b + 1):
-                    act(A("D%d_" % m, 512 * x, 512 * x + 512), A("p%d" % (3 + x)), AF.Abs)
-                sums(m, b)
-
-        for m in range(7, first - 1, -1):
-            plus(m)
-        prep(7, 8)
-        own(7)
-        prep(first, 7)
-        for n, (m, b) in enumerate(theirs):
-            gather(m, b)
-            if n == 0:
-                if rnd == 0:
-                    constants_1()
-                own(6)
-                act(A("h5"), A("hb"), bias=5.0)
-            if n == 1 - SL % 2:
-                prep(0, first)
-            if n:
-                absum(*theirs[n - 1])
-            if (m, b) == (3, 0) and rnd == 0:
-                table()
-            if (m, b) == (2, 1):
-                if rnd == 0:
-                    constants_2()
-                for x in range(7, 3, -1):
-                    near(x)
-                fill(A("SW", 0, NS), 0.0)
-        absum(*theirs[-1])
-
-        tt(A("c10"), look(1), look(0), Op.subtract)
-        near(3)
-        near(2)
-        scan(A("HS"), A("E"), A("E"))
-        M = A("HS", 6, 1024, 8)
-        T1, T2 = A("p7", 128, 256), A("p7", 256, 384)
-        ts(T1, M, 2.0, Op.mult)
-        ts(T2, M, 6.0, Op.is_ge)
-        tt(A("K3"), T1, A("h5"), Op.add)
-        tt(A("q3"), A("K3"), A("p7", 0, 128), Op.mult)
-        ts(A("c3"), A("q3"), 2047, Op.bitwise_and)
-        tt(A("dp"), A("PP"), A("c3"), Op.subtract)
-        tt(A("cc"), A("c3"), look(1), Op.subtract)
-        tt(T1, T2, A("dp"), Op.mult)
-        tt(A("D2"), T1, A("cc"), Op.add)
-        ts(A("p2", 256, 384), pd(1), A("t1f"), Op.is_ge)
-        tt(A("p2", 384, 512), A("p2", 256, 384), A("D2"), Op.mult)
-        tt(A("DV"), A("p2", 384, 512), A("c10"), Op.add)
-        places = ((("p3", 0, 8, "V"), ("p4", 8, 16, "S")), (("p5", 0, 7, "S"), ("p6", 7, 13, "V"), ("p1", 13, 16, "S")))
-        for b in range(2):
-            lo, hi = 64 * b, 64 * b + 64
-            e, d = A("p2", lo, hi), A("p2", 128 + lo, 128 + hi)
-            ts(e, pd(0, b), A("t1f"), Op.is_ge)
-            tt(d, e, A("DV", lo, hi), Op.mult)
-            tt(A("TF", lo, hi), d, A("OI", lo, hi), Op.add)
-            for p, i0, i1, q in places[b]:
-                for i in range(i0, i1):
-                    mm(A(p, 64 * (i - i0), 64 * (i - i0) + 64), EZ(i), A("TF", lo, hi))
-        for b in range(2):
-            for p, i0, i1, q in places[b]:
-                for i in range(i0, i1):
-                    o, n = A("NX", i + 1024 * b, 1024 * b + 1024, 16), A(p, 64 * (i - i0), 64 * (i - i0) + 64)
-                    if q == "V":
-                        ts(o, n, 1.0, Op.add)
-                    else:
-                        act(o, n, bias=1.0)
-        cp(A("NX", W, W + 1), A("NX", 0, 1))
-        cp(A(X, W, W + 4), A(X, 0, 4))
+        def step(name, k):
+            return A(name, 16 * k, 16 * k + 16)
 
         act(A("XS", 0, W, 8), A(X, 0, W, 8))
-        for k in range(1, 8):
-            if k == 1:
-                tt(A("GM"), A("NX", 0, W, 8), A("WM"), Op.mult)
-            else:
-                tt(A("GM"), I(A("NX", 0, W + 1), A("LS", 16 * k - 16, 16 * k)), A("WM"), Op.mult)
-            scan(A("CH"), A("RSW"), A("GM"))
-            cp(A("LS", 16 * k, 16 * k + 16), A("CH", 15, 256, 16))
-            cp(A("SA", k, 128, 8), A("CH", 15, 256, 16))
-            act(A("XS", k, W, 8), I(win, A("LS", 16 * k, 16 * k + 16)))
+        act(A("XS", 1, W, 8), I(win, step("LS", 1)))
+        for k in range(2, 8):
+            o = 256 * k
+            C = A("CH", o + 15, o + 256, 16)
+            for b in range(2):
+                tt(A("GM", o + 128 * b, o + 128 * b + 128), I(A("NX", 0, W + 1), A("LS", 16 * k - 16 + 8 * b, 16 * k - 8 + 8 * b)), A("WM", 0, 128), Op.mult)
+            ts(step("SM", k - 1), step("SA", k - 1), 2047, Op.bitwise_and)
+            for b in range(2):
+                scan(A("CH", o + 128 * b, o + 128 * b + 128), A("RSW"), A("GM", o + 128 * b, o + 128 * b + 128))
+            if k == 7:
+                break
+            for b in range(2):
+                ts(A("LS", 16 * k + 8 * b, 16 * k + 8 * b + 8), A("CH", o + 128 * b + 15, o + 128 * b + 128, 16), 1.0, Op.add)
+            tt(A("D1", k, 128, 8), C, step("SM", k - 1), Op.not_equal)
+            ts(step("SA", k), C, 1.0, Op.add)
+            act(A("XS", k, W, 8), I(win, step("LS", k)))
+            if k == 2 and rnd == 0:
+                constants_late()
+            if k == 6:
+                TW = A("CT", 6, 128, 8)
+                scan(A("CQ"), A("R2"), A("D1"))
+                scan(A("CT"), A("R1"), A("D1"))
+                mm(A("p0", 0, 256), A("ones", 0, 128, parts=1), A("R64", parts=1), True, False)
+                for i in range(16):
+                    mm(A("p0", i, 256, 16), EZ(i), A("CQ", 6, 128, 8), False, i == 15)
+                act(A("VAL"), A("p0", 0, 256), scale=8.0)
+                ts(A("zz"), TW, 0.0, Op.is_equal)
+                scan(A("TX", 1, 17), A("ones", 0, 16), TW)
+                tt(A("Wz"), A("zz"), A("S2"), Op.mult)
+                mm(A("p1", 0, 17), BO, A("TX", 0, 17), True, False)
+                mm(A("p1", 0, 16), A("TriS"), TW, False, False)
 
-        tt(A("dI", 0, 127), A("SA", 1, 128), A("SA", 0, 127), Op.subtract)
-        ts(A("dA", 0, 127), A("dI", 0, 127), 2047, Op.bitwise_and)
-        ts(A("D1", 1, 128), A("dA", 0, 127), 1.0, Op.not_equal)
-        scan(A("CT"), A("R1"), A("D1"))
-        TW = A("CT", 7, 128, 8)
-        mm(A("p7", 16, 32), BO, TW)
-        mm(A("p7", 0, 16), A("TriS"), TW)
-        scan(A("CQ"), A("R2"), A("D1"))
-        for i in range(16):
-            mm(A("p0", i, 256, 16), EZ(i), A("CQ", 7, 128, 8))
-        ts(A("zz"), TW, 0.0, Op.is_equal)
-        tt(A("zs"), A("zz"), A("S2048"), Op.mult)
-        scan(A("XB", 1, 17), A("ones", 0, 16), A("p7", 16, 32))
-        tt(A("bs"), A("p7", 0, 16), A("XB", 0, 16), Op.add)
-        tt(A("ps"), A("bs"), A("zs"), Op.max)
-        cp(A("pl"), A("ps"))
-        tt(A("VAL"), A("p0", 0, 256), A("S128"), Op.add)
+        TAG[0] = "sites"
+        tt(A("f6"), C, step("SM", 6), Op.not_equal)
+        tt(A("n6"), C, step("SM", 6), Op.is_equal)
+        ts(step("LS", 7), C, 1.0, Op.add)
+        act(A("XS", 7, W, 8), I(win, step("LS", 7)))
+        scan(A("FX", 1, 17), A("ones", 0, 16), A("f6"))
+        tt(A("zs"), A("n6"), A("Wz"), Op.mult)
+        mm(A("p1", 0, 16), A("TriS"), A("f6"), False, False)
+        mm(A("p1", 0, 17), BO, A("FX", 0, 17), False, False)
+        mm(A("p1", 0, 16), Id, A("zs"), False, True)
+        cp(A("pl"), A("p1", 0, 16))
+        ts(A("dead"), A("N112"), A("p1", 16, 17), Op.is_ge, 4096.0, Op.mult)
         cp(I(A("SW"), A("pl")), A("VAL"))
-        scan(A("YB", 0, NS), A("SW", 0, NS), A("SW", 0, NS), Op.max, Op.max)
-        ts(A("nm"), A("SW", 0, NS), 0.0, Op.is_equal)
-        scan(A("YB", NS, 2 * NS), A("nm"), A("nm"))
-        tt(A("YM", 0, NS), A("YB", 0, NS), WP, Op.mult)
-        tt(A("YM", NS, 2 * NS), A("YB", NS, 2 * NS), WP, Op.mult)
-        scan(A("YC"), A("RSW", 0, 2 * NS), A("YM"))
-        cp(A("wi", 0, 7), A("YC", 15, NS, 16))
-        ts(A("wr", 0, 7), A("YC", NS + 15, 2 * NS, 16), 7.0, Op.min, 128.0, Op.mult)
-        ts(A("wq", 0, 7), A("wi", 0, 7), 127, Op.bitwise_and)
-        tt(A("wx", 0, 7), A("wr", 0, 7), A("wq", 0, 7), Op.add)
-        cp(A("kl", 0, 7), A("wx", 0, 7))
-        cp(A("VI"), A("YB", 0, NS))
-        ts(A("PL"), A("VI"), 4, Op.logical_shift_right, 65528, Op.bitwise_and)
-        tt(A("PR"), I(A("KT"), A("kl", 0, 7)), A("PL"), Op.add)
-        tt(A("PM"), A("PR"), WP, Op.mult)
-        scan(A("PC"), A("RSW", 0, NS), A("PM"))
-        cp(A("sl", 0, 7), A("PC", 15, NS, 16))
-        cp(A(AS), I(A("XS"), A("sl", 0, 7)))
+        scan(A("Y"), A("ones", 0, NS), A("SW", 0, NS), Op.add, Op.max, -1.0)
+        scan(A("YW"), A("AW"), A("Y"))
+        cp(A("VI"), A("Y"))
+        ts(A("wi", 0, ND), A("YW", 15, NS, 16), A("SC"), Op.mult)
+        ts(A("PL"), A("VI"), 6, Op.logical_shift_right, 65528, Op.bitwise_and)
+        ts(A("wq", 0, ND), A("wi", 0, ND), 511, Op.bitwise_and)
+        tt(A("PD"), A("PL"), A("dead"), Op.add)
+        cp(A("kl", 0, ND), A("wq", 0, ND))
+        tt(A("PR"), I(A("KT", 16, 528), A("kl", 0, ND)), A("PD"), Op.add)
+        scan(A("PW"), A("AW"), A("PR"))
+        ts(A("sl", 0, ND), A("PW", 15, NS, 16), A("SC"), Op.mult, float(NONE), Op.min)
+        cp(A(AS), I(A("XS"), A("sl", 0, ND)))
         exchange(AS, AL, 16, "la%d" % rnd, "ask%d" % rnd, False)
-        ts(A("P4", 0, 7), A("PC", 15, NS, 16), 3.0, Op.subtract, 0.25, Op.mult)
-        ts(A("nl"), A("N112"), A("XB", 16, 17), Op.is_ge, 1000.0, Op.mult)
-        tt(TH, A("nl"), A("MOFF"), Op.max)
+        ts(A("P3", 0, ND), A("sl", 0, ND), 3.0, Op.subtract)
 
+        TAG[0] = "answers"
+        keys = (("p1", 0, 8), ("p2", 8, 12), ("p4", 12, 16))
+        for p, m0, m1 in keys:
+            mm(A(p, 0, ND * (m1 - m0)), Id, A("MB", ND * m0, ND * m1), True, False)
+        for b in range(1, 4):
+            cp(A(AL, NS * b, NS * b + NS), A(AL, 0, NS))
         for i in range(16):
-            mm(A("p0", 0, 7), Z("WZ", i), A(AL, i, NS, 16), i == 0, i == 15)
-        for b in range(4):
-            act(A("A4", NS * b, NS * b + NS), A(AL))
-        cp(A("aI", 0, 7), A("p0", 0, 7))
-        ts(A("U16", 0, 7), A("aI", 0, 7), 2047, Op.bitwise_and)
-        for n in (7, 14, 28, 56):
-            cp(A("U16", n, 2 * n), A("U16", 0, n))
-        ts(A("H16"), A("U16"), 5, Op.logical_shift_right)
-        tt(A("K16"), A("H16"), A("MT"), Op.add)
-        tt(A("Q16"), A("K16"), A("U16"), Op.mult)
+            mm(A("p0", 0, 28), Z("WZ", i), A(AL, i, 4 * NS, 16), i == 0, i == 15)
+        mm(A("p3", 0, 448), A("NId"), A(AL), True, False)
+        cp(A("aI"), A("p0", 0, 28))
+        ts(A("H4"), A("aI"), 5, Op.logical_shift_right, 63, Op.bitwise_and)
+        ts(A("U4"), A("aI"), 2047, Op.bitwise_and)
+        for a in range(4):
+            tt(A("K16", 28 * a, 28 * a + 28), A("H4"), A("MT", 28 * a, 28 * a + 28), Op.add)
+        for a in range(4):
+            tt(A("Q16", 28 * a, 28 * a + 28), A("K16", 28 * a, 28 * a + 28), A("U4"), Op.mult)
         ts(A("C16"), A("Q16"), 2047, Op.bitwise_and)
         cp(A("OA"), A("C16"))
 
         def quarter(b):
             return A("DA", 448 * b, 448 * b + 448)
 
-        act(A("G7", 0, 448), I(win, A("OA", 0, 28)))
-        mm(A("p3", 0, 448), A("NId"), A("A4"), True, False)
-        mm(A("p3", 0, 448), A("Id"), A("G7", 0, 448), False, True)
+        def key(n):
+            p, m0, m1 = keys[n]
+            for i in range(16):
+                mm(A(p, 0, ND * (m1 - m0)), Z("Z32", i), A("DA", NS * m0 + i, NS * m1, 16), False, i == 15)
+
+        act(A("GA"), I(win, A("OA", 0, 28)))
+        mm(A("p3", 0, 448), Id, A("GA"), False, True)
         for b in range(1, 4):
-            tt(quarter(b), I(win, A("OA", 28 * b, 28 * b + 28)), A("A4"), Op.subtract)
+            tt(quarter(b), I(win, A("OA", 28 * b, 28 * b + 28)), A(AL), Op.subtract)
             act(quarter(b), quarter(b), AF.Abs)
             if b == 1:
                 act(quarter(0), A("p3", 0, 448), AF.Abs)
-        for b in range(2):
-            o = A("p%d" % (1 + b), 0, 56)
-            mm(o, A("Id"), A("MB", 56 * b, 56 * b + 56), True, False)
-            for i in range(16):
-                mm(o, Z("Z16", i), A("DA", 896 * b + i, 896 * b + 896, 16), False, i == 15)
-        cp(A("k1"), A("p1", 0, 56))
-        tt(A("k2"), A("p2", 0, 56), A("k1"), Op.min)
-        tt(A("k3", 0, 28), A("k2", 0, 28), A("k2", 28, 56), Op.min)
-        tt(A("k4", 0, 14), A("k3", 0, 14), A("k3", 14, 28), Op.min)
-        tt(A("kb", 0, 7), A("k4", 0, 7), A("k4", 7, 14), Op.min)
-        cp(A("bi", 0, 7), A("kb", 0, 7))
-        ts(A("nf", 0, 7), A("kb", 0, 7), A("t2f"), Op.is_ge, float(NONE - 1), Op.mult)
-        ts(A("bm", 0, 7), A("bi", 0, 7), 15, Op.bitwise_and)
-        ts(A("b2", 0, 7), A("bm", 0, 7), 2.0, Op.mult, 1.0, Op.add)
-        tt(A("b3", 0, 7), A("b2", 0, 7), A("H16", 0, 7), Op.add)
-        tt(A("b4", 0, 7), A("b3", 0, 7), A("U16", 0, 7), Op.mult)
-        ts(A("b5", 0, 7), A("b4", 0, 7), 2047, Op.bitwise_and)
-        tt(A("cf", 0, 7), A("b5", 0, 7), A("nf", 0, 7), Op.max)
+            key(b - 1)
+        cp(A("k1"), A("p1", 0, 28))
+        tt(A("k2"), A("p1", 28, 56), A("k1"), Op.min)
+        tt(A("k3"), A("p2", 0, 28), A("k2"), Op.min)
+        tt(A("k4"), A("p4", 0, 28), A("k3"), Op.min)
+        tt(A("k5", 0, 14), A("k4", 0, 14), A("k4", 14, 28), Op.min)
+        tt(A("bi", 0, ND), A("k5", 0, ND), A("k5", ND, 14), Op.min)
+        ts(A("bm", 0, ND), A("bi", 0, ND), 31, Op.bitwise_and)
+        ts(A(FS, F, ND * FB, FB), A("bi", 0, ND), A("t2f"), Op.is_lt, 4096.0, Op.mult)
+        tt(A("b3", 0, ND), A("bm", 0, ND), A("K16", 0, ND), Op.add)
+        tt(A("b4", 0, ND), A("b3", 0, ND), A("U4", 0, ND), Op.mult)
+        ts(A("b5", 0, ND), A("b4", 0, ND), 2047, Op.bitwise_and)
         for f in (2, 3, 0, 1):
-            ts(A("OL", 8 * f, 8 * f + 7), A("cf", 0, 7), float(1 + f), Op.add)
+            ts(A("OL", 8 * f, 8 * f + ND), A("b5", 0, ND), float(1 + f), Op.add)
             if f > 1:
-                act(A(FS, f, 448, F), I(win, A("OL", 8 * f, 8 * f + 7)))
+                act(A(FS, f, ND * FB, F + 1), I(win, A("OL", 8 * f, 8 * f + ND)))
         for f in (0, 1):
-            cp(A(FS, f, 448, F), I(win, A("OL", 8 * f, 8 * f + 7)))
-        exchange(FS, FL, 64, "lb%d" % rnd, "ans%d" % rnd, True)
+            cp(A(FS, f, ND * FB, F + 1), I(win, A("OL", 8 * f, 8 * f + ND)))
+        exchange(FS, FL, FB, "lb%d" % rnd, "ans%d" % rnd, True)
 
-        CN = A("p4", 0, 128)
-        mm(CN, L16, A("R16c", parts=16), True, False)
-        mm(CN, L16, A("Rs", parts=16), False, False)
-        tt(A("FM"), A(FL, 0, 448, F), TH, Op.is_ge)
-        scan(A("FC"), A("RSW", 0, NS), A("FM"))
-        FW = A("FC", 15, NS, 16)
-        mm(A("p7", 8, 15), BO, FW)
-        mm(A("p7", 0, 7), A("TriI"), FW)
-        ts(A("zf", 0, 7), FW, 0.0, Op.is_equal)
-        tt(A("zd", 0, 7), A("zf", 0, 7), A("D640", 0, 7), Op.mult)
-        scan(A("X7", 1, 8), A("ones", 0, 7), A("p7", 8, 15))
-        tt(A("in7", 0, 7), A("p7", 0, 7), A("X7", 0, 7), Op.add)
-        tt(A("A7", 0, 7), A("in7", 0, 7), A("P4", 0, 7), Op.add)
-        tt(A("AQ", 0, 7), A("A7", 0, 7), A("zd", 0, 7), Op.max)
-        ts(A("Ai", 0, 7), A("AQ", 0, 7), 4.0, Op.mult)
-        ts(A("lh", 7, 14), A("Ai", 0, 7), 4, Op.logical_shift_right)
-        ts(A("lh", 0, 7), A("Ai", 0, 7), 15, Op.bitwise_and)
-        cp(A("lf", 0, 14), A("lh", 0, 14))
-        ts(A("hh", 0, 7), A("lf", 7, 14), -1.0, Op.mult, -0.5, Op.add)
+        TAG[0] = "next"
+        CN = [A("p5", 0, 64), A("p6", 0, 64)]
+        for b in range(2):
+            mm(CN[b], L16, A("R16c", 64 * b, 64 * b + 64, parts=16), True, False)
+            mm(CN[b], L16, A("Rs", 0, 64, parts=16), False, False)
+        mm(A("p0", 0, ND), Id, A("P3", 0, ND), True, False)
+        FW = A(FL, F, ND * FB, FB)
+        mm(A("p0", 0, ND), A("TriI4"), FW, False, False)
+        for s in range(1, ND):
+            mm(A("p0", s, ND), A("BO4"), A(FL, F, (ND - s) * FB, FB), False, s == ND - 1)
+        tt(A("zd", 0, ND), A("D4n", 0, ND), FW, Op.subtract)
+        tt(A("Ai", 0, ND), A("p0", 0, ND), A("zd", 0, ND), Op.max)
+        tt(A("Af", 0, ND), A("p0", 0, ND), A("zd", 0, ND), Op.max)
+        ts(A("lo", 0, ND), A("Ai", 0, ND), 15, Op.bitwise_and)
+        for f in range(F):
+            ts(A("SL", 8 * f, 8 * f + ND), A("Ai", 0, ND), float(f), Op.add)
+            if f == 1:
+                cp(A("lf", 0, ND), A("lo", 0, ND))
         for d in range(ND):
-            rg, ld, re_ = (A(n, 128 * d, 128 * d + 128) for n in ("RG", "LD", "RE"))
-            act(rg, A("Rc"), AF.Sign, bias=A("hh", d, d + 1))
-            mm(CN, A("BOm2"), rg, False, False)
-            ts(ld, A("IT"), A("lf", d, d + 1), Op.is_ge, -4.0, Op.mult)
-            ts(re_, A("Rc"), A("lf", 7 + d, 8 + d), Op.is_equal)
-            mm(CN, ld, re_, False, d == ND - 1)
+            ld, le = (A(n, 128 * d, 128 * d + 128) for n in ("LD", "LE"))
+            act(A("RG", 144 * d, 144 * d + 129), A("R16h", 0, 129), AF.Sign, scale=-1.0, bias=A("Af", d, d + 1))
+            ts(ld, A("IT"), A("lf", d, d + 1), Op.is_ge, 2.0, Op.mult)
+            ts(le, A("IU"), A("lf", d, d + 1), Op.is_lt, 2.0, Op.mult)
+            for b in (1, 0):
+                o = 144 * d + 64 * b
+                mm(CN[b], ld, A("RG", o + 1, o + 65), False, False)
+                mm(CN[b], le, A("RG", o, o + 64), False, d == ND - 1)
+        cp(A("SR", 64, 128), CN[1])
+        cp(A("SR", 0, 64), CN[0])
+        act(half(XN, 1), I(A("XS"), A("SR", 64, 128)))
+        cp(half(XN, 0), I(A("XS"), A("SR", 0, 64)))
         for f in range(F):
-            ts(A("SL", 8 * f, 8 * f + 7), A("AQ", 0, 7), 4.0, Op.mult, float(f), Op.add)
-        cp(A("SR"), CN)
-        act(A(XN, 1024, 2048), I(A("XS"), A("SR", 64, 128)))
-        cp(A(XN, 0, 1024), I(A("XS"), A("SR", 0, 64)))
-        for f in range(F):
-            cp(I(A(XN), A("SL", 8 * f, 8 * f + 7)), A(FL, f, 448, F))
-        if rnd < RO - 1:
-            fill(A(XN, W, W + 32), -1.0)
+            cp(I(A(XN), A("SL", 8 * f, 8 * f + ND)), A(FL, f, ND * FB, F + 1))
 
     for rnd in range(RO):
         one_round(rnd)
@@ -572,7 +667,7 @@ def rank_program(g, core, T, topo):
     sync("Y", [], y[1])
     g.sync.dma_start(T.y[:], y[0]).then_inc(T.sem.dY, 16)
     g.sync.wait_ge(T.sem.dY, 16)
-    for s in ("dX", "dW", "dT"):
+    for s in ("dX0", "dX1", "dW", "dT"):
         g.wait_ge(T.sem[s], 16)
     for q in ("V", "S", "P", "G"):
         g.wait_ge(T.sem["q" + q], done[q])

@@ -7,30 +7,31 @@ NS = ND * 16
 XW = 3072
 NONE = 2056
 DUMP = 2560
-FB = 16 * (F + 1)
 BIG = 2.0 ** 31
 ENG = 2
+CUT = 70
+ROUND16 = 1.5 * 2.0 ** 27
+ORDER = ("t70 A t50 u70 g40 B u50 f70 r40 t30 g20 u30 g60 C f50 D s20 f30 r60 E F t71 g00 u71 g61 g10 s00 r61 g41 t51 s10 u51 G H f71 t31 u31 "
+         "r41 f51 I t11 g21 J u11 K g01a s21 g01b f31 L M P N f11 s01a s01b O")
 TAG = [""]
 
 SB = {
     "X0": (XW, "bfloat16"), "X1": (XW, "bfloat16"), "X2": (XW, "bfloat16"), "XC": (2048, "bfloat16"), "wtb": (1, "bfloat16"), "thi": (2, "int32"),
     "t1f": (1, "float32"), "t2f": (1, "float32"), "ones": (2048, "bfloat16"),
-    "B144": (144, "bfloat16"), "Z": (144, "bfloat16"), "WZ": (144, "bfloat16"), "Z2": (144, "bfloat16"), "Zn": (144, "bfloat16"),
+    "B144": (144, "bfloat16"), "Z": (144, "bfloat16"), "WZ": (144, "bfloat16"), "Zn": (144, "bfloat16"),
     "Z32": (144, "bfloat16"), "Pk": (144, "bfloat16"), "BO4": (128, "bfloat16"), "TriS": (128, "bfloat16"), "TriI": (128, "bfloat16"),
     "TriI4": (128, "bfloat16"), "Id": (128, "bfloat16"), "NId": (128, "bfloat16"), "EZ": (2048, "bfloat16"),
     "M16": (272, "bfloat16"), "R16c": (128, "bfloat16"), "Rk": (128, "bfloat16"), "Rs": (128, "bfloat16"), "R64": (256, "bfloat16"),
-    "R16f": (144, "float32"), "R16h": (144, "float32"), "WM": (272, "bfloat16"), "AV": (112, "bfloat16"), "AW": (112, "bfloat16"), "SC": (1, "float32"),
-    "PP": (128, "float32"), "S2": (16, "float32"), "D4n": (8, "float32"), "RSW": (128, "bfloat16"), "R1": (128, "bfloat16"), "R2": (128, "bfloat16"),
+    "R16h": (144, "bfloat16"), "WM": (272, "bfloat16"), "AV": (112, "bfloat16"), "AW": (112, "bfloat16"), "SC": (1, "float32"),
+    "PP": (128, "float32"), "S2": (16, "float32"), "D4n": (8, "float32"), "RSW": (128, "bfloat16"), "R1": (96, "bfloat16"), "R2": (96, "bfloat16"),
     "N112": (112, "float32"), "MB": (112, "bfloat16"), "MT": (112, "int32"), "IT": (128, "bfloat16"), "IU": (128, "bfloat16"), "ITa": (128, "bfloat16"),
     "O16": (128, "float32"), "O17": (128, "float32"), "KM": (512, "bfloat16"), "KT": (528, "bfloat16"),
     "vI": (128, "int32"), "u": (128, "int32"), "h": (128, "int32"), "hb": (128, "bfloat16"), "KK": (1024, "float32"),
     "QI": (1024, "int32"), "OI": (1024, "int32"), "OF": (1024, "uint16"),
-    "E0": (576, "bfloat16"), "H0": (576, "bfloat16"), "E1": (448, "bfloat16"), "H1": (448, "bfloat16"),
-    "K3": (128, "float32"), "q3": (128, "int32"), "c3": (128, "int32"), "dp": (128, "float32"), "cc": (64, "float32"), "DV": (64, "float32"),
-    "D2": (64, "float32"), "c10": (64, "float32"), "TF": (128, "float16"),
+    "E": (1152, "bfloat16"), "DL": (1152, "float16"), "TF": (1152, "float16"), "x1": (8, "float32"), "x2": (8, "float32"), "T6": (8, "float32"),
     "NX": (2064, "float32"), "GM": (2048, "float16"), "CH": (2048, "float16"), "LS": (128, "uint16"),
-    "SA": (128, "int32"), "SM": (128, "int32"), "XS": (2064, "bfloat16"), "D1": (128, "bfloat16"),
-    "CT": (128, "bfloat16"), "CQ": (128, "bfloat16"), "TX": (32, "bfloat16"), "FX": (32, "bfloat16"), "zz": (16, "float32"), "Wz": (16, "float32"),
+    "SM": (32, "float32"), "XS": (2064, "bfloat16"), "D1": (96, "bfloat16"),
+    "CT": (96, "bfloat16"), "CQ": (96, "bfloat16"), "TX": (32, "bfloat16"), "FX": (32, "bfloat16"), "zz": (16, "float32"), "Wz": (16, "float32"),
     "f6": (16, "bfloat16"), "n6": (16, "float32"), "zs": (16, "float16"), "pl": (16, "uint16"), "VAL": (256, "float32"), "SW": (4352, "float32"),
     "Y": (112, "float32"), "YW": (112, "float32"), "VI": (112, "int32"), "PL": (112, "int32"), "dead": (112, "float32"), "PD": (112, "float32"),
     "wi": (8, "int32"), "wq": (8, "int32"), "kl": (8, "uint16"), "PR": (112, "float32"), "PW": (112, "float32"), "sl": (8, "uint16"), "P3": (8, "float16"),
@@ -38,7 +39,7 @@ SB = {
     "OA": (112, "uint16"), "GA": (448, "bfloat16"), "DA": (1792, "bfloat16"),
     "k1": (28, "float32"), "k2": (28, "float32"), "k3": (28, "float32"), "k4": (28, "float32"), "k5": (16, "float32"),
     "bi": (8, "int32"), "bm": (8, "int32"), "b3": (8, "int32"), "b4": (8, "int32"), "b5": (8, "int32"), "OL": (32, "uint16"),
-    "zd": (8, "float32"), "Af": (8, "float32"), "Ai": (8, "int32"), "lo": (8, "int32"), "lf": (8, "float32"),
+    "zd": (8, "float32"), "Af": (8, "float32"), "Ah": (8, "float32"), "c75": (8, "bfloat16"), "Lh": (128, "bfloat16"),
     "SL": (32, "uint16"), "LD": (896, "bfloat16"), "LE": (896, "bfloat16"), "RG": (1008, "bfloat16"), "SR": (128, "uint16"),
 }
 HOME = {}
@@ -67,10 +68,11 @@ for _i in range(8):
     SCRATCH["p%d" % _i] = ("psum", [128, 512], "float32")
     HOME["p%d" % _i] = ("p%d" % _i, 0)
 for _i in range(RO):
-    for _n, _c in (("AS", NS), ("AL", 4 * NS), ("FS", ND * FB), ("FL", ND * FB)):
+    for _n, _c in (("AS", NS), ("AL", 4 * NS), ("YS", ND), ("YL", ND), ("FS", F * NS), ("FL", F * NS)):
         SCRATCH["%s%d" % (_n, _i)] = ("sbuf", [128, _c], "bfloat16")
         HOME["%s%d" % (_n, _i)] = ("%s%d" % (_n, _i), 0)
-SEMAPHORES = ["qV", "qS", "qP", "qG", "dX0", "dX1", "dW", "dT", "dY"] + ["%s%d" % (n, i) for i in range(RO) for n in ("ask", "ans", "la", "lb")]
+EXCHANGES = ("ask", "yes", "ans", "la", "ly", "lb")
+SEMAPHORES = ["qV", "qS", "qP", "qG", "dX0", "dX1", "dW", "dT", "dY"] + ["%s%d" % (n, i) for i in range(RO) for n in EXCHANGES]
 
 
 def rank_program(g, core, T, topo):
@@ -93,7 +95,8 @@ def rank_program(g, core, T, topo):
         return (win[0].indirect(off[0]), win[1] + off[1])
 
     def apart(lo, hi, st, lo2, hi2, st2):
-        return lo >= hi2 or lo2 >= hi or (st > 1 and st2 > 1 and st % min(st, st2) == 0 and st2 % min(st, st2) == 0 and (lo - lo2) % min(st, st2) != 0)
+        s = min(st, st2)
+        return lo >= hi2 or lo2 >= hi or (s > 1 and st % s == 0 and st2 % s == 0 and (lo - lo2) % s != 0)
 
     def sync(q, outs, ins):
         need = {}
@@ -156,13 +159,12 @@ def rank_program(g, core, T, topo):
         do("V", lambda: g.vector.tensor_tensor(out[0], a[0], b[0], op), [out], [a, b])
 
     def ts(out, a, s1, op0, s2=None, op1=None):
-        col = isinstance(s1, tuple)
-        x1 = s1[0] if col else s1
-        ins = [a, s1] if col else [a]
+        ins = [a] + [x for x in (s1, s2) if isinstance(x, tuple)]
+        x1, x2 = (x[0] if isinstance(x, tuple) else x for x in (s1, s2))
         if op1 is None:
             do("V", lambda: g.vector.tensor_scalar(out[0], a[0], x1, None, op0), [out], ins)
         else:
-            do("V", lambda: g.vector.tensor_scalar(out[0], a[0], x1, s2, op0, op1), [out], ins)
+            do("V", lambda: g.vector.tensor_scalar(out[0], a[0], x1, x2, op0, op1), [out], ins)
 
     def scan(out, a, b, op0=Op.mult, op1=Op.add, initial=0.0):
         do("V", lambda: g.vector.tensor_tensor_scan(out[0], a[0], b[0], initial, op0, op1), [out], [a, b])
@@ -219,35 +221,35 @@ def rank_program(g, core, T, topo):
         if j == 0:
             fill(A("ones", 272, 2048), 1.0)
         if j == 1:
-            for name in ("E0", "E1"):
+            fill(A("E", 0, 1152, 9), 0.0)
+            for name in ("TX", "FX"):
                 fill(A(name), 0.0)
         if j == 2:
-            for name in ("FS0", "FS1"):
-                fill(A(name), 0.0)
-        if j == 3:
-            for name in ("D1", "TX", "FX"):
-                fill(A(name), 0.0)
             fill(A("XS", W, W + 16), 512.0)
-    ts(A("WZ"), A("Z"), A("wtb"), Op.mult)
-    cp(A("t1f"), A("thi", 0, 1))
-    ts(A("t2f"), A("thi", 1, 2), 32.0, Op.mult)
+            fill(A("c75"), 7.5)
+        if j == 3:
+            ts(A("WZ"), A("Z"), A("wtb"), Op.mult)
+            cp(A("t1f"), A("thi", 0, 1))
+        if j == 4:
+            ts(A("t2f"), A("thi", 1, 2), 32.0, Op.mult)
     act(A("NId"), Id, scale=-1.0)
-    act(A("Z2"), A("Z"), scale=2.0)
     act(A("Zn"), A("Z"), scale=-1.0)
     act(A("Z32"), A("Z"), scale=32.0)
     act(A("BO4"), BO, scale=1.0 / 1024)
-    mm(A("p3", 0, 272), L16, A("M16", parts=16))
-    mm(A("p4", 0, 128), L16, A("R16c", parts=16), True, False)
-    mm(A("p4", 0, 128), L16, A("Rk", parts=16), False, True)
-    act(A("WM"), A("p3", 0, 272))
-    act(A("PP"), A("p4", 0, 128))
+    act(A("Lh", parts=16), L16, scale=0.5)
 
     def constants_G():
+        mm(A("p3", 0, 272), L16, A("M16", parts=16))
+        mm(A("p4", 0, 128), L16, A("R16c", parts=16), True, False)
+        mm(A("p4", 0, 128), L16, A("Rk", parts=16), False, True)
+        act(A("WM"), A("p3", 0, 272))
+        act(A("PP"), A("p4", 0, 128))
         sel(A("EZ"), A("ones"), [[-1, 16], [-16, 8], [0, 16]], Op.is_equal, 0, 1)
+        iota(A("T6"), [[1, 8]], -1024, 0)
         sel(A("Pk"), A("ones", 0, 144), [[-16, 9], [-8, 16]], Op.is_equal, 112, 1)
         sel(A("Pk"), A("Pk"), [[0, 9], [1, 16]], Op.is_ge, -14, 0)
         sel(A("RSW"), A("ones", 0, 128), [[0, 8], [1, 16]], Op.is_gt, 0, 0)
-        sel(A("R1"), A("ones", 0, 128), [[0, 16], [1, 8]], Op.not_equal, -1, 0)
+        sel(A("R1"), A("ones", 0, 96), [[0, 16], [1, 6]], Op.is_gt, 0, 0)
         sel(A("TriS"), BO, [[1, 128]], Op.is_gt, 0, -1)
         sel(A("TriI"), BO, [[1, 128]], Op.is_ge, 0, -1)
         iota(A("R64", parts=16), [[64, 256]], 0, 0)
@@ -256,21 +258,20 @@ def rank_program(g, core, T, topo):
         iota(A("MB"), [[2, 16], [0, ND]], 0, 0)
         iota(A("MT"), [[2, 16], [0, ND]], 1, 0)
         iota(A("ITa"), [[0, 8], [1, 16]], 1, 0)
-        iota(A("R16f"), [[16, 144]], 0, 0)
+        iota(A("R16h", 0, 129), [[16, 129]], -8, 0)
 
     def constants_late():
         act(A("R2"), A("R1"), scale=2.0)
         act(A("TriI4"), A("TriI"), scale=1.0 / 1024)
         act(A("S2"), A("PP", 0, 16), scale=2.0, bias=2048.0)
-        act(A("D4n", 0, ND), A("PP", 0, ND), scale=4.0, bias=float(DUMP))
-        act(A("R16h"), A("R16f"), bias=-0.5)
-        ts(A("SM", 0, 16), A("PP", 0, 16), 8.0, Op.mult)
+        act(A("D4n", 0, ND), A("PP", 0, ND), scale=4.0, bias=DUMP - 7.5)
+        ts(A("CH", 15, 256, 16), A("PP", 0, 16), 8.0, Op.mult, -1025.0, Op.add)
         ts(A("AV"), A("WM", 15, 15 + NS), BIG, Op.mult, 1.0, Op.max)
         ts(A("SC"), A("WM", 15, 16), 1.0, Op.mult, 1.0 / BIG, Op.max)
         tt(A("O16"), A("ITa"), BO, Op.mult)
-        ts(A("O17"), BO, -100.0, Op.mult, 99.0, Op.add)
+        ts(A("O17"), BO, -108.5, Op.mult, 100.0, Op.add)
         tt(A("AW"), A("AV"), A("WM", 0, NS), Op.subtract)
-        ts(A("IT"), A("O16"), 1.0, Op.subtract)
+        ts(A("IT"), A("O16"), 8.5, Op.subtract)
         tt(A("IU"), A("O16"), A("O17"), Op.add)
 
     def exchange(src, dst, w, ls, rs, back):
@@ -296,9 +297,6 @@ def rank_program(g, core, T, topo):
 
         def lk(name, b, m0, m1=None):
             return A(name, 512 * b + 64 * m0, 512 * b + 64 * (m0 + 1 if m1 is None else m1))
-
-        def temp(k):
-            return A("p7", 128 + 64 * k, 192 + 64 * k)
 
         def pd(m, b, lo=0, hi=64):
             bank, o = ("p1", 64 * m) if b == 0 else ("p2", 64 * m) if m > 1 else ("p0", 128) if m else ("p1", 0)
@@ -334,54 +332,58 @@ def rank_program(g, core, T, topo):
             o = 512 * b + 64 * m
             tt(part("D%d_", m, b, lo, hi), I(win, A("OF", o + lo, o + hi)), A("XC", 1024 * b + 16 * lo, 1024 * b + 16 * hi), Op.subtract)
 
-        def relu(m, b):
-            ts(part("R%d_", m, b, 0, 64), part("D%d_", m, b, 0, 64), 0.0, Op.max)
-            sums(m, b, (("Zn", "D%d_"), ("Z2", "R%d_")))
+        def relu(m, b, lo=0, hi=64):
+            ts(part("R%d_", m, b, lo, hi), part("D%d_", m, b, lo, hi), 0.0, Op.max, 2.0, Op.mult)
+            sums(m, b, (("Zn", "D%d_"), ("Z", "R%d_")), lo, hi)
 
         def size(m, b, lo=0, hi=64):
             act(part("R%d_", m, b, lo, hi), part("D%d_", m, b, lo, hi), AF.Abs)
             sums(m, b, (("Z", "R%d_"),), lo, hi)
 
-        turn = [0]
+        banks = {}
 
         def take(m, b):
             act(half("D%d_" % m, b), I(win, lk("OF", b, m)))
-            turn[0] = 1 - turn[0]
+            banks[(m, b)] = 3 + 2 * (len(banks) % 2)
+
+        def under(m, b):
             for x in range(2):
-                o, c = A("p%d" % (3 + 2 * turn[0] + x)), 1024 * b + 512 * x
+                o, c = A("p%d" % (banks[(m, b)] + x)), 1024 * b + 512 * x
                 mm(o, A("NId"), A(X, c, c + 512), True, False)
                 mm(o, Id, A("D%d_" % m, c, c + 512), False, True)
-            return (m, b, 3 + 2 * turn[0])
 
-        def finish(t):
-            m, b, bank = t
+        def finish(m, b):
             for x in range(2):
-                act(part("R%d_", m, b, 32 * x, 32 * x + 32), A("p%d" % (bank + x)), AF.Abs)
+                act(part("R%d_", m, b, 32 * x, 32 * x + 32), A("p%d" % (banks[(m, b)] + x)), AF.Abs)
             sums(m, b, (("Z", "R%d_"),))
 
+        def slot(name, b, k):
+            return A(name, 576 * b + k, 576 * b + 576, 9)
+
         def far(b, ms):
-            n = 9 - 2 * b
             for m in ms:
-                ts(A("E%d" % b, 8 - m, 64 * n, n), pd(m, b), A("t1f"), Op.is_ge)
+                ts(slot("E", b, 8 - m), pd(m, b), A("t1f"), Op.is_ge)
 
-        def first_near(b):
-            n, m0 = 9 - 2 * b, 2 * b
-            M = A("H%d" % b, n - 1, 64 * n, n)
-            K, q, c, dp = (hw(x, b) for x in ("K3", "q3", "c3", "dp"))
-            return [lambda: scan(A("H%d" % b), A("E%d" % b), A("E%d" % b)),
-                    lambda: (ts(temp(0), M, 2.0, Op.mult, 2.0 * m0 + 1, Op.add), ts(temp(1), M, float(n - 1), Op.is_ge)),
-                    lambda: tt(K, temp(0), hw("hb", b), Op.add),
-                    lambda: tt(q, K, hw("p7", b), Op.mult),
-                    lambda: ts(c, q, 2047, Op.bitwise_and),
-                    lambda: tt(dp, hw("PP", b), c, Op.subtract),
-                    lambda: tt(temp(0), temp(1), dp, Op.mult)]
+        def steps(b, ks):
+            for k in ks:
+                if k == 8:
+                    cp(slot("DL", b, 8), lk("OI", b, 0))
+                else:
+                    tt(slot("DL", b, k), lk("OI", b, 8 - k) if k else hw("PP", b), lk("OI", b, 7 - k), Op.subtract)
 
-        def spread(b, banks):
-            for i in range(16):
-                mm(A(banks[i // 8], 64 * (i % 8), 64 * (i % 8) + 64), EZ(i), hw("TF", b))
+        def choose(b):
+            scan(A("TF", 576 * b, 576 * b + 576), A("E", 576 * b, 576 * b + 576), A("DL", 576 * b, 576 * b + 576))
 
-        def table(b, banks, i):
-            return A("NX", 1024 * b + i, 1024 * b + 1024, 16), A(banks[i // 8], 64 * (i % 8), 64 * (i % 8) + 64)
+        def spread(b, bk, which):
+            for i in which:
+                mm(A(bk[i // 8], 64 * (i % 8), 64 * (i % 8) + 64), EZ(i), slot("TF", b, 8))
+
+        def table(b, bk, i, q):
+            o, n = A("NX", 1024 * b + i, 1024 * b + 1024, 16), A(bk[i // 8], 64 * (i % 8), 64 * (i % 8) + 64)
+            if q == "V":
+                ts(o, n, -1024.0, Op.add)
+            else:
+                act(o, n, bias=-1024.0)
 
         TAG[0] = "head"
         for b in range(2):
@@ -406,104 +408,53 @@ def rank_program(g, core, T, topo):
         offsets(0, 7, 8)
         offsets(0, 4, 7)
         cp(hw("vI", 1), hw("p0", 1))
-        TAG[0] = "dist0"
-        t7 = take(7, 0)
-        gather(6, 0)
-        times(0, (3, 2, 1, 0))
-        split(1)
-        t5 = take(5, 0)
-        gather(4, 0)
-        mod(0, 0, 4)
-        cp(hw("hb", 1), hw("h", 1))
-        cp(hw("p7", 1), hw("u", 1))
-        offsets(0, 0, 4)
-        relu(6, 0)
-        finish(t7)
-        plus(1, range(7, -1, -1))
-        t3 = take(3, 0)
-        gather(2, 0)
-        times(1, range(7, -1, -1))
-        relu(4, 0)
-        finish(t5)
-        mod(1, 0, 8)
-        t1 = take(1, 0)
-        gather(0, 0)
-        offsets(1, 0, 8)
-        relu(2, 0)
-        finish(t3)
-        relu(0, 0)
-        TAG[0] = "dist1"
-        t7 = take(7, 1)
-        gather(6, 1)
-        finish(t1)
-        t5 = take(5, 1)
-        gather(4, 1)
-        far(0, range(7, -1, -1))
-        steps = first_near(0)
-        relu(6, 1)
-        finish(t7)
-        steps[0]()
-        relu(4, 1)
-        for s in steps[1:4]:
-            s()
-        t3 = take(3, 1)
-        gather(2, 1, 0, 32)
-        steps[4]()
-        gather(2, 1, 32, 64)
-        steps[5]()
-        finish(t5)
-        fill(A("SW", 0, NS), 0.0)
-        tt(A("c10"), lk("OI", 1, 1), lk("OI", 1, 0), Op.subtract)
-        steps[6]()
-        relu(2, 1)
-        tt(hw("TF", 0), temp(0), hw("c3", 0), Op.add)
-        finish(t3)
-        spread(0, ("p0", "p1"))
-        TAG[0] = "last"
-        gather(1, 1, 0, 32)
-        gather(1, 1, 32, 64)
-        for i in range(16):
-            act(*table(0, ("p0", "p1"), i))
-        far(1, range(7, 1, -1))
-        steps = first_near(1)
-        size(1, 1)
-        steps[0]()
-        gather(0, 1, 0, 32)
-        steps[1]()
-        steps[2]()
-        gather(0, 1, 32, 64)
-        size(0, 1, 0, 32)
-        size(0, 1, 32, 64)
-        for s in steps[3:6]:
-            s()
-        tt(A("cc"), hw("c3", 1), lk("OI", 1, 1), Op.subtract)
-        steps[6]()
-        ts(temp(2), pd(1, 1), A("t1f"), Op.is_ge)
-        tt(A("D2"), temp(0), A("cc"), Op.add)
-        tt(temp(3), temp(2), A("D2"), Op.mult)
-        tt(A("DV"), temp(3), A("c10"), Op.add)
-        ts(temp(4), pd(0, 1), A("t1f"), Op.is_ge)
-        tt(temp(5), temp(4), A("DV"), Op.mult)
-        tt(hw("TF", 1), temp(5), lk("OI", 1, 0), Op.add)
+        TAG[0] = "dist"
+        small = {
+            "A": lambda: (times(0, (3, 2, 1, 0)), split(1)),
+            "B": lambda: (mod(0, 0, 4), cp(hw("hb", 1), hw("h", 1)), cp(hw("p7", 1), hw("u", 1)), offsets(0, 0, 4)),
+            "C": lambda: plus(1, range(7, -1, -1)),
+            "D": lambda: times(1, range(7, -1, -1)),
+            "E": lambda: mod(1, 0, 8),
+            "F": lambda: offsets(1, 0, 8),
+            "G": lambda: steps(0, range(9)),
+            "H": lambda: far(0, range(8)),
+            "I": lambda: (choose(0), spread(0, ("p0", "p1"), range(16))),
+            "J": lambda: steps(1, range(9)),
+            "K": lambda: [table(0, ("p0", "p1"), i, "V") for i in range(8)],
+            "L": lambda: [table(0, ("p0", "p1"), i, "V") for i in range(8, 16)],
+            "k": lambda: [table(0, ("p0", "p1"), i, "S") for i in range(8)],
+            "l": lambda: [table(0, ("p0", "p1"), i, "S") for i in range(8, 16)],
+            "M": lambda: (fill(A("SW", 0, NS), 0.0), tt(A("x1", 0, 6), A("NX", 0, 6), A("T6", 0, 6), Op.is_equal)),
+            "N": lambda: ts(A("x2", 0, 6), A("x1", 0, 6), 2048.0, Op.mult),
+            "O": lambda: tt(A("NX", W, W + 6), A("NX", 0, 6), A("x2", 0, 6), Op.add),
+            "P": lambda: far(1, range(7, 1, -1)),
+        }
+        calls = {"t": take, "u": under, "f": finish, "g": gather, "r": relu, "s": size}
+        for w in ORDER.split():
+            if len(w) == 1:
+                small[w]()
+            else:
+                calls[w[0]](int(w[1]), int(w[2]), *{"": (), "a": (0, 32), "b": (32, 64)}[w[3:]])
+        far(1, (1, 0))
+        choose(1)
         TAG[0] = "table"
-        act(A("NX", W, W + 1), A("NX", 0, 1))
-        act(A(X, W, W + F), A(X, 0, F))
+        free = 3 + 2 * (len(banks) % 2)
+        last = ("p%d" % free, "p%d" % (free + 1))
+        act(A(X, W, W + 8), A(X, 0, 8))
+        spread(1, last, list(range(8, 16)) + list(range(8)))
         for t in range(8):
-            mm(A("p2", 0, 16), A("Pk", 14 - 2 * t, 142 - 2 * t), A("TF", t, 128, 8), t == 0, t == 7)
-        spread(1, ("p3", "p4"))
-        ts(A("LS", 16, 32), A("p2", 0, 16), 1.0, Op.add)
-        ts(A("SA", 16, 32), A("p2", 0, 16), 1.0, Op.add)
-        tt(A("D1", 1, 128, 8), A("p2", 0, 16), A("SM", 0, 16), Op.not_equal)
+            mm(A("p2", 0, 16), A("Pk", 14 - 2 * t, 142 - 2 * t), A("TF", 9 * t + 8, 1152, 72), t == 0, t == 7)
         for i in range(8):
-            cp(*table(1, ("p3", "p4"), i))
-            act(*table(1, ("p3", "p4"), 8 + i))
+            table(1, last, 8 + i, "S")
+        for i in range(8):
+            table(1, last, i, "V")
+        ts(A("LS", 16, 32), A("p2", 0, 16), 1.0, Op.add)
+        ts(A("CH", 256 + 15, 512, 16), A("p2", 0, 16), -1024.0, Op.add)
 
     def one_round(rnd):
         X, XN = "X%d" % rnd, "X%d" % (rnd + 1)
-        AL, AS, FL, FS = ("%s%d" % (n, rnd) for n in ("AL", "AS", "FL", "FS"))
-        win = A(X, 0, W + F)
-        if rnd == 0:
-            ts(A("SM", 0, 16), A("PP", 0, 16), 8.0, Op.mult)
+        AL, AS, YL, YS, FL, FS = ("%s%d" % (n, rnd) for n in ("AL", "AS", "YL", "YS", "FL", "FS"))
+        win = A(X, 0, W + 8)
         successors(rnd)
 
         TAG[0] = "runs"
@@ -511,43 +462,52 @@ def rank_program(g, core, T, topo):
         def step(name, k):
             return A(name, 16 * k, 16 * k + 16)
 
+        def col(k):
+            return A("CH", 256 * k + 15, 256 * k + 256, 16)
+
+        TW = A("CT", 5, 96, 6)
         act(A("XS", 0, W, 8), A(X, 0, W, 8))
         act(A("XS", 1, W, 8), I(win, step("LS", 1)))
         for k in range(2, 8):
             o = 256 * k
-            C = A("CH", o + 15, o + 256, 16)
             for b in range(2):
-                tt(A("GM", o + 128 * b, o + 128 * b + 128), I(A("NX", 0, W + 1), A("LS", 16 * k - 16 + 8 * b, 16 * k - 8 + 8 * b)), A("WM", 0, 128), Op.mult)
-            ts(step("SM", k - 1), step("SA", k - 1), 2047, Op.bitwise_and)
-            for b in range(2):
-                scan(A("CH", o + 128 * b, o + 128 * b + 128), A("RSW"), A("GM", o + 128 * b, o + 128 * b + 128))
-            if k == 7:
-                break
-            for b in range(2):
-                ts(A("LS", 16 * k + 8 * b, 16 * k + 8 * b + 8), A("CH", o + 128 * b + 15, o + 128 * b + 128, 16), 1.0, Op.add)
-            tt(A("D1", k, 128, 8), C, step("SM", k - 1), Op.not_equal)
-            ts(step("SA", k), C, 1.0, Op.add)
-            act(A("XS", k, W, 8), I(win, step("LS", k)))
+                tt(A("GM", o + 128 * b, o + 128 * b + 128), I(A("NX", 0, W + 6), A("LS", 16 * k - 16 + 8 * b, 16 * k - 8 + 8 * b)), A("WM", 0, 128), Op.mult)
             if k == 2 and rnd == 0:
                 constants_late()
             if k == 6:
-                TW = A("CT", 6, 128, 8)
+                for j in range(6):
+                    mm(A("p2", j, 96, 6), Id, col(min(j + 1, 5)), True, False)
+                    mm(A("p2", j, 96, 6), A("NId"), col(j), False, True)
+                ts(step("SM", 0), col(5), 1.0, Op.add)
+            if k == 7:
+                ts(step("SM", 1), col(6), 1.0, Op.add)
+                ts(A("zz"), TW, 0.0, Op.is_equal)
+                scan(A("TX", 1, 17), A("ones", 0, 16), TW)
+            for b in range(2):
+                scan(A("CH", o + 128 * b, o + 128 * b + 128), A("RSW"), A("GM", o + 128 * b, o + 128 * b + 128))
+            if k == 6:
+                ts(A("D1"), A("p2", 0, 96), 1.0, Op.not_equal)
+            if k == 7:
+                break
+            for b in range(2):
+                ts(A("LS", 16 * k + 8 * b, 16 * k + 8 * b + 8), A("CH", o + 128 * b + 15, o + 128 * b + 128, 16), 1025.0, Op.add)
+            act(A("XS", k, W, 8), I(win, step("LS", k)))
+            if k == 6:
+                tt(A("D1", 5, 96, 6), col(6), step("SM", 0), Op.not_equal)
                 scan(A("CQ"), A("R2"), A("D1"))
                 scan(A("CT"), A("R1"), A("D1"))
                 mm(A("p0", 0, 256), A("ones", 0, 128, parts=1), A("R64", parts=1), True, False)
                 for i in range(16):
-                    mm(A("p0", i, 256, 16), EZ(i), A("CQ", 6, 128, 8), False, i == 15)
+                    mm(A("p0", i, 256, 16), EZ(i), A("CQ", 5, 96, 6), False, i == 15)
                 act(A("VAL"), A("p0", 0, 256), scale=8.0)
-                ts(A("zz"), TW, 0.0, Op.is_equal)
-                scan(A("TX", 1, 17), A("ones", 0, 16), TW)
-                tt(A("Wz"), A("zz"), A("S2"), Op.mult)
-                mm(A("p1", 0, 17), BO, A("TX", 0, 17), True, False)
-                mm(A("p1", 0, 16), A("TriS"), TW, False, False)
+        tt(A("Wz"), A("zz"), A("S2"), Op.mult)
+        mm(A("p1", 0, 17), BO, A("TX", 0, 17), True, False)
+        mm(A("p1", 0, 16), A("TriS"), TW, False, False)
 
         TAG[0] = "sites"
-        tt(A("f6"), C, step("SM", 6), Op.not_equal)
-        tt(A("n6"), C, step("SM", 6), Op.is_equal)
-        ts(step("LS", 7), C, 1.0, Op.add)
+        tt(A("f6"), col(7), step("SM", 1), Op.not_equal)
+        tt(A("n6"), col(7), step("SM", 1), Op.is_equal)
+        ts(step("LS", 7), col(7), 1025.0, Op.add)
         act(A("XS", 7, W, 8), I(win, step("LS", 7)))
         scan(A("FX", 1, 17), A("ones", 0, 16), A("f6"))
         tt(A("zs"), A("n6"), A("Wz"), Op.mult)
@@ -576,20 +536,23 @@ def rank_program(g, core, T, topo):
         keys = (("p1", 0, 8), ("p2", 8, 12), ("p4", 12, 16))
         for p, m0, m1 in keys:
             mm(A(p, 0, ND * (m1 - m0)), Id, A("MB", ND * m0, ND * m1), True, False)
+        for i in range(16):
+            mm(A("p0", 0, ND), Z("WZ", i), A(AL, i, NS, 16), i == 0, i == 15)
         for b in range(1, 4):
             cp(A(AL, NS * b, NS * b + NS), A(AL, 0, NS))
-        for i in range(16):
-            mm(A("p0", 0, 28), Z("WZ", i), A(AL, i, 4 * NS, 16), i == 0, i == 15)
         mm(A("p3", 0, 448), A("NId"), A(AL), True, False)
-        cp(A("aI"), A("p0", 0, 28))
+        for a in range(4):
+            cp(A("aI", ND * a, ND * a + ND), A("p0", 0, ND))
         ts(A("H4"), A("aI"), 5, Op.logical_shift_right, 63, Op.bitwise_and)
         ts(A("U4"), A("aI"), 2047, Op.bitwise_and)
         for a in range(4):
             tt(A("K16", 28 * a, 28 * a + 28), A("H4"), A("MT", 28 * a, 28 * a + 28), Op.add)
         for a in range(4):
             tt(A("Q16", 28 * a, 28 * a + 28), A("K16", 28 * a, 28 * a + 28), A("U4"), Op.mult)
-        ts(A("C16"), A("Q16"), 2047, Op.bitwise_and)
-        cp(A("OA"), A("C16"))
+        for a in range(2):
+            ts(A("C16", 56 * a, 56 * a + 56), A("Q16", 56 * a, 56 * a + 56), 2047, Op.bitwise_and)
+        for a in range(2):
+            cp(A("OA", 56 * a, 56 * a + 56), A("C16", 56 * a, 56 * a + 56))
 
         def quarter(b):
             return A("DA", 448 * b, 448 * b + 448)
@@ -613,52 +576,48 @@ def rank_program(g, core, T, topo):
         tt(A("k4"), A("p4", 0, 28), A("k3"), Op.min)
         tt(A("k5", 0, 14), A("k4", 0, 14), A("k4", 14, 28), Op.min)
         tt(A("bi", 0, ND), A("k5", 0, ND), A("k5", ND, 14), Op.min)
+        ts(A(YS), A("bi", 0, ND), A("t2f"), Op.is_lt, 4096.0, Op.mult)
+        exchange(YS, YL, 1, "ly%d" % rnd, "yes%d" % rnd, True)
         ts(A("bm", 0, ND), A("bi", 0, ND), 31, Op.bitwise_and)
-        ts(A(FS, F, ND * FB, FB), A("bi", 0, ND), A("t2f"), Op.is_lt, 4096.0, Op.mult)
         tt(A("b3", 0, ND), A("bm", 0, ND), A("K16", 0, ND), Op.add)
         tt(A("b4", 0, ND), A("b3", 0, ND), A("U4", 0, ND), Op.mult)
         ts(A("b5", 0, ND), A("b4", 0, ND), 2047, Op.bitwise_and)
-        for f in (2, 3, 0, 1):
-            ts(A("OL", 8 * f, 8 * f + ND), A("b5", 0, ND), float(1 + f), Op.add)
-            if f > 1:
-                act(A(FS, f, ND * FB, F + 1), I(win, A("OL", 8 * f, 8 * f + ND)))
-        for f in (0, 1):
-            cp(A(FS, f, ND * FB, F + 1), I(win, A("OL", 8 * f, 8 * f + ND)))
-        exchange(FS, FL, FB, "lb%d" % rnd, "ans%d" % rnd, True)
+        for f in range(F):
+            ts(A("OL", f, F * ND, F), A("b5", 0, ND), float(1 + f), Op.add)
+        cp(A(FS), I(win, A("OL", 0, F * ND)))
+        exchange(FS, FL, 16 * F, "lb%d" % rnd, "ans%d" % rnd, True)
 
         TAG[0] = "next"
         CN = [A("p5", 0, 64), A("p6", 0, 64)]
         for b in range(2):
-            mm(CN[b], L16, A("R16c", 64 * b, 64 * b + 64, parts=16), True, False)
-            mm(CN[b], L16, A("Rs", 0, 64, parts=16), False, False)
+            mm(CN[b], A("Lh", parts=16), A("R16c", 64 * b, 64 * b + 64, parts=16), True, False)
+            mm(CN[b], A("Lh", parts=16), A("Rs", 0, 64, parts=16), False, False)
         mm(A("p0", 0, ND), Id, A("P3", 0, ND), True, False)
-        FW = A(FL, F, ND * FB, FB)
-        mm(A("p0", 0, ND), A("TriI4"), FW, False, False)
+        mm(A("p0", 0, ND), A("NId"), A("c75", 0, ND), False, False)
+        mm(A("p0", 0, ND), A("TriI4"), A(YL), False, False)
         for s in range(1, ND):
-            mm(A("p0", s, ND), A("BO4"), A(FL, F, (ND - s) * FB, FB), False, s == ND - 1)
-        tt(A("zd", 0, ND), A("D4n", 0, ND), FW, Op.subtract)
-        tt(A("Ai", 0, ND), A("p0", 0, ND), A("zd", 0, ND), Op.max)
+            mm(A("p0", s, ND), A("BO4"), A(YL, 0, ND - s), False, s == ND - 1)
+        tt(A("zd", 0, ND), A("D4n", 0, ND), A(YL), Op.subtract)
         tt(A("Af", 0, ND), A("p0", 0, ND), A("zd", 0, ND), Op.max)
-        ts(A("lo", 0, ND), A("Ai", 0, ND), 15, Op.bitwise_and)
-        for f in range(F):
-            ts(A("SL", 8 * f, 8 * f + ND), A("Ai", 0, ND), float(f), Op.add)
-            if f == 1:
-                cp(A("lf", 0, ND), A("lo", 0, ND))
+        ts(A("Ah", 0, ND), A("Af", 0, ND), ROUND16, Op.add, ROUND16, Op.subtract)
+        for f in range(2):
+            ts(A("SL", f, F * ND, F), A("Af", 0, ND), f + 7.5, Op.add)
         for d in range(ND):
             ld, le = (A(n, 128 * d, 128 * d + 128) for n in ("LD", "LE"))
             act(A("RG", 144 * d, 144 * d + 129), A("R16h", 0, 129), AF.Sign, scale=-1.0, bias=A("Af", d, d + 1))
-            ts(ld, A("IT"), A("lf", d, d + 1), Op.is_ge, 2.0, Op.mult)
-            ts(le, A("IU"), A("lf", d, d + 1), Op.is_lt, 2.0, Op.mult)
+            ts(ld, A("IT"), A("Ah", d, d + 1), Op.add, A("Af", d, d + 1), Op.is_ge)
+            ts(le, A("IU"), A("Ah", d, d + 1), Op.add, A("Af", d, d + 1), Op.is_lt)
             for b in (1, 0):
                 o = 144 * d + 64 * b
                 mm(CN[b], ld, A("RG", o + 1, o + 65), False, False)
                 mm(CN[b], le, A("RG", o, o + 64), False, d == ND - 1)
-        cp(A("SR", 64, 128), CN[1])
-        cp(A("SR", 0, 64), CN[0])
-        act(half(XN, 1), I(A("XS"), A("SR", 64, 128)))
-        cp(half(XN, 0), I(A("XS"), A("SR", 0, 64)))
-        for f in range(F):
-            cp(I(A(XN), A("SL", 8 * f, 8 * f + ND)), A(FL, f, ND * FB, F + 1))
+        for f in range(2, F):
+            ts(A("SL", f, F * ND, F), A("Af", 0, ND), f + 7.5, Op.add)
+        ts(A("SR", 64, 128), CN[1], 2.0, Op.mult)
+        ts(A("SR", 0, 64), CN[0], 2.0, Op.mult)
+        act(A(XN, 16 * CUT, W), I(A("XS"), A("SR", CUT, 128)))
+        cp(A(XN, 0, 16 * CUT), I(A("XS"), A("SR", 0, CUT)))
+        cp(I(A(XN), A("SL", 0, F * ND)), A(FL))
 
     for rnd in range(RO):
         one_round(rnd)
@@ -672,5 +631,5 @@ def rank_program(g, core, T, topo):
     for q in ("V", "S", "P", "G"):
         g.wait_ge(T.sem["q" + q], done[q])
     for rnd in range(RO):
-        for n in ("la", "lb", "ask", "ans"):
+        for n in EXCHANGES:
             g.wait_ge(T.sem["%s%d" % (n, rnd)], ENG * ND)

@@ -5,6 +5,7 @@ NR, W, F, RO = 8, 2048, 4, 2
 ND = NR - 1
 NS = ND * 16
 XW = 3072
+XB = W + 8
 NONE = 2056
 DUMP = 2560
 BIG = 2.0 ** 31
@@ -17,12 +18,12 @@ TAG = [""]
 
 SB = {
     "X0": (XW, "bfloat16"), "X1": (XW, "bfloat16"), "X2": (XW, "bfloat16"), "XC": (2048, "bfloat16"), "wtb": (1, "bfloat16"), "thi": (2, "int32"),
-    "t1f": (1, "float32"), "t2f": (1, "float32"), "ones": (2048, "bfloat16"),
+    "t1f": (1, "float32"), "ones": (2048, "bfloat16"),
     "B144": (144, "bfloat16"), "Z": (144, "bfloat16"), "WZ": (144, "bfloat16"), "Zn": (144, "bfloat16"),
     "Z32": (144, "bfloat16"), "Pk": (144, "bfloat16"), "BO4": (128, "bfloat16"), "TriS": (128, "bfloat16"), "TriI": (128, "bfloat16"),
     "TriI4": (128, "bfloat16"), "Id": (128, "bfloat16"), "NId": (128, "bfloat16"), "EZ": (2048, "bfloat16"),
     "M16": (272, "bfloat16"), "R16c": (128, "bfloat16"), "Rk": (128, "bfloat16"), "Rs": (128, "bfloat16"), "R64": (256, "bfloat16"),
-    "R16h": (144, "bfloat16"), "WM": (272, "bfloat16"), "AV": (112, "bfloat16"), "AW": (112, "bfloat16"), "SC": (1, "float32"),
+    "R16h": (144, "float32"), "WM": (272, "bfloat16"), "AV": (112, "bfloat16"), "AW": (112, "bfloat16"), "SC": (1, "float32"),
     "PP": (128, "float32"), "S2": (16, "float32"), "D4n": (8, "float32"), "RSW": (128, "bfloat16"), "R1": (96, "bfloat16"), "R2": (96, "bfloat16"),
     "N112": (112, "float32"), "MB": (112, "bfloat16"), "MT": (112, "int32"), "IT": (128, "bfloat16"), "IU": (128, "bfloat16"), "ITa": (128, "bfloat16"),
     "O16": (128, "float32"), "O17": (128, "float32"), "KM": (512, "bfloat16"), "KT": (528, "bfloat16"),
@@ -36,10 +37,11 @@ SB = {
     "Y": (112, "float32"), "YW": (112, "float32"), "VI": (112, "int32"), "PL": (112, "int32"), "dead": (112, "float32"), "PD": (112, "float32"),
     "wi": (8, "int32"), "wq": (8, "int32"), "kl": (8, "uint16"), "PR": (112, "float32"), "PW": (112, "float32"), "sl": (8, "uint16"), "P3": (8, "float16"),
     "aI": (28, "int32"), "U4": (28, "int32"), "H4": (28, "int32"), "K16": (112, "int32"), "Q16": (112, "int32"), "C16": (112, "int32"),
-    "OA": (112, "uint16"), "GA": (448, "bfloat16"), "DA": (1792, "bfloat16"),
+    "O16A": (112, "int32"), "MO": (56, "int32"), "WB": (896, "bfloat16"), "HW": (112, "float32"), "A4": (448, "bfloat16"), "FL": (448, "bfloat16"),
+    "yes": (8, "bfloat16"), "no": (8, "float32"), "b6": (8, "int32"), "OA": (112, "uint16"), "GA": (448, "bfloat16"), "DA": (1792, "bfloat16"),
     "k1": (28, "float32"), "k2": (28, "float32"), "k3": (28, "float32"), "k4": (28, "float32"), "k5": (16, "float32"),
     "bi": (8, "int32"), "bm": (8, "int32"), "b3": (8, "int32"), "b4": (8, "int32"), "b5": (8, "int32"), "OL": (32, "uint16"),
-    "zd": (8, "float32"), "Af": (8, "float32"), "Ah": (8, "float32"), "c75": (8, "bfloat16"), "Lh": (128, "bfloat16"),
+    "zd": (8, "float32"), "Af": (8, "float32"), "Ah": (8, "float32"), "c85": (8, "bfloat16"), "Lh": (128, "bfloat16"),
     "SL": (32, "uint16"), "LD": (896, "bfloat16"), "LE": (896, "bfloat16"), "RG": (1008, "bfloat16"), "SR": (128, "uint16"),
 }
 HOME = {}
@@ -63,16 +65,15 @@ def _pack():
 SCRATCH = {k: ("sbuf", [128, c], d) for k, (c, d) in _pack().items()}
 for _i in range(8):
     for _n in ("D%d_", "R%d_"):
-        SCRATCH[_n % _i] = ("sbuf", [128, 2048], "bfloat16")
+        SCRATCH[_n % _i] = ("sbuf", [128, 1024], "bfloat16")
         HOME[_n % _i] = (_n % _i, 0)
     SCRATCH["p%d" % _i] = ("psum", [128, 512], "float32")
     HOME["p%d" % _i] = ("p%d" % _i, 0)
-for _i in range(RO):
-    for _n, _c in (("AS", NS), ("AL", 4 * NS), ("YS", ND), ("YL", ND), ("FS", F * NS), ("FL", F * NS)):
-        SCRATCH["%s%d" % (_n, _i)] = ("sbuf", [128, _c], "bfloat16")
-        HOME["%s%d" % (_n, _i)] = ("%s%d" % (_n, _i), 0)
-EXCHANGES = ("ask", "yes", "ans", "la", "ly", "lb")
-SEMAPHORES = ["qV", "qS", "qP", "qG", "dX0", "dX1", "dW", "dT", "dY"] + ["%s%d" % (n, i) for i in range(RO) for n in EXCHANGES]
+for _n, _c, _d in [("XA%d" % _i, ND * XB, "bfloat16") for _i in range(RO)] + [("WS", 2, "float32"), ("WL", 2 * ND, "float32")]:
+    SCRATCH[_n] = ("sbuf", [128, _c], _d)
+    HOME[_n] = (_n, 0)
+SENDS = ["WL"] + ["XA%d" % _i for _i in range(RO)]
+SEMAPHORES = ["qV", "qS", "qP", "qG", "dX0", "dX1", "dW", "dT", "dY"] + [a + n for n in SENDS for a in ("in", "out")]
 
 
 def rank_program(g, core, T, topo):
@@ -195,6 +196,23 @@ def rank_program(g, core, T, topo):
     def half(name, b):
         return A(name, 1024 * b, 1024 * b + 1024)
 
+    def send(src, dst, w):
+        sync("G", [], A(src, 0, w)[1])
+        tr, used = [], [0, 0]
+        for d in range(1, NR):
+            to = T.cores[(rank - d) % NR]
+            rid, pid, _ = topo.addr(to)
+            near = int(topo.die(to) == topo.die(core))
+            mask = 0
+            for e in topo.engines(core, to)[near::2][used[near]:used[near] + ENG]:
+                mask |= 1 << e
+            used[near] += ENG
+            tr.append(RemoteDMATransfer(dst_ids=[DstId(rid=rid, pnc=pid)], dma_engine_mask=mask, remote_sem=T.sem["in" + dst],
+                                        src=A(src, 0, w)[0], dst=A(dst, w * (d - 1), w * d)[0]))
+        g.remote_dma_fused(tr, local_sem=T.sem["out" + dst])
+        event("in" + dst, ENG * ND, [A(dst)], [], {})
+        event("out" + dst, ENG * ND, [], [A(src, 0, w)], known["G"])
+
     BO = A("B144", 0, 128)
     L16 = A("M16", 0, 128, parts=16)
     Id = A("Id")
@@ -226,16 +244,18 @@ def rank_program(g, core, T, topo):
                 fill(A(name), 0.0)
         if j == 2:
             fill(A("XS", W, W + 16), 512.0)
-            fill(A("c75"), 7.5)
+            fill(A("c85"), 8.5)
         if j == 3:
             ts(A("WZ"), A("Z"), A("wtb"), Op.mult)
             cp(A("t1f"), A("thi", 0, 1))
         if j == 4:
-            ts(A("t2f"), A("thi", 1, 2), 32.0, Op.mult)
+            ts(A("WS", 1, 2), A("thi", 1, 2), 32.0, Op.mult)
+            cp(A("WS", 0, 1), A("wtb"))
+            send("WS", "WL", 2)
     act(A("NId"), Id, scale=-1.0)
     act(A("Zn"), A("Z"), scale=-1.0)
     act(A("Z32"), A("Z"), scale=32.0)
-    act(A("BO4"), BO, scale=1.0 / 1024)
+    act(A("BO4"), BO, scale=4.0)
     act(A("Lh", parts=16), L16, scale=0.5)
 
     def constants_G():
@@ -257,14 +277,17 @@ def rank_program(g, core, T, topo):
         iota(A("N112"), [[1, NS]], 0, 0)
         iota(A("MB"), [[2, 16], [0, ND]], 0, 0)
         iota(A("MT"), [[2, 16], [0, ND]], 1, 0)
+        iota(A("MO"), [[0, 8], [XB, ND]], 0, 0)
         iota(A("ITa"), [[0, 8], [1, 16]], 1, 0)
-        iota(A("R16h", 0, 129), [[16, 129]], -8, 0)
+        iota(A("R16h", 0, 129), [[16, 129]], 8, 0)
 
     def constants_late():
         act(A("R2"), A("R1"), scale=2.0)
-        act(A("TriI4"), A("TriI"), scale=1.0 / 1024)
+        act(A("TriI4"), A("TriI"), scale=4.0)
+        for d in range(ND):
+            act(A("WB", 128 * d, 128 * d + 128), BO, scale=A("WL", 2 * d, 2 * d + 1))
         act(A("S2"), A("PP", 0, 16), scale=2.0, bias=2048.0)
-        act(A("D4n", 0, ND), A("PP", 0, ND), scale=4.0, bias=DUMP - 7.5)
+        act(A("D4n", 0, ND), A("PP", 0, ND), scale=4.0, bias=DUMP + 8.5)
         ts(A("CH", 15, 256, 16), A("PP", 0, 16), 8.0, Op.mult, -1025.0, Op.add)
         ts(A("AV"), A("WM", 15, 15 + NS), BIG, Op.mult, 1.0, Op.max)
         ts(A("SC"), A("WM", 15, 16), 1.0, Op.mult, 1.0 / BIG, Op.max)
@@ -273,20 +296,6 @@ def rank_program(g, core, T, topo):
         tt(A("AW"), A("AV"), A("WM", 0, NS), Op.subtract)
         ts(A("IT"), A("O16"), 8.5, Op.subtract)
         tt(A("IU"), A("O16"), A("O17"), Op.add)
-
-    def exchange(src, dst, w, ls, rs, back):
-        sync("G", [], A(src)[1])
-        tr = []
-        for d in range(1, NR):
-            to = T.cores[(rank - d) % NR if back else (rank + d) % NR]
-            rid, pid, _ = topo.addr(to)
-            mask = 0
-            for e in topo.engines(core, to)[ENG * (d - 1):ENG * d]:
-                mask |= 1 << e
-            tr.append(RemoteDMATransfer(dst_ids=[DstId(rid=rid, pnc=pid)], dma_engine_mask=mask, remote_sem=T.sem[rs],
-                                        src=A(src, w * (d - 1), w * d)[0], dst=A(dst, w * (d - 1), w * d)[0]))
-        g.remote_dma_fused(tr, local_sem=T.sem[ls])
-        event(rs, ENG * ND, [A(dst, 0, w * ND)], [], {})
 
     def successors(rnd):
         X = "X%d" % rnd
@@ -321,7 +330,7 @@ def rank_program(g, core, T, topo):
             cp(lk("OF", b, m0, m1), lk("OI", b, m0, m1))
 
         def part(name, m, b, lo, hi, first=0, st=1):
-            return A(name % m, 1024 * b + 16 * lo + first, 1024 * b + 16 * hi, st)
+            return A(name % m, 16 * lo + first, 16 * hi, st)
 
         def sums(m, b, sides, lo=0, hi=64):
             for n, (z, name) in enumerate(sides):
@@ -343,14 +352,14 @@ def rank_program(g, core, T, topo):
         banks = {}
 
         def take(m, b):
-            act(half("D%d_" % m, b), I(win, lk("OF", b, m)))
+            act(A("D%d_" % m), I(win, lk("OF", b, m)))
             banks[(m, b)] = 3 + 2 * (len(banks) % 2)
 
         def under(m, b):
             for x in range(2):
                 o, c = A("p%d" % (banks[(m, b)] + x)), 1024 * b + 512 * x
                 mm(o, A("NId"), A(X, c, c + 512), True, False)
-                mm(o, Id, A("D%d_" % m, c, c + 512), False, True)
+                mm(o, Id, A("D%d_" % m, 512 * x, 512 * x + 512), False, True)
 
         def finish(m, b):
             for x in range(2):
@@ -392,6 +401,8 @@ def rank_program(g, core, T, topo):
             if b == 0:
                 act(half("XC", 0), half(X, 0))
                 cp(hw("vI", 0), hw("p0", 0))
+        sel(A(X, W, XB), A(X, 0, XB - W), [[0, XB - W]], Op.is_ge, 0, 0)
+        send(X, "XA%d" % rnd, XB)
         sel(half("XC", 1), half(X, 1), [[0, 1024]], Op.is_ge, 0, 0)
         if rnd == 0:
             constants_G()
@@ -440,7 +451,6 @@ def rank_program(g, core, T, topo):
         TAG[0] = "table"
         free = 3 + 2 * (len(banks) % 2)
         last = ("p%d" % free, "p%d" % (free + 1))
-        act(A(X, W, W + 8), A(X, 0, 8))
         spread(1, last, list(range(8, 16)) + list(range(8)))
         for t in range(8):
             mm(A("p2", 0, 16), A("Pk", 14 - 2 * t, 142 - 2 * t), A("TF", 9 * t + 8, 1152, 72), t == 0, t == 7)
@@ -453,8 +463,7 @@ def rank_program(g, core, T, topo):
 
     def one_round(rnd):
         X, XN = "X%d" % rnd, "X%d" % (rnd + 1)
-        AL, AS, YL, YS, FL, FS = ("%s%d" % (n, rnd) for n in ("AL", "AS", "YL", "YS", "FL", "FS"))
-        win = A(X, 0, W + 8)
+        win, theirs = A(X, 0, XB), A("XA%d" % rnd)
         successors(rnd)
 
         TAG[0] = "runs"
@@ -528,21 +537,21 @@ def rank_program(g, core, T, topo):
         tt(A("PR"), I(A("KT", 16, 528), A("kl", 0, ND)), A("PD"), Op.add)
         scan(A("PW"), A("AW"), A("PR"))
         ts(A("sl", 0, ND), A("PW", 15, NS, 16), A("SC"), Op.mult, float(NONE), Op.min)
-        cp(A(AS), I(A("XS"), A("sl", 0, ND)))
-        exchange(AS, AL, 16, "la%d" % rnd, "ask%d" % rnd, False)
+        cp(A("A4", 0, NS), I(A("XS"), A("sl", 0, ND)))
         ts(A("P3", 0, ND), A("sl", 0, ND), 3.0, Op.subtract)
 
         TAG[0] = "answers"
         keys = (("p1", 0, 8), ("p2", 8, 12), ("p4", 12, 16))
         for p, m0, m1 in keys:
             mm(A(p, 0, ND * (m1 - m0)), Id, A("MB", ND * m0, ND * m1), True, False)
-        for i in range(16):
-            mm(A("p0", 0, ND), Z("WZ", i), A(AL, i, NS, 16), i == 0, i == 15)
+        for d in range(ND):
+            mm(A("p0", 16 * d, 16 * d + 16), A("WB", 128 * d, 128 * d + 128), A("A4", 16 * d, 16 * d + 16))
         for b in range(1, 4):
-            cp(A(AL, NS * b, NS * b + NS), A(AL, 0, NS))
-        mm(A("p3", 0, 448), A("NId"), A(AL), True, False)
+            cp(A("A4", NS * b, NS * b + NS), A("A4", 0, NS))
+        mm(A("p3", 0, 448), A("NId"), A("A4"), True, False)
+        scan(A("HW"), A("AW"), A("p0", 0, NS))
         for a in range(4):
-            cp(A("aI", ND * a, ND * a + ND), A("p0", 0, ND))
+            ts(A("aI", ND * a, ND * a + ND), A("HW", 15, NS, 16), A("SC"), Op.mult)
         ts(A("H4"), A("aI"), 5, Op.logical_shift_right, 63, Op.bitwise_and)
         ts(A("U4"), A("aI"), 2047, Op.bitwise_and)
         for a in range(4):
@@ -552,7 +561,9 @@ def rank_program(g, core, T, topo):
         for a in range(2):
             ts(A("C16", 56 * a, 56 * a + 56), A("Q16", 56 * a, 56 * a + 56), 2047, Op.bitwise_and)
         for a in range(2):
-            cp(A("OA", 56 * a, 56 * a + 56), A("C16", 56 * a, 56 * a + 56))
+            tt(A("O16A", 56 * a, 56 * a + 56), A("C16", 56 * a, 56 * a + 56), A("MO"), Op.add)
+        for a in range(2):
+            cp(A("OA", 56 * a, 56 * a + 56), A("O16A", 56 * a, 56 * a + 56))
 
         def quarter(b):
             return A("DA", 448 * b, 448 * b + 448)
@@ -562,10 +573,10 @@ def rank_program(g, core, T, topo):
             for i in range(16):
                 mm(A(p, 0, ND * (m1 - m0)), Z("Z32", i), A("DA", NS * m0 + i, NS * m1, 16), False, i == 15)
 
-        act(A("GA"), I(win, A("OA", 0, 28)))
+        act(A("GA"), I(theirs, A("OA", 0, 28)))
         mm(A("p3", 0, 448), Id, A("GA"), False, True)
         for b in range(1, 4):
-            tt(quarter(b), I(win, A("OA", 28 * b, 28 * b + 28)), A(AL), Op.subtract)
+            tt(quarter(b), I(theirs, A("OA", 28 * b, 28 * b + 28)), A("A4"), Op.subtract)
             act(quarter(b), quarter(b), AF.Abs)
             if b == 1:
                 act(quarter(0), A("p3", 0, 448), AF.Abs)
@@ -576,16 +587,12 @@ def rank_program(g, core, T, topo):
         tt(A("k4"), A("p4", 0, 28), A("k3"), Op.min)
         tt(A("k5", 0, 14), A("k4", 0, 14), A("k4", 14, 28), Op.min)
         tt(A("bi", 0, ND), A("k5", 0, ND), A("k5", ND, 14), Op.min)
-        ts(A(YS), A("bi", 0, ND), A("t2f"), Op.is_lt, 4096.0, Op.mult)
-        exchange(YS, YL, 1, "ly%d" % rnd, "yes%d" % rnd, True)
+        tt(A("yes", 0, ND), A("bi", 0, ND), A("WL", 1, 2 * ND, 2), Op.is_lt)
+        tt(A("no", 0, ND), A("bi", 0, ND), A("WL", 1, 2 * ND, 2), Op.is_ge)
         ts(A("bm", 0, ND), A("bi", 0, ND), 31, Op.bitwise_and)
+        tt(A("zd", 0, ND), A("no", 0, ND), A("D4n", 0, ND), Op.mult)
         tt(A("b3", 0, ND), A("bm", 0, ND), A("K16", 0, ND), Op.add)
         tt(A("b4", 0, ND), A("b3", 0, ND), A("U4", 0, ND), Op.mult)
-        ts(A("b5", 0, ND), A("b4", 0, ND), 2047, Op.bitwise_and)
-        for f in range(F):
-            ts(A("OL", f, F * ND, F), A("b5", 0, ND), float(1 + f), Op.add)
-        cp(A(FS), I(win, A("OL", 0, F * ND)))
-        exchange(FS, FL, 16 * F, "lb%d" % rnd, "ans%d" % rnd, True)
 
         TAG[0] = "next"
         CN = [A("p5", 0, 64), A("p6", 0, 64)]
@@ -593,15 +600,15 @@ def rank_program(g, core, T, topo):
             mm(CN[b], A("Lh", parts=16), A("R16c", 64 * b, 64 * b + 64, parts=16), True, False)
             mm(CN[b], A("Lh", parts=16), A("Rs", 0, 64, parts=16), False, False)
         mm(A("p0", 0, ND), Id, A("P3", 0, ND), True, False)
-        mm(A("p0", 0, ND), A("NId"), A("c75", 0, ND), False, False)
-        mm(A("p0", 0, ND), A("TriI4"), A(YL), False, False)
+        mm(A("p0", 0, ND), Id, A("c85", 0, ND), False, False)
+        mm(A("p0", 0, ND), A("TriI4"), A("yes", 0, ND), False, False)
         for s in range(1, ND):
-            mm(A("p0", s, ND), A("BO4"), A(YL, 0, ND - s), False, s == ND - 1)
-        tt(A("zd", 0, ND), A("D4n", 0, ND), A(YL), Op.subtract)
+            mm(A("p0", s, ND), A("BO4"), A("yes", 0, ND - s), False, s == ND - 1)
         tt(A("Af", 0, ND), A("p0", 0, ND), A("zd", 0, ND), Op.max)
+        ts(A("b5", 0, ND), A("b4", 0, ND), 2047, Op.bitwise_and)
         ts(A("Ah", 0, ND), A("Af", 0, ND), ROUND16, Op.add, ROUND16, Op.subtract)
-        for f in range(2):
-            ts(A("SL", f, F * ND, F), A("Af", 0, ND), f + 7.5, Op.add)
+        tt(A("b6", 0, ND), A("b5", 0, ND), A("MO", 0, ND), Op.add)
+        ts(A("SL", 0, F * ND, F), A("Af", 0, ND), -8.5, Op.add)
         for d in range(ND):
             ld, le = (A(n, 128 * d, 128 * d + 128) for n in ("LD", "LE"))
             act(A("RG", 144 * d, 144 * d + 129), A("R16h", 0, 129), AF.Sign, scale=-1.0, bias=A("Af", d, d + 1))
@@ -611,13 +618,16 @@ def rank_program(g, core, T, topo):
                 o = 144 * d + 64 * b
                 mm(CN[b], ld, A("RG", o + 1, o + 65), False, False)
                 mm(CN[b], le, A("RG", o, o + 64), False, d == ND - 1)
-        for f in range(2, F):
-            ts(A("SL", f, F * ND, F), A("Af", 0, ND), f + 7.5, Op.add)
+        for f in range(F):
+            ts(A("OL", f, F * ND, F), A("b6", 0, ND), float(1 + f), Op.add)
+        for f in range(1, F):
+            ts(A("SL", f, F * ND, F), A("Af", 0, ND), f - 8.5, Op.add)
         ts(A("SR", 64, 128), CN[1], 2.0, Op.mult)
         ts(A("SR", 0, 64), CN[0], 2.0, Op.mult)
+        act(A("FL"), I(theirs, A("OL", 0, F * ND)))
         act(A(XN, 16 * CUT, W), I(A("XS"), A("SR", CUT, 128)))
         cp(A(XN, 0, 16 * CUT), I(A("XS"), A("SR", 0, CUT)))
-        cp(I(A(XN), A("SL", 0, F * ND)), A(FL))
+        cp(I(A(XN), A("SL", 0, F * ND)), A("FL"))
 
     for rnd in range(RO):
         one_round(rnd)
@@ -630,6 +640,6 @@ def rank_program(g, core, T, topo):
         g.wait_ge(T.sem[s], 16)
     for q in ("V", "S", "P", "G"):
         g.wait_ge(T.sem["q" + q], done[q])
-    for rnd in range(RO):
-        for n in EXCHANGES:
-            g.wait_ge(T.sem["%s%d" % (n, rnd)], ENG * ND)
+    for n in SENDS[:RO + 1]:
+        for a in ("in", "out"):
+            g.wait_ge(T.sem[a + n], ENG * ND)

from concourse.bass import DstId, RemoteDMATransfer
from concourse.mybir import AluOpType as Op, ActivationFunctionType as AF

NR, W, F, RO = 8, 2048, 4, 2
ND = NR - 1
NS = ND * 16
XW = 3072
XB = W + 8
NONE = 2056
DUMP = 2560
BIG = 2.0 ** 31
ENG = 2
CUT = 70
ROUND16 = 1.5 * 2.0 ** 27
ORDER = ("t70 A t50 u70 g40 B u50 f70 r40 t30 g20 u30 g60 C f50 D s20 f30 r60 E F t71 g00 u71 g61 g10 s00 r61 g41 t51 s10 u51 G H f71 t31 u31 "
         "r41 f51 I t11 g21 J u11 K g01a s21 g01b f31 L M P N f11 s01a s01b O")
TAG = [""]

SB = {
    "X0": (XW, "bfloat16"), "X1": (XW, "bfloat16"), "X2": (XW, "bfloat16"), "XC": (2048, "bfloat16"), "wtb": (1, "bfloat16"), "thi": (2, "int32"),
    "t1f": (1, "float32"), "ones": (2048, "bfloat16"),
    "B144": (144, "bfloat16"), "Z": (144, "bfloat16"), "WZ": (144, "bfloat16"), "Zn": (144, "bfloat16"),
    "Z32": (144, "bfloat16"), "Pk": (144, "bfloat16"), "BO4": (128, "bfloat16"), "TriS": (128, "bfloat16"), "TriI": (128, "bfloat16"),
    "TriI4": (128, "bfloat16"), "Id": (128, "bfloat16"), "NId": (128, "bfloat16"), "EZ": (2048, "bfloat16"),
    "M16": (272, "bfloat16"), "R16c": (128, "bfloat16"), "Rk": (128, "bfloat16"), "Rs": (128, "bfloat16"), "R64": (256, "bfloat16"),
    "R16h": (144, "float32"), "WM": (272, "bfloat16"), "AV": (112, "bfloat16"), "AW": (112, "bfloat16"), "SC": (1, "float32"),
    "PP": (128, "float32"), "S2": (16, "float32"), "D4n": (8, "float32"), "RSW": (128, "bfloat16"), "R1": (96, "bfloat16"), "R2": (96, "bfloat16"),
    "N112": (112, "float32"), "MB": (112, "bfloat16"), "MT": (112, "int32"), "IT": (128, "bfloat16"), "IU": (128, "bfloat16"), "ITa": (128, "bfloat16"),
    "O16": (128, "float32"), "O17": (128, "float32"), "KM": (512, "bfloat16"), "KT": (528, "bfloat16"),
    "vI": (128, "int32"), "u": (128, "int32"), "h": (128, "int32"), "hb": (128, "bfloat16"), "KK": (1024, "float32"),
    "QI": (1024, "int32"), "OI": (1024, "int32"), "OF": (1024, "uint16"),
    "E": (1152, "bfloat16"), "DL": (1152, "float16"), "TF": (1152, "float16"), "x1": (8, "float32"), "x2": (8, "float32"), "T6": (8, "float32"),
    "NX": (2064, "float32"), "GM": (2048, "float16"), "CH": (2048, "float16"), "LS": (128, "uint16"),
    "SM": (32, "float32"), "XS": (2064, "bfloat16"), "D1": (96, "bfloat16"),
    "CT": (96, "bfloat16"), "CQ": (96, "bfloat16"), "TX": (32, "bfloat16"), "FX": (32, "bfloat16"), "zz": (16, "float32"), "Wz": (16, "float32"),
    "f6": (16, "bfloat16"), "n6": (16, "float32"), "zs": (16, "float16"), "pl": (16, "uint16"), "VAL": (256, "float32"), "SW": (4352, "float32"),
    "Y": (112, "float32"), "YW": (112, "float32"), "VI": (112, "int32"), "PL": (112, "int32"), "dead": (112, "float32"), "PD": (112, "float32"),
    "wi": (8, "int32"), "wq": (8, "int32"), "kl": (8, "uint16"), "PR": (112, "float32"), "PW": (112, "float32"), "sl": (8, "uint16"), "P3": (8, "float16"),
    "aI": (28, "int32"), "U4": (28, "int32"), "H4": (28, "int32"), "K16": (112, "int32"), "Q16": (112, "int32"), "C16": (112, "int32"),
    "O16A": (112, "int32"), "MO": (56, "int32"), "WB": (896, "bfloat16"), "HW": (112, "float32"), "A4": (448, "bfloat16"), "FL": (448, "bfloat16"),
    "yes": (8, "bfloat16"), "no": (8, "float32"), "b6": (8, "int32"), "OA": (112, "uint16"), "GA": (448, "bfloat16"), "DA": (1792, "bfloat16"),
    "k1": (28, "float32"), "k2": (28, "float32"), "k3": (28, "float32"), "k4": (28, "float32"), "k5": (16, "float32"),
    "bi": (8, "int32"), "bm": (8, "int32"), "b3": (8, "int32"), "b4": (8, "int32"), "b5": (8, "int32"), "OL": (32, "uint16"),
    "zd": (8, "float32"), "Af": (8, "float32"), "Ah": (8, "float32"), "c85": (8, "bfloat16"), "Lh": (128, "bfloat16"),
    "SL": (32, "uint16"), "LD": (896, "bfloat16"), "LE": (896, "bfloat16"), "RG": (1008, "bfloat16"), "SR": (128, "uint16"),
}
HOME = {}


def _pack():
    homes, n = {}, {}
    for k, (c, d) in SB.items():
        if c > 448 or k in ("wtb", "thi"):
            homes[k] = (c, d)
            HOME[k] = (k, 0)
        else:
            h = "pool_" + d
            o = n.get(h, 0)
            HOME[k] = (h, o)
            n[h] = o + (c + 15) // 16 * 16
            homes[h] = (n[h], d)
    return homes


SCRATCH = {k: ("sbuf", [128, c], d) for k, (c, d) in _pack().items()}
for _i in range(8):
    for _n in ("D%d_", "R%d_"):
        SCRATCH[_n % _i] = ("sbuf", [128, 1024], "bfloat16")
        HOME[_n % _i] = (_n % _i, 0)
    SCRATCH["p%d" % _i] = ("psum", [128, 512], "float32")
    HOME["p%d" % _i] = ("p%d" % _i, 0)
for _n, _c, _d in [("XA%d" % _i, ND * XB, "bfloat16") for _i in range(RO)] + [("WS", 2, "float32"), ("WL", 2 * ND, "float32")]:
    SCRATCH[_n] = ("sbuf", [128, _c], _d)
    HOME[_n] = (_n, 0)
SENDS = ["WL"] + ["XA%d" % _i for _i in range(RO)]
SEMAPHORES = ["qV", "qS", "qP", "qG", "dX0", "dX1", "dW", "dT", "dY"] + [a + n for n in SENDS for a in ("in", "out")]


def rank_program(g, core, T, topo):
    rank = T.rank_of(core)
    if rank is None:
        return
    queues = {"V": g.vector, "S": g.scalar, "P": g.tensor, "G": g, "Y": g.sync}
    done = {q: 0 for q in queues}
    known = {q: {} for q in queues}
    clocks, log = {}, {}

    def A(name, lo=0, hi=None, st=1, parts=128):
        home, o = HOME[name]
        if hi is None:
            hi = SB[name][0] if name in SB else SCRATCH[name][1][1]
        ap = T[home][0:parts, o + lo:o + hi] if st == 1 else T[home][0:parts, o + lo:o + hi:st]
        return (ap, [(home, o + lo, o + hi, st)])

    def I(win, off):
        return (win[0].indirect(off[0]), win[1] + off[1])

    def apart(lo, hi, st, lo2, hi2, st2):
        s = min(st, st2)
        return lo >= hi2 or lo2 >= hi or (s > 1 and st % s == 0 and st2 % s == 0 and (lo - lo2) % s != 0)

    def sync(q, outs, ins):
        need = {}
        for w, regs in ((True, outs), (False, ins)):
            for (n, lo, hi, st) in regs:
                bank = n[0] == "p" and n[1].isdigit()
                for (q2, i2, lo2, hi2, st2, w2) in log.get(n, ()):
                    if bank and q2 != q:
                        hit = True
                    elif q2 == q and q == "P":
                        hit = False
                    else:
                        hit = (w or w2) and not apart(lo, hi, st, lo2, hi2, st2)
                    if hit:
                        need[q2] = max(need.get(q2, 0), i2)
        k = known[q]
        for q2, i2 in sorted(need.items(), key=lambda t: -sum(clocks[t].values())):
            if k.get(q2, 0) >= i2:
                continue
            queues[q].wait_ge(T.sem[q2 if q2 not in queues else "q" + q2], i2)
            for a, b in clocks[(q2, i2)].items():
                k[a] = max(k.get(a, 0), b)

    def note(q, i, outs, ins):
        for w, regs in ((True, outs), (False, ins)):
            for (n, lo, hi, st) in regs:
                def inside(e):
                    return lo <= e[2] and e[3] <= hi and (st == 1 or (e[4] == st and (e[2] - lo) % st == 0))
                l = log.setdefault(n, [])
                if w:
                    l[:] = [e for e in l if not (inside(e) and e[1] <= clocks[(q, i)].get(e[0], 0))]
                l[:] = [e for e in l if not (e[0] == q and e[5] == w and inside(e))]
                l.append((q, i, lo, hi, st, w))

    def do(q, call, outs, ins):
        o = [r for x in outs for r in x[1]]
        n = [r for x in ins for r in x[1]]
        sync(q, o, n)
        done[q] += 1
        call().then_inc(T.sem["q" + q], 1)
        c = dict(known[q])
        c[q] = done[q]
        clocks[(q, done[q])] = c
        note(q, done[q], o, n)

    def event(sem, val, outs, ins, base):
        c = dict(base)
        c[sem] = val
        clocks[(sem, val)] = c
        note(sem, val, [r for x in outs for r in x[1]], [r for x in ins for r in x[1]])

    def load(q, sem, out, src):
        queues[q].dma_start(out[0], src).then_inc(T.sem[sem], 16)
        event(sem, 16, [out], [], known[q])

    def cp(out, in_):
        do("V", lambda: g.vector.tensor_copy(out[0], in_[0]), [out], [in_])

    def tt(out, a, b, op):
        do("V", lambda: g.vector.tensor_tensor(out[0], a[0], b[0], op), [out], [a, b])

    def ts(out, a, s1, op0, s2=None, op1=None):
        ins = [a] + [x for x in (s1, s2) if isinstance(x, tuple)]
        x1, x2 = (x[0] if isinstance(x, tuple) else x for x in (s1, s2))
        if op1 is None:
            do("V", lambda: g.vector.tensor_scalar(out[0], a[0], x1, None, op0), [out], ins)
        else:
            do("V", lambda: g.vector.tensor_scalar(out[0], a[0], x1, x2, op0, op1), [out], ins)

    def scan(out, a, b, op0=Op.mult, op1=Op.add, initial=0.0):
        do("V", lambda: g.vector.tensor_tensor_scan(out[0], a[0], b[0], initial, op0, op1), [out], [a, b])

    def fill(out, c):
        do("V", lambda: g.vector.memset(out[0], c), [out], [])

    def act(out, in_, f=AF.Copy, **kw):
        ins = [in_] + [x for x in kw.values() if isinstance(x, tuple)]
        k2 = {a: x[0] if isinstance(x, tuple) else x for a, x in kw.items()}
        do("S", lambda: g.scalar.activation(out[0], in_[0], f, **k2), [out], ins)

    def mm(out, l, r, start=True, stop=True):
        do("P", lambda: g.tensor.matmul(out[0], l[0], r[0], start, stop), [out], [l, r])

    def sel(out, in_, pat, op, base, cm):
        do("G", lambda: g.affine_select(out[0], in_[0], pat, op, 0.0, base, cm), [out], [in_])

    def iota(out, pat, base, cm):
        do("G", lambda: g.iota(out[0], pat, base, cm, allow_small_or_imprecise_dtypes=True), [out], [])

    def Z(name, i):
        return A(name, 15 - i, 143 - i)

    def EZ(i):
        return A("EZ", 128 * i, 128 * i + 128)

    def half(name, b):
        return A(name, 1024 * b, 1024 * b + 1024)

    def send(src, dst, w):
        sync("G", [], A(src, 0, w)[1])
        tr, used = [], [0, 0]
        for d in range(1, NR):
            to = T.cores[(rank - d) % NR]
            rid, pid, _ = topo.addr(to)
            near = int(topo.die(to) == topo.die(core))
            mask = 0
            for e in topo.engines(core, to)[near::2][used[near]:used[near] + ENG]:
                mask |= 1 << e
            used[near] += ENG
            tr.append(RemoteDMATransfer(dst_ids=[DstId(rid=rid, pnc=pid)], dma_engine_mask=mask, remote_sem=T.sem["in" + dst],
                                        src=A(src, 0, w)[0], dst=A(dst, w * (d - 1), w * d)[0]))
        g.remote_dma_fused(tr, local_sem=T.sem["out" + dst])
        event("in" + dst, ENG * ND, [A(dst)], [], {})
        event("out" + dst, ENG * ND, [], [A(src, 0, w)], known["G"])

    BO = A("B144", 0, 128)
    L16 = A("M16", 0, 128, parts=16)
    Id = A("Id")

    for b in range(2):
        load("Y", "dX%d" % b, half("X0", b), T.x0[:, 1024 * b:1024 * b + 1024])
    load("S", "dW", A("wtb"), T.wt[:])
    load("S", "dT", A("thi"), T.th[:])
    fill(A("ones", 0, 272), 1.0)
    sel(A("B144"), A("ones", 0, 144), [[-16, 9], [0, 16]], Op.is_ge, 0, 1)
    sel(A("B144"), A("B144"), [[16, 9], [0, 16]], Op.is_ge, 15, -1)
    sel(A("Z"), A("B144"), [[0, 9], [1, 16]], Op.is_equal, -15, 0)
    sel(Id, A("ones", 0, 128), [[-1, 128]], Op.is_equal, 0, 1)
    sel(A("M16", parts=16), A("ones", 0, 272, parts=16), [[0, 17], [1, 16]], Op.is_equal, 0, -1)
    iota(A("R16c", parts=16), [[16, 128]], 0, 0)
    iota(A("Rk", parts=16), [[0, 128]], 0, 1)
    fill(A("KM"), 7.0)
    fill(A("KT", 0, 24), 6.0)
    for j in range(6):
        fill(A("KM", 8 << j, 16 << j, 8), 5.0 - j)
    for j in range(6):
        n = 8 << j
        tt(A("KT", 16 + n, 16 + 2 * n), A("KT", 15, 15 + n), A("KM", n, 2 * n), Op.min)
        if j == 0:
            fill(A("ones", 272, 2048), 1.0)
        if j == 1:
            fill(A("E", 0, 1152, 9), 0.0)
            for name in ("TX", "FX"):
                fill(A(name), 0.0)
        if j == 2:
            fill(A("XS", W, W + 16), 512.0)
            fill(A("c85"), 8.5)
        if j == 3:
            ts(A("WZ"), A("Z"), A("wtb"), Op.mult)
            cp(A("t1f"), A("thi", 0, 1))
        if j == 4:
            ts(A("WS", 1, 2), A("thi", 1, 2), 32.0, Op.mult)
            cp(A("WS", 0, 1), A("wtb"))
            send("WS", "WL", 2)
    act(A("NId"), Id, scale=-1.0)
    act(A("Zn"), A("Z"), scale=-1.0)
    act(A("Z32"), A("Z"), scale=32.0)
    act(A("BO4"), BO, scale=4.0)
    act(A("Lh", parts=16), L16, scale=0.5)

    def constants_G():
        mm(A("p3", 0, 272), L16, A("M16", parts=16))
        mm(A("p4", 0, 128), L16, A("R16c", parts=16), True, False)
        mm(A("p4", 0, 128), L16, A("Rk", parts=16), False, True)
        act(A("WM"), A("p3", 0, 272))
        act(A("PP"), A("p4", 0, 128))
        sel(A("EZ"), A("ones"), [[-1, 16], [-16, 8], [0, 16]], Op.is_equal, 0, 1)
        iota(A("T6"), [[1, 8]], -1024, 0)
        sel(A("Pk"), A("ones", 0, 144), [[-16, 9], [-8, 16]], Op.is_equal, 112, 1)
        sel(A("Pk"), A("Pk"), [[0, 9], [1, 16]], Op.is_ge, -14, 0)
        sel(A("RSW"), A("ones", 0, 128), [[0, 8], [1, 16]], Op.is_gt, 0, 0)
        sel(A("R1"), A("ones", 0, 96), [[0, 16], [1, 6]], Op.is_gt, 0, 0)
        sel(A("TriS"), BO, [[1, 128]], Op.is_gt, 0, -1)
        sel(A("TriI"), BO, [[1, 128]], Op.is_ge, 0, -1)
        iota(A("R64", parts=16), [[64, 256]], 0, 0)
        iota(A("Rs", parts=16), [[0, 128]], -2 * NS, 1)
        iota(A("N112"), [[1, NS]], 0, 0)
        iota(A("MB"), [[2, 16], [0, ND]], 0, 0)
        iota(A("MT"), [[2, 16], [0, ND]], 1, 0)
        iota(A("MO"), [[0, 8], [XB, ND]], 0, 0)
        iota(A("ITa"), [[0, 8], [1, 16]], 1, 0)
        iota(A("R16h", 0, 129), [[16, 129]], 8, 0)

    def constants_late():
        act(A("R2"), A("R1"), scale=2.0)
        act(A("TriI4"), A("TriI"), scale=4.0)
        for d in range(ND):
            act(A("WB", 128 * d, 128 * d + 128), BO, scale=A("WL", 2 * d, 2 * d + 1))
        act(A("S2"), A("PP", 0, 16), scale=2.0, bias=2048.0)
        act(A("D4n", 0, ND), A("PP", 0, ND), scale=4.0, bias=DUMP + 8.5)
        ts(A("CH", 15, 256, 16), A("PP", 0, 16), 8.0, Op.mult, -1025.0, Op.add)
        ts(A("AV"), A("WM", 15, 15 + NS), BIG, Op.mult, 1.0, Op.max)
        ts(A("SC"), A("WM", 15, 16), 1.0, Op.mult, 1.0 / BIG, Op.max)
        tt(A("O16"), A("ITa"), BO, Op.mult)
        ts(A("O17"), BO, -108.5, Op.mult, 100.0, Op.add)
        tt(A("AW"), A("AV"), A("WM", 0, NS), Op.subtract)
        ts(A("IT"), A("O16"), 8.5, Op.subtract)
        tt(A("IU"), A("O16"), A("O17"), Op.add)

    def successors(rnd):
        X = "X%d" % rnd
        win = A(X, 0, W)

        def hw(name, b):
            return A(name, 64 * b, 64 * b + 64)

        def lk(name, b, m0, m1=None):
            return A(name, 512 * b + 64 * m0, 512 * b + 64 * (m0 + 1 if m1 is None else m1))

        def pd(m, b, lo=0, hi=64):
            bank, o = ("p1", 64 * m) if b == 0 else ("p2", 64 * m) if m > 1 else ("p0", 128) if m else ("p1", 0)
            return A(bank, o + lo, o + hi)

        def split(b):
            ts(hw("u", b), hw("vI", b), 2047, Op.bitwise_and)
            ts(hw("h", b), hw("vI", b), 5, Op.logical_shift_right, 63, Op.bitwise_and)

        def plus(b, ms):
            for m in ms:
                act(lk("KK", b, m), hw("hb", b), bias=float(2 * m + 1))

        def times(b, ms):
            for m in ms:
                tt(lk("QI", b, m), lk("KK", b, m), hw("p7", b), Op.mult)

        def mod(b, m0, m1):
            ts(lk("OI", b, m0, m1), lk("QI", b, m0, m1), 2047, Op.bitwise_and)

        def offsets(b, m0, m1):
            cp(lk("OF", b, m0, m1), lk("OI", b, m0, m1))

        def part(name, m, b, lo, hi, first=0, st=1):
            return A(name % m, 16 * lo + first, 16 * hi, st)

        def sums(m, b, sides, lo=0, hi=64):
            for n, (z, name) in enumerate(sides):
                for i in range(16):
                    mm(pd(m, b, lo, hi), Z(z, i), part(name, m, b, lo, hi, i, 16), n == 0 and i == 0, n == len(sides) - 1 and i == 15)

        def gather(m, b, lo=0, hi=64):
            o = 512 * b + 64 * m
            tt(part("D%d_", m, b, lo, hi), I(win, A("OF", o + lo, o + hi)), A("XC", 1024 * b + 16 * lo, 1024 * b + 16 * hi), Op.subtract)

        def relu(m, b, lo=0, hi=64):
            ts(part("R%d_", m, b, lo, hi), part("D%d_", m, b, lo, hi), 0.0, Op.max, 2.0, Op.mult)
            sums(m, b, (("Zn", "D%d_"), ("Z", "R%d_")), lo, hi)

        def size(m, b, lo=0, hi=64):
            act(part("R%d_", m, b, lo, hi), part("D%d_", m, b, lo, hi), AF.Abs)
            sums(m, b, (("Z", "R%d_"),), lo, hi)

        banks = {}

        def take(m, b):
            act(A("D%d_" % m), I(win, lk("OF", b, m)))
            banks[(m, b)] = 3 + 2 * (len(banks) % 2)

        def under(m, b):
            for x in range(2):
                o, c = A("p%d" % (banks[(m, b)] + x)), 1024 * b + 512 * x
                mm(o, A("NId"), A(X, c, c + 512), True, False)
                mm(o, Id, A("D%d_" % m, 512 * x, 512 * x + 512), False, True)

        def finish(m, b):
            for x in range(2):
                act(part("R%d_", m, b, 32 * x, 32 * x + 32), A("p%d" % (banks[(m, b)] + x)), AF.Abs)
            sums(m, b, (("Z", "R%d_"),))

        def slot(name, b, k):
            return A(name, 576 * b + k, 576 * b + 576, 9)

        def far(b, ms):
            for m in ms:
                ts(slot("E", b, 8 - m), pd(m, b), A("t1f"), Op.is_ge)

        def steps(b, ks):
            for k in ks:
                if k == 8:
                    cp(slot("DL", b, 8), lk("OI", b, 0))
                else:
                    tt(slot("DL", b, k), lk("OI", b, 8 - k) if k else hw("PP", b), lk("OI", b, 7 - k), Op.subtract)

        def choose(b):
            scan(A("TF", 576 * b, 576 * b + 576), A("E", 576 * b, 576 * b + 576), A("DL", 576 * b, 576 * b + 576))

        def spread(b, bk, which):
            for i in which:
                mm(A(bk[i // 8], 64 * (i % 8), 64 * (i % 8) + 64), EZ(i), slot("TF", b, 8))

        def table(b, bk, i, q):
            o, n = A("NX", 1024 * b + i, 1024 * b + 1024, 16), A(bk[i // 8], 64 * (i % 8), 64 * (i % 8) + 64)
            if q == "V":
                ts(o, n, -1024.0, Op.add)
            else:
                act(o, n, bias=-1024.0)

        TAG[0] = "head"
        for b in range(2):
            for i in range(16):
                mm(hw("p0", b), Z("WZ", i), A(X, 1024 * b + i, 1024 * b + 1024, 16), i == 0, i == 15)
            if b == 0:
                act(half("XC", 0), half(X, 0))
                cp(hw("vI", 0), hw("p0", 0))
        sel(A(X, W, XB), A(X, 0, XB - W), [[0, XB - W]], Op.is_ge, 0, 0)
        send(X, "XA%d" % rnd, XB)
        sel(half("XC", 1), half(X, 1), [[0, 1024]], Op.is_ge, 0, 0)
        if rnd == 0:
            constants_G()
        split(0)
        ts(lk("KK", 0, 7), hw("h", 0), 15.0, Op.add)
        cp(hw("p7", 0), hw("u", 0))
        cp(hw("hb", 0), hw("h", 0))
        for m in (6, 5, 4):
            ts(lk("KK", 0, m), hw("h", 0), 2.0 * m + 1, Op.add)
        plus(0, (3, 2, 1, 0))
        times(0, (7, 6, 5, 4))
        mod(0, 7, 8)
        mod(0, 4, 7)
        offsets(0, 7, 8)
        offsets(0, 4, 7)
        cp(hw("vI", 1), hw("p0", 1))
        TAG[0] = "dist"
        small = {
            "A": lambda: (times(0, (3, 2, 1, 0)), split(1)),
            "B": lambda: (mod(0, 0, 4), cp(hw("hb", 1), hw("h", 1)), cp(hw("p7", 1), hw("u", 1)), offsets(0, 0, 4)),
            "C": lambda: plus(1, range(7, -1, -1)),
            "D": lambda: times(1, range(7, -1, -1)),
            "E": lambda: mod(1, 0, 8),
            "F": lambda: offsets(1, 0, 8),
            "G": lambda: steps(0, range(9)),
            "H": lambda: far(0, range(8)),
            "I": lambda: (choose(0), spread(0, ("p0", "p1"), range(16))),
            "J": lambda: steps(1, range(9)),
            "K": lambda: [table(0, ("p0", "p1"), i, "V") for i in range(8)],
            "L": lambda: [table(0, ("p0", "p1"), i, "V") for i in range(8, 16)],
            "k": lambda: [table(0, ("p0", "p1"), i, "S") for i in range(8)],
            "l": lambda: [table(0, ("p0", "p1"), i, "S") for i in range(8, 16)],
            "M": lambda: (fill(A("SW", 0, NS), 0.0), tt(A("x1", 0, 6), A("NX", 0, 6), A("T6", 0, 6), Op.is_equal)),
            "N": lambda: ts(A("x2", 0, 6), A("x1", 0, 6), 2048.0, Op.mult),
            "O": lambda: tt(A("NX", W, W + 6), A("NX", 0, 6), A("x2", 0, 6), Op.add),
            "P": lambda: far(1, range(7, 1, -1)),
        }
        calls = {"t": take, "u": under, "f": finish, "g": gather, "r": relu, "s": size}
        for w in ORDER.split():
            if len(w) == 1:
                small[w]()
            else:
                calls[w[0]](int(w[1]), int(w[2]), *{"": (), "a": (0, 32), "b": (32, 64)}[w[3:]])
        far(1, (1, 0))
        choose(1)
        TAG[0] = "table"
        free = 3 + 2 * (len(banks) % 2)
        last = ("p%d" % free, "p%d" % (free + 1))
        spread(1, last, list(range(8, 16)) + list(range(8)))
        for t in range(8):
            mm(A("p2", 0, 16), A("Pk", 14 - 2 * t, 142 - 2 * t), A("TF", 9 * t + 8, 1152, 72), t == 0, t == 7)
        for i in range(8):
            table(1, last, 8 + i, "S")
        for i in range(8):
            table(1, last, i, "V")
        ts(A("LS", 16, 32), A("p2", 0, 16), 1.0, Op.add)
        ts(A("CH", 256 + 15, 512, 16), A("p2", 0, 16), -1024.0, Op.add)

    def one_round(rnd):
        X, XN = "X%d" % rnd, "X%d" % (rnd + 1)
        win, theirs = A(X, 0, XB), A("XA%d" % rnd)
        successors(rnd)

        TAG[0] = "runs"

        def step(name, k):
            return A(name, 16 * k, 16 * k + 16)

        def col(k):
            return A("CH", 256 * k + 15, 256 * k + 256, 16)

        TW = A("CT", 5, 96, 6)
        act(A("XS", 0, W, 8), A(X, 0, W, 8))
        act(A("XS", 1, W, 8), I(win, step("LS", 1)))
        for k in range(2, 8):
            o = 256 * k
            for b in range(2):
                tt(A("GM", o + 128 * b, o + 128 * b + 128), I(A("NX", 0, W + 6), A("LS", 16 * k - 16 + 8 * b, 16 * k - 8 + 8 * b)), A("WM", 0, 128), Op.mult)
            if k == 2 and rnd == 0:
                constants_late()
            if k == 6:
                for j in range(6):
                    mm(A("p2", j, 96, 6), Id, col(min(j + 1, 5)), True, False)
                    mm(A("p2", j, 96, 6), A("NId"), col(j), False, True)
                ts(step("SM", 0), col(5), 1.0, Op.add)
            if k == 7:
                ts(step("SM", 1), col(6), 1.0, Op.add)
                ts(A("zz"), TW, 0.0, Op.is_equal)
                scan(A("TX", 1, 17), A("ones", 0, 16), TW)
            for b in range(2):
                scan(A("CH", o + 128 * b, o + 128 * b + 128), A("RSW"), A("GM", o + 128 * b, o + 128 * b + 128))
            if k == 6:
                ts(A("D1"), A("p2", 0, 96), 1.0, Op.not_equal)
            if k == 7:
                break
            for b in range(2):
                ts(A("LS", 16 * k + 8 * b, 16 * k + 8 * b + 8), A("CH", o + 128 * b + 15, o + 128 * b + 128, 16), 1025.0, Op.add)
            act(A("XS", k, W, 8), I(win, step("LS", k)))
            if k == 6:
                tt(A("D1", 5, 96, 6), col(6), step("SM", 0), Op.not_equal)
                scan(A("CQ"), A("R2"), A("D1"))
                scan(A("CT"), A("R1"), A("D1"))
                mm(A("p0", 0, 256), A("ones", 0, 128, parts=1), A("R64", parts=1), True, False)
                for i in range(16):
                    mm(A("p0", i, 256, 16), EZ(i), A("CQ", 5, 96, 6), False, i == 15)
                act(A("VAL"), A("p0", 0, 256), scale=8.0)
        tt(A("Wz"), A("zz"), A("S2"), Op.mult)
        mm(A("p1", 0, 17), BO, A("TX", 0, 17), True, False)
        mm(A("p1", 0, 16), A("TriS"), TW, False, False)

        TAG[0] = "sites"
        tt(A("f6"), col(7), step("SM", 1), Op.not_equal)
        tt(A("n6"), col(7), step("SM", 1), Op.is_equal)
        ts(step("LS", 7), col(7), 1025.0, Op.add)
        act(A("XS", 7, W, 8), I(win, step("LS", 7)))
        scan(A("FX", 1, 17), A("ones", 0, 16), A("f6"))
        tt(A("zs"), A("n6"), A("Wz"), Op.mult)
        mm(A("p1", 0, 16), A("TriS"), A("f6"), False, False)
        mm(A("p1", 0, 17), BO, A("FX", 0, 17), False, False)
        mm(A("p1", 0, 16), Id, A("zs"), False, True)
        cp(A("pl"), A("p1", 0, 16))
        ts(A("dead"), A("N112"), A("p1", 16, 17), Op.is_ge, 4096.0, Op.mult)
        cp(I(A("SW"), A("pl")), A("VAL"))
        scan(A("Y"), A("ones", 0, NS), A("SW", 0, NS), Op.add, Op.max, -1.0)
        scan(A("YW"), A("AW"), A("Y"))
        cp(A("VI"), A("Y"))
        ts(A("wi", 0, ND), A("YW", 15, NS, 16), A("SC"), Op.mult)
        ts(A("PL"), A("VI"), 6, Op.logical_shift_right, 65528, Op.bitwise_and)
        ts(A("wq", 0, ND), A("wi", 0, ND), 511, Op.bitwise_and)
        tt(A("PD"), A("PL"), A("dead"), Op.add)
        cp(A("kl", 0, ND), A("wq", 0, ND))
        tt(A("PR"), I(A("KT", 16, 528), A("kl", 0, ND)), A("PD"), Op.add)
        scan(A("PW"), A("AW"), A("PR"))
        ts(A("sl", 0, ND), A("PW", 15, NS, 16), A("SC"), Op.mult, float(NONE), Op.min)
        cp(A("A4", 0, NS), I(A("XS"), A("sl", 0, ND)))
        ts(A("P3", 0, ND), A("sl", 0, ND), 3.0, Op.subtract)

        TAG[0] = "answers"
        keys = (("p1", 0, 8), ("p2", 8, 12), ("p4", 12, 16))
        for p, m0, m1 in keys:
            mm(A(p, 0, ND * (m1 - m0)), Id, A("MB", ND * m0, ND * m1), True, False)
        for d in range(ND):
            mm(A("p0", 16 * d, 16 * d + 16), A("WB", 128 * d, 128 * d + 128), A("A4", 16 * d, 16 * d + 16))
        for b in range(1, 4):
            cp(A("A4", NS * b, NS * b + NS), A("A4", 0, NS))
        mm(A("p3", 0, 448), A("NId"), A("A4"), True, False)
        scan(A("HW"), A("AW"), A("p0", 0, NS))
        for a in range(4):
            ts(A("aI", ND * a, ND * a + ND), A("HW", 15, NS, 16), A("SC"), Op.mult)
        ts(A("H4"), A("aI"), 5, Op.logical_shift_right, 63, Op.bitwise_and)
        ts(A("U4"), A("aI"), 2047, Op.bitwise_and)
        for a in range(4):
            tt(A("K16", 28 * a, 28 * a + 28), A("H4"), A("MT", 28 * a, 28 * a + 28), Op.add)
        for a in range(4):
            tt(A("Q16", 28 * a, 28 * a + 28), A("K16", 28 * a, 28 * a + 28), A("U4"), Op.mult)
        for a in range(2):
            ts(A("C16", 56 * a, 56 * a + 56), A("Q16", 56 * a, 56 * a + 56), 2047, Op.bitwise_and)
        for a in range(2):
            tt(A("O16A", 56 * a, 56 * a + 56), A("C16", 56 * a, 56 * a + 56), A("MO"), Op.add)
        for a in range(2):
            cp(A("OA", 56 * a, 56 * a + 56), A("O16A", 56 * a, 56 * a + 56))

        def quarter(b):
            return A("DA", 448 * b, 448 * b + 448)

        def key(n):
            p, m0, m1 = keys[n]
            for i in range(16):
                mm(A(p, 0, ND * (m1 - m0)), Z("Z32", i), A("DA", NS * m0 + i, NS * m1, 16), False, i == 15)

        act(A("GA"), I(theirs, A("OA", 0, 28)))
        mm(A("p3", 0, 448), Id, A("GA"), False, True)
        for b in range(1, 4):
            tt(quarter(b), I(theirs, A("OA", 28 * b, 28 * b + 28)), A("A4"), Op.subtract)
            act(quarter(b), quarter(b), AF.Abs)
            if b == 1:
                act(quarter(0), A("p3", 0, 448), AF.Abs)
            key(b - 1)
        cp(A("k1"), A("p1", 0, 28))
        tt(A("k2"), A("p1", 28, 56), A("k1"), Op.min)
        tt(A("k3"), A("p2", 0, 28), A("k2"), Op.min)
        tt(A("k4"), A("p4", 0, 28), A("k3"), Op.min)
        tt(A("k5", 0, 14), A("k4", 0, 14), A("k4", 14, 28), Op.min)
        tt(A("bi", 0, ND), A("k5", 0, ND), A("k5", ND, 14), Op.min)
        tt(A("yes", 0, ND), A("bi", 0, ND), A("WL", 1, 2 * ND, 2), Op.is_lt)
        tt(A("no", 0, ND), A("bi", 0, ND), A("WL", 1, 2 * ND, 2), Op.is_ge)
        ts(A("bm", 0, ND), A("bi", 0, ND), 31, Op.bitwise_and)
        tt(A("zd", 0, ND), A("no", 0, ND), A("D4n", 0, ND), Op.mult)
        tt(A("b3", 0, ND), A("bm", 0, ND), A("K16", 0, ND), Op.add)
        tt(A("b4", 0, ND), A("b3", 0, ND), A("U4", 0, ND), Op.mult)

        TAG[0] = "next"
        CN = [A("p5", 0, 64), A("p6", 0, 64)]
        for b in range(2):
            mm(CN[b], A("Lh", parts=16), A("R16c", 64 * b, 64 * b + 64, parts=16), True, False)
            mm(CN[b], A("Lh", parts=16), A("Rs", 0, 64, parts=16), False, False)
        mm(A("p0", 0, ND), Id, A("P3", 0, ND), True, False)
        mm(A("p0", 0, ND), Id, A("c85", 0, ND), False, False)
        mm(A("p0", 0, ND), A("TriI4"), A("yes", 0, ND), False, False)
        for s in range(1, ND):
            mm(A("p0", s, ND), A("BO4"), A("yes", 0, ND - s), False, s == ND - 1)
        tt(A("Af", 0, ND), A("p0", 0, ND), A("zd", 0, ND), Op.max)
        ts(A("b5", 0, ND), A("b4", 0, ND), 2047, Op.bitwise_and)
        ts(A("Ah", 0, ND), A("Af", 0, ND), ROUND16, Op.add, ROUND16, Op.subtract)
        tt(A("b6", 0, ND), A("b5", 0, ND), A("MO", 0, ND), Op.add)
        ts(A("SL", 0, F * ND, F), A("Af", 0, ND), -8.5, Op.add)
        for d in range(ND):
            ld, le = (A(n, 128 * d, 128 * d + 128) for n in ("LD", "LE"))
            act(A("RG", 144 * d, 144 * d + 129), A("R16h", 0, 129), AF.Sign, scale=-1.0, bias=A("Af", d, d + 1))
            ts(ld, A("IT"), A("Ah", d, d + 1), Op.add, A("Af", d, d + 1), Op.is_ge)
            ts(le, A("IU"), A("Ah", d, d + 1), Op.add, A("Af", d, d + 1), Op.is_lt)
            for b in (1, 0):
                o = 144 * d + 64 * b
                mm(CN[b], ld, A("RG", o + 1, o + 65), False, False)
                mm(CN[b], le, A("RG", o, o + 64), False, d == ND - 1)
        for f in range(F):
            ts(A("OL", f, F * ND, F), A("b6", 0, ND), float(1 + f), Op.add)
        for f in range(1, F):
            ts(A("SL", f, F * ND, F), A("Af", 0, ND), f - 8.5, Op.add)
        ts(A("SR", 64, 128), CN[1], 2.0, Op.mult)
        ts(A("SR", 0, 64), CN[0], 2.0, Op.mult)
        act(A("FL"), I(theirs, A("OL", 0, F * ND)))
        act(A(XN, 16 * CUT, W), I(A("XS"), A("SR", CUT, 128)))
        cp(A(XN, 0, 16 * CUT), I(A("XS"), A("SR", 0, CUT)))
        cp(I(A(XN), A("SL", 0, F * ND)), A("FL"))

    for rnd in range(RO):
        one_round(rnd)

    y = A("X%d" % RO, 0, W)
    sync("Y", [], y[1])
    g.sync.dma_start(T.y[:], y[0]).then_inc(T.sem.dY, 16)
    g.sync.wait_ge(T.sem.dY, 16)
    for s in ("dX0", "dX1", "dW", "dT"):
        g.wait_ge(T.sem[s], 16)
    for q in ("V", "S", "P", "G"):
        g.wait_ge(T.sem["q" + q], done[q])
    for n in SENDS[:RO + 1]:
        for a in ("in", "out"):
            g.wait_ge(T.sem[a + n], ENG * ND)
